import numpy as np
import ml_dtypes


def mxq(x, axis, fmt="e4m3"):
    dtype, down = {"e4m3": (ml_dtypes.float8_e4m3fn, 7), "e5m2": (ml_dtypes.float8_e5m2, 14)}[fmt]
    v = np.moveaxis(np.asarray(x, np.float32).astype(ml_dtypes.bfloat16).astype(np.float64), axis, -1)
    blocks = v.reshape(v.shape[:-1] + (-1, 32))
    amax = np.abs(blocks).max(-1, keepdims=True)
    byte = np.maximum(np.where(amax > 0, np.frexp(amax)[1] - 1 + 127, 0) - down, 1)
    scale = np.exp2(byte - 127.0)
    codes = (blocks / scale).astype(np.float32).astype(dtype).astype(np.float64)
    return np.moveaxis((codes * scale).reshape(v.shape), -1, axis)


WIDE = False


def mx_kscale(k):
    if not WIDE:
        return np.ones(k)
    levels = np.array([24, -24, 12, -12, 0])
    if k % 512:
        return np.exp2(np.random.permutation(np.resize(levels, k // 32))).repeat(32)
    a = np.empty((k // 512, 16))
    for p in range(k // 512):
        a[p, :8] = np.random.permutation(np.resize(levels, 8))
        for g in range(8):
            far = levels[np.abs(levels - a[p, g]) >= 10]
            a[p, g + 8] = far[np.random.randint(len(far))]
    return np.exp2(a.ravel()).repeat(32)


def f64(x):
    return np.asarray(x).astype(np.float64)


def striped(idx):
    return np.tile(idx.reshape(-1, 16).T, (8, 1)).astype(np.uint16)


def unstriped(offs):
    return offs[:16].T.reshape(-1).astype(np.int64)


E2M1 = np.array([0.0, 0.5, 1.0, 1.5, 2.0, 3.0, 4.0, 6.0, -0.0, -0.5, -1.0, -1.5, -2.0, -3.0, -4.0, -6.0])


def pack_weight(w, fmt):
    k, n = w.shape
    w = f64(np.asarray(w, np.float32).astype(ml_dtypes.bfloat16)).reshape(k // 32, 32, n)
    amax = np.abs(w).max(1)
    if fmt == "e4m3":
        byte = np.frexp(amax)[1] - 1 + 127 - 7
    else:
        mant, ex = np.frexp(amax / 6.0)
        byte = np.where(mant > 0.5, ex, ex - 1) + 127
    byte = np.clip(np.where(amax > 0, byte, 1), 1, 254)
    scaled = (w * np.exp2(127.0 - byte)[:, None, :]).reshape(k, n).astype(np.float32)
    by_word = np.ascontiguousarray(scaled.reshape(k // 512, 128, 4, n).transpose(0, 1, 3, 2))
    if fmt == "e4m3":
        words = by_word.astype(ml_dtypes.float8_e4m3fn).view(np.uint8)
    else:
        c = by_word.astype(ml_dtypes.float4_e2m1fn).view(np.uint8) & 0xF
        words = (c[..., 0::2] | (c[..., 1::2] << 4)).reshape(k // 512, 128, 2 * n)
    return np.ascontiguousarray(words), np.ascontiguousarray(byte.astype(np.uint8).reshape(k // 512, 16, n))


def unpack_weight(words, scales, fmt):
    g, _, n = scales.shape
    words = np.ascontiguousarray(words).reshape(g, 128, n, -1)
    if fmt == "e4m3":
        vals = words.view(ml_dtypes.float8_e4m3fn).astype(np.float64)
    else:
        nib = np.empty((g, 128, n, 4), np.uint8)
        nib[..., 0::2] = words & 0xF
        nib[..., 1::2] = words >> 4
        vals = E2M1[nib]
    vals = vals * np.repeat(np.exp2(scales.astype(np.float64) - 127.0), 8, axis=1)[..., None]
    return vals.transpose(0, 1, 3, 2).reshape(g * 512, n)


def pack_table4(v):
    words, scales = pack_weight(v, "e2m1")
    g, t = words.shape[0] // 2, v.shape[1]
    return np.ascontiguousarray(words.reshape(g, 2, 128, t, 2).transpose(0, 2, 3, 1, 4).reshape(g, 128, t, 4)), scales


def unpack_table4(words, scales):
    g, _, t, _ = words.shape
    return unpack_weight(words.reshape(g, 128, t, 2, 2).transpose(0, 3, 1, 2, 4).reshape(2 * g, 128, 2 * t), scales, "e2m1")


def planes(y):
    n, m = y.shape
    v = y.astype(np.float32).astype(ml_dtypes.bfloat16).astype(np.float64).reshape(n // 32, 32, m)
    top = np.abs(v).max(1)
    byte = np.clip(np.where(top > 0, np.frexp(top)[1] - 1 + 127 - 7, 1), 1, 254)
    codes = (v * np.exp2(127.0 - byte)[:, None, :]).reshape(n, m).astype(np.float32).astype(ml_dtypes.float8_e4m3fn).view(np.uint8)
    words = codes.reshape(n // 512, 128, 4, m).transpose(0, 1, 3, 2)
    return np.ascontiguousarray(words), np.ascontiguousarray(byte.astype(np.uint8).reshape(n // 512, 16, m))


K, R, N, T, J = 1024, 512, 512, 2048, 1024


def setup_inputs():
    n = np.random.standard_normal
    s = mx_kscale(K)[:, None]
    u = mx_kscale(R)[:, None]
    p_tab = pack_table4(n((K, T)) * s)
    p_wu = pack_weight(n((K, R)) / np.sqrt(K) / s, "e4m3")
    p_wd = pack_weight(n((R, N)) / np.sqrt(R) / u, "e4m3")
    return {
        "tab_words": p_tab[0],
        "tab_scales": p_tab[1],
        "wu_words": p_wu[0],
        "wu_scales": p_wu[1],
        "sm": (np.random.uniform(0.5, 2.0, R) * u[:, 0]).astype(np.float32),
        "wd_words": p_wd[0],
        "wd_scales": p_wd[1],
        "gT": (n((N, T))).astype(np.float32),
        "wgo": np.tile(np.random.uniform(0.5, 2.0, J), (128, 1)).astype(np.float32),
        "offs": striped(np.random.permutation(T)[:J]),
    }


def reference(tab_words, tab_scales, wu_words, wu_scales, sm, wd_words, wd_scales, gT, wgo, offs):
    idx = unstriped(offs)
    tab_ = unpack_table4(tab_words, tab_scales)[:, idx]
    wu_ = unpack_weight(wu_words, wu_scales, "e4m3")
    a = wu_.T @ tab_
    h = f64(sm)[:, None] * (np.maximum(a, 0.0)) ** 2
    h_ = mxq(h, 0, "e4m3")
    wd_ = unpack_weight(wd_words, wd_scales, "e4m3")
    y = wd_.T @ h_
    out = np.zeros((N, T))
    out[:, idx] = f64(wgo)[0] * (y * f64(gT)[:, idx])
    return (out,) + planes(out)

@@ -1,0 +1,240 @@
+from contextlib import ExitStack
+
+import concourse.mybir as mybir
+
+K, R, N, T, J = 1024, 512, 512, 2048, 1024
+FLOPS = 2 * K * R * J + 2 * R * N * J
+
+F32 = mybir.dt.float32
+BF16 = mybir.dt.bfloat16
+I32 = mybir.dt.int32
+U32 = mybir.dt.uint32
+U16 = mybir.dt.uint16
+U8 = mybir.dt.uint8
+FP8X4 = mybir.dt.float8_e4m3fn_x4
+FP4X4 = mybir.dt.float4_e2m1fn_x4
+MULT = mybir.AluOpType.mult
+ACT = mybir.ActivationFunctionType
+
+P = 128
+PACK = 4
+QUADS = 4
+HALF = 512
+PIECE = 256
+PIECES = J // PIECE
+CHUNK = 256
+CHUNKS = T // CHUNK
+
+
+def tile_list_modp_relu2_gateP_kernel(
+    tc, tab_words, tab_scales, wu_words, wu_scales, sm, wd_words, wd_scales, gT, wgo, offs, out_0, out_1, out_2
+):
+    nc = tc.nc
+    with ExitStack() as ctx:
+        keep = ctx.enter_context(tc.tile_pool(name="keep", bufs=1))
+        psum = ctx.enter_context(tc.psum_pool(name="psum", bufs=1))
+
+        def entries(start, count):
+            return offsets[:, start // 16 : (start + count) // 16]
+
+        offsets = keep.tile([P, J // 16], U16, name="offsets")
+        tab_s = keep.tile([P, T], U8, name="tab_s", tag="then_g1", align_bytes=64)
+        tab_w = keep.tile([P, T], I32, name="tab_w", tag="then_g2", align_bytes=64)
+        w_s = keep.tile([P, 2, R], U8, name="w_s", tag="then_g3", align_bytes=64)
+        wu_w = keep.tile([P, 2, R], I32, name="wu_w", tag="wu_w", align_bytes=64)
+        sm_t = keep.tile([P, PACK], F32, name="sm_t")
+        wgo_t = keep.tile([P, J], F32, name="wgo_t", align_bytes=64)
+        pick_s0 = keep.tile([P, J], U8, name="pick_s0", align_bytes=64)
+        pick_s1 = keep.tile([P, J], U8, name="pick_s1", align_bytes=64)
+        g_src = gT.rearrange("(p t) c -> t p c", t=PACK)
+
+        def load_gates(t, tag):
+            rows = keep.tile([P, T], F32, name="g_rows%d" % t, tag=tag, align_bytes=64)
+            nc.sync.dma_start(rows[:], g_src[t])
+            return rows
+
+        def clear_page(t, tag, engine):
+            cleared = keep.tile([P, T], F32, name="page%d" % t, tag=tag, align_bytes=64)
+            engine.memset(cleared[:].bitcast(I32), 0)
+            return cleared
+
+        nc.vector.memset(w_s[:].rearrange("p a r -> p (a r)").bitcast(I32), 0)
+        nc.vector.memset(pick_s1[:].bitcast(I32), 0)
+        page = [clear_page(t, "page%d" % t, nc.vector) for t in range(2)]
+
+        nc.sync.dma_start(offsets[:], offs)
+        s_rows = tab_scales.rearrange("a q c -> (a q) c").bitcast(I32)
+        nc.sync.dma_start(tab_s[0:112, :].bitcast(I32), s_rows[0:28, :].unsqueeze(0).to_broadcast([4, 28, T // 4]))
+        nc.sync.dma_start(tab_s[112:P, :].bitcast(I32), s_rows[28:32, :].unsqueeze(0).to_broadcast([4, 4, T // 4]))
+        nc.sync.dma_start(tab_w[:], tab_words[0].rearrange("p c b -> p (c b)").bitcast(I32))
+        nc.sync.dma_start(wu_w[:], wu_words.rearrange("a p r b -> p a (r b)").bitcast(I32))
+        for q in range(QUADS):
+            nc.scalar.dma_start(
+                w_s[32 * q : 32 * q + 4, :, :].bitcast(I32),
+                wu_scales[:, 4 * q : 4 * q + 4, :].rearrange("a s r -> s a r").bitcast(I32),
+            )
+        nc.sync.dma_start(sm_t[:], sm.rearrange("(p t) -> p t", t=PACK))
+        nc.sync.dma_start(wgo_t[:], wgo)
+        g_rows = [load_gates(0, "g0")]
+
+        nc.vector.tensor_copy(pick_s0[:], tab_s[:].indirect(offsets[:]))
+        nc.scalar.dma_start(pick_s1[0:112, :].bitcast(I32), pick_s0[16:P, :].bitcast(I32))
+        pick_s = [pick_s0, pick_s1]
+        g_rows.append(load_gates(1, "then_g1"))
+
+        def pick_words(h, tag):
+            both = keep.tile([P, HALF], I32, name="both%d" % h, tag=tag, align_bytes=64)
+            nc.vector.tensor_copy(both[:].bitcast(U32), tab_w[:].bitcast(U32).indirect(entries(h * HALF, HALF)))
+            parted = keep.tile([P, 2, 2 * HALF], U8, name="parted%d" % h, align_bytes=64)
+            nc.vector.tensor_copy(
+                parted[:].bitcast(U16), both[:].bitcast(U16).rearrange("p (j d) -> p d j", d=2)
+            )
+            return parted
+
+        parted = [pick_words(0, "both0")]
+        wd_w = keep.tile([P, N], I32, name="wd_w", tag="both0", align_bytes=64)
+        nc.sync.dma_start(wd_w[:], wd_words[0].rearrange("p n b -> p (n b)").bitcast(I32))
+        wu_p = keep.tile([P, 2, PACK, P], I32, name="wu_p", align_bytes=64)
+        nc.vector.tensor_copy(
+            wu_p[:].rearrange("p a t m -> p a m t"), wu_w[:].rearrange("p a (m t) -> p a m t", t=PACK)
+        )
+        ws_p = keep.tile([P, 2, PACK, P], U8, name="ws_p", align_bytes=64)
+        nc.vector.tensor_copy(
+            ws_p[:].rearrange("p a t m -> p a m t"), w_s[:].rearrange("p a (m t) -> p a m t", t=PACK)
+        )
+        parted.append(pick_words(1, "then_g3"))
+        wd_s = keep.tile([P, N], U8, name="wd_s", tag="wu_w", align_bytes=64)
+        nc.vector.memset(wd_s[:].bitcast(I32), 0)
+        for q in range(QUADS):
+            nc.sync.dma_start(
+                wd_s[32 * q : 32 * q + 4, :].bitcast(I32), wd_scales[0, 4 * q : 4 * q + 4, :].bitcast(I32)
+            )
+        g_rows.append(load_gates(2, "then_g2"))
+        g_rows.append(load_gates(3, "then_g3"))
+        wd_p = keep.tile([P, PACK, P], I32, name="wd_p", align_bytes=64)
+        nc.vector.tensor_copy(wd_p[:].rearrange("p t m -> p m t"), wd_w[:].rearrange("p (m t) -> p m t", t=PACK))
+        wds_p = keep.tile([P, PACK, P], U8, name="wds_p", align_bytes=64)
+        nc.vector.tensor_copy(wds_p[:].rearrange("p t m -> p m t"), wd_s[:].rearrange("p (m t) -> p m t", t=PACK))
+
+        def up(h):
+            pos = keep.tile([P, PACK, HALF], F32, name="pos%d" % h, align_bytes=64)
+            for t in range(PACK):
+                acc = psum.tile([P, HALF], F32, name="acc_up", tag="acc_up", bufs=6)
+                for a in range(2):
+                    nc.tensor.matmul_mx(
+                        out=acc[:],
+                        lhsT=wu_p[:, a, t, :].bitcast(FP8X4),
+                        lhsT_scale=ws_p[:, a, t, :],
+                        rhs=parted[h][:, a, :].bitcast(FP4X4),
+                        rhs_scale=pick_s[a][:, h * HALF : (h + 1) * HALF],
+                        start=(a == 0),
+                        stop=(a == 1),
+                    )
+                nc.scalar.activation(pos[:, t, :], acc[:], ACT.Relu)
+            return pos
+
+        h_codes = keep.tile([P, J], I32, name="h_codes", align_bytes=64)
+        h_scales = keep.tile([P, J], U8, name="h_scales", align_bytes=64)
+
+        def hidden(pos, p):
+            c0 = (p * PIECE) % HALF
+            cols = slice(p * PIECE, (p + 1) * PIECE)
+            sq = keep.tile([P, PACK, PIECE], F32, name="sq", tag="sq", bufs=2, align_bytes=64)
+            rows = keep.tile([P, PACK, PIECE], BF16, name="rows", tag="rows", bufs=2, align_bytes=64)
+            for t in range(PACK):
+                nc.scalar.activation(sq[:, t, :], pos[:, t, c0 : c0 + PIECE], ACT.Square)
+            for t in range(PACK):
+                nc.scalar.activation(rows[:, t, :], sq[:, t, :], ACT.Copy, scale=sm_t[:, t : t + 1])
+            woven = keep.tile([P, PIECE, PACK], BF16, name="woven%d" % p, tag="turn%d" % p, align_bytes=64)
+            nc.scalar.copy(
+                woven[:].rearrange("p (c i) t -> p c t i", i=4), rows[:].rearrange("p t (c i) -> p c t i", i=4)
+            )
+            nc.vector.quantize_mx(
+                out=h_codes[:, cols].bitcast(FP8X4),
+                scales=h_scales[:, cols],
+                in_=woven[:].rearrange("p c t -> p (c t)"),
+            )
+
+        def down(acc, t, cols):
+            nc.tensor.matmul_mx(
+                out=acc,
+                lhsT=wd_p[:, t, :].bitcast(FP8X4),
+                lhsT_scale=wds_p[:, t, :],
+                rhs=h_codes[:, cols].bitcast(FP8X4),
+                rhs_scale=h_scales[:, cols],
+                start=True,
+                stop=True,
+            )
+
+        def gates(t, start, count, tag):
+            gate = keep.tile([P, count], F32, name="gate_%d_%d" % (t, start), tag=tag, align_bytes=64)
+            nc.vector.tensor_tensor(
+                gate[:], g_rows[t][:].indirect(entries(start, count)), wgo_t[:, start : start + count], MULT
+            )
+            return gate
+
+        def put(t, start, count, y, gate):
+            nc.vector.tensor_tensor(page[t][:].indirect(entries(start, count)), y, gate, MULT)
+
+        early = [[gates(t, h * HALF, HALF, "gate%d%d" % (t, h)) for h in range(2)] for t in range(2)]
+        late = []
+        pos = None
+        for p in range(PIECES):
+            h, c0 = divmod(p * PIECE, HALF)
+            if c0 == 0:
+                pos = up(h)
+            hidden(pos, p)
+            acc = psum.tile([P, 2, PIECE], F32, name="acc_down", tag="acc_down", bufs=2)
+            for t in range(2):
+                down(acc[:, t, :], t, slice(p * PIECE, (p + 1) * PIECE))
+            y = keep.tile([P, 2, PIECE], F32, name="y_early%d" % p, align_bytes=64)
+            nc.scalar.copy(y[:], acc[:])
+            late.append(gates(2 + p // 2, (p % 2) * HALF, HALF, "turn%d" % p))
+            for t in range(2):
+                put(t, p * PIECE, PIECE, y[:, t, :], early[t][h][:, c0 : c0 + PIECE])
+
+        for t in range(2, PACK):
+            page.append(clear_page(t, "then_g%d" % t, nc.gpsimd))
+            for h in range(2):
+                acc = psum.tile([P, HALF], F32, name="acc_late", tag="acc_up", bufs=6)
+                down(acc[:], t, slice(h * HALF, (h + 1) * HALF))
+                y = keep.tile([P, HALF], F32, name="y_late%d%d" % (t, h), align_bytes=64)
+                nc.scalar.copy(y[:], acc[:])
+                put(t, h * HALF, HALF, y[:], late[2 * (t - 2) + h][:])
+
+        out_rows = out_0.rearrange("(p t) c -> t p c", t=PACK)
+        for t in range(PACK):
+            nc.sync.dma_start(out_rows[t], page[t][:])
+
+        o_scales = keep.tile([P, T], U8, name="o_scales", align_bytes=64)
+        words_out = out_1[0].rearrange("p c b -> p (c b)").bitcast(I32)
+        chunk_cols = [slice(c * CHUNK, (c + 1) * CHUNK) for c in range(CHUNKS)]
+        woven_o = [keep.tile([P, CHUNK, PACK], BF16, name="woven_o%d" % c, align_bytes=64) for c in range(CHUNKS)]
+        rows_lo = keep.tile([P, 2, T], BF16, name="rows_lo", align_bytes=64)
+        rows_hi = [keep.tile([P, 2, CHUNK], BF16, name="rows_hi%d" % c, align_bytes=64) for c in range(CHUNKS)]
+        for t in range(2):
+            nc.scalar.copy(rows_lo[:, t, :], page[t][:])
+        for c in range(CHUNKS):
+            nc.scalar.copy(woven_o[c][:, :, 0:2], rows_lo[:, :, chunk_cols[c]].rearrange("p t c -> p c t"))
+        for c in range(CHUNKS):
+            nc.scalar.copy(rows_hi[c][:, 0, :], page[2][:, chunk_cols[c]])
+        half_chunks = CHUNKS // 2
+        for c in range(CHUNKS):
+            copy = nc.vector.tensor_copy if c < half_chunks else nc.scalar.copy
+            copy(rows_hi[c][:, 1, :], page[3][:, chunk_cols[c]])
+        for i in range(half_chunks):
+            for c, copy in ((i, nc.vector.tensor_copy), (half_chunks + i, nc.scalar.copy)):
+                copy(woven_o[c][:, :, 2:4], rows_hi[c][:].rearrange("p t c -> p c t"))
+        for i in range(CHUNKS):
+            c = (i % 2) * half_chunks + i // 2
+            o_codes = keep.tile([P, CHUNK], I32, name="o_codes%d" % c, align_bytes=64)
+            nc.vector.quantize_mx(
+                out=o_codes[:].bitcast(FP8X4),
+                scales=o_scales[:, chunk_cols[c]],
+                in_=woven_o[c][:].rearrange("p c t -> p (c t)"),
+            )
+            nc.sync.dma_start(words_out[:, chunk_cols[c]], o_codes[:])
+        for q in range(QUADS):
+            nc.scalar.dma_start(
+                out_2[0, 4 * q : 4 * q + 4, :].bitcast(I32), o_scales[32 * q : 32 * q + 4, :].bitcast(I32)
+            )

@@ -20,8 +20,6 @@ P = 128
 PACK = 4
 QUADS = 4
 HALF = 512
-PIECE = 256
-PIECES = J // PIECE
 CHUNK = 256
 CHUNKS = T // CHUNK
 
@@ -38,10 +36,10 @@ def tile_list_modp_relu2_gateP_kernel(
             return offsets[:, start // 16 : (start + count) // 16]
 
         offsets = keep.tile([P, J // 16], U16, name="offsets")
-        tab_s = keep.tile([P, T], U8, name="tab_s", tag="then_g1", align_bytes=64)
-        tab_w = keep.tile([P, T], I32, name="tab_w", tag="then_g2", align_bytes=64)
-        w_s = keep.tile([P, 2, R], U8, name="w_s", tag="then_g3", align_bytes=64)
-        wu_w = keep.tile([P, 2, R], I32, name="wu_w", tag="wu_w", align_bytes=64)
+        tab_s = keep.tile([P, T], U8, name="tab_s", align_bytes=64)
+        tab_w = keep.tile([P, T], I32, name="tab_w", align_bytes=64)
+        w_s = keep.tile([P, 2, R], U8, name="w_s", tag="w_s", align_bytes=64)
+        wu_w = keep.tile([P, 2, R], I32, name="wu_w", align_bytes=64)
         sm_t = keep.tile([P, PACK], F32, name="sm_t")
         wgo_t = keep.tile([P, J], F32, name="wgo_t", align_bytes=64)
         pick_s0 = keep.tile([P, J], U8, name="pick_s0", align_bytes=64)
@@ -58,9 +56,11 @@ def tile_list_modp_relu2_gateP_kernel(
             engine.memset(cleared[:].bitcast(I32), 0)
             return cleared
 
-        nc.vector.memset(w_s[:].rearrange("p a r -> p (a r)").bitcast(I32), 0)
+        wd_s = keep.tile([P, N], U8, name="wd_s", align_bytes=64)
+        wd_w = keep.tile([P, N], I32, name="wd_w", tag="wd_w", align_bytes=64)
+        nc.vector.memset(wd_s[:].bitcast(I32), 0)
         nc.vector.memset(pick_s1[:].bitcast(I32), 0)
-        page = [clear_page(t, "page%d" % t, nc.vector) for t in range(2)]
+        page = [clear_page(0, "page0", nc.vector)]
 
         nc.sync.dma_start(offsets[:], offs)
         s_rows = tab_scales.rearrange("a q c -> (a q) c").bitcast(I32)
@@ -68,32 +68,36 @@ def tile_list_modp_relu2_gateP_kernel(
         nc.sync.dma_start(tab_s[112:P, :].bitcast(I32), s_rows[28:32, :].unsqueeze(0).to_broadcast([4, 4, T // 4]))
         nc.sync.dma_start(tab_w[:], tab_words[0].rearrange("p c b -> p (c b)").bitcast(I32))
         nc.sync.dma_start(wu_w[:], wu_words.rearrange("a p r b -> p a (r b)").bitcast(I32))
-        for q in range(QUADS):
-            nc.scalar.dma_start(
-                w_s[32 * q : 32 * q + 4, :, :].bitcast(I32),
-                wu_scales[:, 4 * q : 4 * q + 4, :].rearrange("a s r -> s a r").bitcast(I32),
-            )
+        u_rows = wu_scales.rearrange("a q r -> (a q) r").bitcast(I32)
+        nc.sync.dma_start(w_s[0:112, 0, :].bitcast(I32), u_rows[0:28, :].unsqueeze(0).to_broadcast([4, 28, R // 4]))
+        nc.sync.dma_start(w_s[112:P, 0, :].bitcast(I32), u_rows[0:16, :])
+        nc.sync.dma_start(w_s[16:P, 1, :].bitcast(I32), u_rows[4:32, :].unsqueeze(0).to_broadcast([4, 28, R // 4]))
+        nc.sync.dma_start(w_s[0:16, 1, :].bitcast(I32), u_rows[16:32, :])
         nc.sync.dma_start(sm_t[:], sm.rearrange("(p t) -> p t", t=PACK))
         nc.sync.dma_start(wgo_t[:], wgo)
-        g_rows = [load_gates(0, "g0")]
+        g_rows = {t: load_gates(t, "g%d" % t) for t in (3, 1)}
+        nc.sync.dma_start(wd_w[:], wd_words[0].rearrange("p n b -> p (n b)").bitcast(I32))
+        for q in range(QUADS):
+            nc.sync.dma_start(
+                wd_s[32 * q : 32 * q + 4, :].bitcast(I32), wd_scales[0, 4 * q : 4 * q + 4, :].bitcast(I32)
+            )
+        for t in (0, 2):
+            g_rows[t] = load_gates(t, "g%d" % t)
 
         nc.vector.tensor_copy(pick_s0[:], tab_s[:].indirect(offsets[:]))
         nc.scalar.dma_start(pick_s1[0:112, :].bitcast(I32), pick_s0[16:P, :].bitcast(I32))
         pick_s = [pick_s0, pick_s1]
-        g_rows.append(load_gates(1, "then_g1"))
 
         def pick_words(h, tag):
             both = keep.tile([P, HALF], I32, name="both%d" % h, tag=tag, align_bytes=64)
             nc.vector.tensor_copy(both[:].bitcast(U32), tab_w[:].bitcast(U32).indirect(entries(h * HALF, HALF)))
-            parted = keep.tile([P, 2, 2 * HALF], U8, name="parted%d" % h, align_bytes=64)
+            parted = keep.tile([P, 2, 2 * HALF], U8, name="parted%d" % h, tag="parted%d" % h, align_bytes=64)
             nc.vector.tensor_copy(
                 parted[:].bitcast(U16), both[:].bitcast(U16).rearrange("p (j d) -> p d j", d=2)
             )
             return parted
 
         parted = [pick_words(0, "both0")]
-        wd_w = keep.tile([P, N], I32, name="wd_w", tag="both0", align_bytes=64)
-        nc.sync.dma_start(wd_w[:], wd_words[0].rearrange("p n b -> p (n b)").bitcast(I32))
         wu_p = keep.tile([P, 2, PACK, P], I32, name="wu_p", align_bytes=64)
         nc.vector.tensor_copy(
             wu_p[:].rearrange("p a t m -> p a m t"), wu_w[:].rearrange("p a (m t) -> p a m t", t=PACK)
@@ -102,24 +106,15 @@ def tile_list_modp_relu2_gateP_kernel(
         nc.vector.tensor_copy(
             ws_p[:].rearrange("p a t m -> p a m t"), w_s[:].rearrange("p a (m t) -> p a m t", t=PACK)
         )
-        parted.append(pick_words(1, "then_g3"))
-        wd_s = keep.tile([P, N], U8, name="wd_s", tag="wu_w", align_bytes=64)
-        nc.vector.memset(wd_s[:].bitcast(I32), 0)
-        for q in range(QUADS):
-            nc.sync.dma_start(
-                wd_s[32 * q : 32 * q + 4, :].bitcast(I32), wd_scales[0, 4 * q : 4 * q + 4, :].bitcast(I32)
-            )
-        g_rows.append(load_gates(2, "then_g2"))
-        g_rows.append(load_gates(3, "then_g3"))
-        wd_p = keep.tile([P, PACK, P], I32, name="wd_p", align_bytes=64)
-        nc.vector.tensor_copy(wd_p[:].rearrange("p t m -> p m t"), wd_w[:].rearrange("p (m t) -> p m t", t=PACK))
-        wds_p = keep.tile([P, PACK, P], U8, name="wds_p", align_bytes=64)
-        nc.vector.tensor_copy(wds_p[:].rearrange("p t m -> p m t"), wd_s[:].rearrange("p (m t) -> p m t", t=PACK))
+        parted.append(pick_words(1, "w_s"))
+
+        def bank(b, shape):
+            return psum.tile(shape, F32, name="bank%d" % b, tag="bank%d" % b)
 
         def up(h):
-            pos = keep.tile([P, PACK, HALF], F32, name="pos%d" % h, align_bytes=64)
+            sums = []
             for t in range(PACK):
-                acc = psum.tile([P, HALF], F32, name="acc_up", tag="acc_up", bufs=6)
+                acc = bank(PACK * h + t, [P, HALF])
                 for a in range(2):
                     nc.tensor.matmul_mx(
                         out=acc[:],
@@ -130,41 +125,55 @@ def tile_list_modp_relu2_gateP_kernel(
                         start=(a == 0),
                         stop=(a == 1),
                     )
-                nc.scalar.activation(pos[:, t, :], acc[:], ACT.Relu)
-            return pos
+                sums.append(acc)
+            return sums
 
-        h_codes = keep.tile([P, J], I32, name="h_codes", align_bytes=64)
-        h_scales = keep.tile([P, J], U8, name="h_scales", align_bytes=64)
-
-        def hidden(pos, p):
-            c0 = (p * PIECE) % HALF
-            cols = slice(p * PIECE, (p + 1) * PIECE)
-            sq = keep.tile([P, PACK, PIECE], F32, name="sq", tag="sq", bufs=2, align_bytes=64)
-            rows = keep.tile([P, PACK, PIECE], BF16, name="rows", tag="rows", bufs=2, align_bytes=64)
+        def hidden(h, on_vector, tag):
+            pos = keep.tile([P, PACK, HALF], F32, name="pos%d" % h, align_bytes=64)
+            sq = keep.tile([P, PACK, HALF], F32, name="sq", tag="sq", align_bytes=64)
+            rows = keep.tile([P, PACK, HALF], BF16, name="rows%d" % h, tag=tag, align_bytes=64)
+            on_scalar = range(PACK - on_vector)
             for t in range(PACK):
-                nc.scalar.activation(sq[:, t, :], pos[:, t, c0 : c0 + PIECE], ACT.Square)
-            for t in range(PACK):
+                nc.scalar.activation(pos[:, t, :], sums[h][t][:], ACT.Relu)
+            for t in on_scalar:
+                nc.scalar.activation(sq[:, t, :], pos[:, t, :], ACT.Square)
+            for t in on_scalar:
                 nc.scalar.activation(rows[:, t, :], sq[:, t, :], ACT.Copy, scale=sm_t[:, t : t + 1])
-            woven = keep.tile([P, PIECE, PACK], BF16, name="woven%d" % p, tag="turn%d" % p, align_bytes=64)
+            for t in range(PACK - on_vector, PACK):
+                nc.vector.scalar_tensor_tensor(
+                    out=rows[:, t, :],
+                    in0=pos[:, t, :],
+                    scalar=sm_t[:, t : t + 1],
+                    in1=sums[h][t][:],
+                    op0=MULT,
+                    op1=MULT,
+                )
+            woven = keep.tile([P, HALF, PACK], BF16, name="woven%d" % h, tag="woven%d" % h, align_bytes=64)
             nc.scalar.copy(
                 woven[:].rearrange("p (c i) t -> p c t i", i=4), rows[:].rearrange("p t (c i) -> p c t i", i=4)
             )
-            nc.vector.quantize_mx(
-                out=h_codes[:, cols].bitcast(FP8X4),
-                scales=h_scales[:, cols],
-                in_=woven[:].rearrange("p c t -> p (c t)"),
-            )
+            return woven
 
-        def down(acc, t, cols):
-            nc.tensor.matmul_mx(
-                out=acc,
-                lhsT=wd_p[:, t, :].bitcast(FP8X4),
-                lhsT_scale=wds_p[:, t, :],
-                rhs=h_codes[:, cols].bitcast(FP8X4),
-                rhs_scale=h_scales[:, cols],
-                start=True,
-                stop=True,
+        def down(h, woven):
+            codes = keep.tile([P, HALF], I32, name="h_codes%d" % h, align_bytes=64)
+            scales = keep.tile([P, HALF], U8, name="h_scales%d" % h, tag="h_scales%d" % h, align_bytes=64)
+            nc.vector.quantize_mx(
+                out=codes[:].bitcast(FP8X4), scales=scales[:], in_=woven[:].rearrange("p c t -> p (c t)")
             )
+            results = []
+            for t in range(PACK):
+                acc = bank(PACK * h + t, [P, HALF])
+                nc.tensor.matmul_mx(
+                    out=acc[:],
+                    lhsT=wd_p[:, t, :].bitcast(FP8X4),
+                    lhsT_scale=wds_p[:, t, :],
+                    rhs=codes[:].bitcast(FP8X4),
+                    rhs_scale=scales[:],
+                    start=True,
+                    stop=True,
+                )
+                results.append(acc)
+            return results
 
         def gates(t, start, count, tag):
             gate = keep.tile([P, count], F32, name="gate_%d_%d" % (t, start), tag=tag, align_bytes=64)
@@ -176,31 +185,42 @@ def tile_list_modp_relu2_gateP_kernel(
         def put(t, start, count, y, gate):
             nc.vector.tensor_tensor(page[t][:].indirect(entries(start, count)), y, gate, MULT)
 
-        early = [[gates(t, h * HALF, HALF, "gate%d%d" % (t, h)) for h in range(2)] for t in range(2)]
-        late = []
-        pos = None
-        for p in range(PIECES):
-            h, c0 = divmod(p * PIECE, HALF)
-            if c0 == 0:
-                pos = up(h)
-            hidden(pos, p)
-            acc = psum.tile([P, 2, PIECE], F32, name="acc_down", tag="acc_down", bufs=2)
-            for t in range(2):
-                down(acc[:, t, :], t, slice(p * PIECE, (p + 1) * PIECE))
-            y = keep.tile([P, 2, PIECE], F32, name="y_early%d" % p, align_bytes=64)
-            nc.scalar.copy(y[:], acc[:])
-            late.append(gates(2 + p // 2, (p % 2) * HALF, HALF, "turn%d" % p))
-            for t in range(2):
-                put(t, p * PIECE, PIECE, y[:, t, :], early[t][h][:, c0 : c0 + PIECE])
+        y = [keep.tile([P, J], F32, name="y%d" % t, align_bytes=64) for t in range(2)]
+        halves = [slice(h * HALF, (h + 1) * HALF) for h in range(2)]
 
+        def drain(h, results, t):
+            nc.scalar.copy(y[t][:, halves[h]], results[t][:])
+
+        def put_early(h, results):
+            for t in range(2):
+                drain(h, results, t)
+                put(t, h * HALF, HALF, y[t][:, halves[h]], gate[t][:, halves[h]])
+
+        gate = {3: gates(3, 0, J, "gate3")}
+        sums = [up(0), up(1)]
+        woven = hidden(0, 2, "g3")
+        gate[1] = gates(1, 0, J, "gate1")
+        wd_p = keep.tile([P, PACK, P], I32, name="wd_p", align_bytes=64)
+        nc.vector.tensor_copy(wd_p[:].rearrange("p t m -> p m t"), wd_w[:].rearrange("p (m t) -> p m t", t=PACK))
+        wds_p = keep.tile([P, PACK, P], U8, name="wds_p", align_bytes=64)
+        nc.vector.tensor_copy(wds_p[:].rearrange("p t m -> p m t"), wd_s[:].rearrange("p (m t) -> p m t", t=PACK))
+
+        results0 = down(0, woven)
+        gate[0] = gates(0, 0, J, "gate0")
+        page.append(clear_page(1, "g0", nc.gpsimd))
+        put_early(0, results0)
+        woven = hidden(1, 0, "rows1")
+        y.append(keep.tile([P, J], F32, name="y2", tag="rows1", align_bytes=64))
+        results1 = down(1, woven)
+        y.append(keep.tile([P, J], F32, name="y3", tag="h_scales1", align_bytes=64))
+        gate[2] = gates(2, 0, J, "woven1")
+        page.append(clear_page(2, "g2", nc.gpsimd))
+        put_early(1, results1)
+        page.append(clear_page(3, "gate0", nc.gpsimd))
         for t in range(2, PACK):
-            page.append(clear_page(t, "then_g%d" % t, nc.gpsimd))
-            for h in range(2):
-                acc = psum.tile([P, HALF], F32, name="acc_late", tag="acc_up", bufs=6)
-                down(acc[:], t, slice(h * HALF, (h + 1) * HALF))
-                y = keep.tile([P, HALF], F32, name="y_late%d%d" % (t, h), align_bytes=64)
-                nc.scalar.copy(y[:], acc[:])
-                put(t, h * HALF, HALF, y[:], late[2 * (t - 2) + h][:])
+            drain(0, results0, t)
+            drain(1, results1, t)
+            put(t, 0, J, y[t][:], gate[t][:])
 
         out_rows = out_0.rearrange("(p t) c -> t p c", t=PACK)
         for t in range(PACK):

@@ -21,7 +21,6 @@ PACK = 4
 QUADS = 4
 HALF = 512
 CHUNK = 256
-CHUNKS = T // CHUNK
 
 
 def tile_list_modp_relu2_gateP_kernel(
@@ -58,21 +57,26 @@ def tile_list_modp_relu2_gateP_kernel(
 
         wd_s = keep.tile([P, N], U8, name="wd_s", align_bytes=64)
         wd_w = keep.tile([P, N], I32, name="wd_w", tag="wd_w", align_bytes=64)
+        nc.vector.memset(w_s[:].rearrange("p a r -> p (a r)").bitcast(I32), 0)
         nc.vector.memset(wd_s[:].bitcast(I32), 0)
         nc.vector.memset(pick_s1[:].bitcast(I32), 0)
         page = [clear_page(0, "page0", nc.vector)]
 
         nc.sync.dma_start(offsets[:], offs)
         s_rows = tab_scales.rearrange("a q c -> (a q) c").bitcast(I32)
-        nc.sync.dma_start(tab_s[0:112, :].bitcast(I32), s_rows[0:28, :].unsqueeze(0).to_broadcast([4, 28, T // 4]))
-        nc.sync.dma_start(tab_s[112:P, :].bitcast(I32), s_rows[28:32, :].unsqueeze(0).to_broadcast([4, 4, T // 4]))
+        for q in range(QUADS):
+            for e in range(2):
+                first = 4 * q + 4 * e
+                nc.sync.dma_start(
+                    tab_s[32 * q + 16 * e : 32 * q + 16 * e + 16, :].bitcast(I32), s_rows[first : first + 16, :]
+                )
         nc.sync.dma_start(tab_w[:], tab_words[0].rearrange("p c b -> p (c b)").bitcast(I32))
         nc.sync.dma_start(wu_w[:], wu_words.rearrange("a p r b -> p a (r b)").bitcast(I32))
-        u_rows = wu_scales.rearrange("a q r -> (a q) r").bitcast(I32)
-        nc.sync.dma_start(w_s[0:112, 0, :].bitcast(I32), u_rows[0:28, :].unsqueeze(0).to_broadcast([4, 28, R // 4]))
-        nc.sync.dma_start(w_s[112:P, 0, :].bitcast(I32), u_rows[0:16, :])
-        nc.sync.dma_start(w_s[16:P, 1, :].bitcast(I32), u_rows[4:32, :].unsqueeze(0).to_broadcast([4, 28, R // 4]))
-        nc.sync.dma_start(w_s[0:16, 1, :].bitcast(I32), u_rows[16:32, :])
+        for q in range(QUADS):
+            nc.sync.dma_start(
+                w_s[32 * q : 32 * q + 4, :, :].bitcast(I32),
+                wu_scales[:, 4 * q : 4 * q + 4, :].rearrange("a s r -> s a r").bitcast(I32),
+            )
         nc.sync.dma_start(sm_t[:], sm.rearrange("(p t) -> p t", t=PACK))
         nc.sync.dma_start(wgo_t[:], wgo)
         g_rows = {t: load_gates(t, "g%d" % t) for t in (3, 1)}
@@ -85,7 +89,7 @@ def tile_list_modp_relu2_gateP_kernel(
             g_rows[t] = load_gates(t, "g%d" % t)
 
         nc.vector.tensor_copy(pick_s0[:], tab_s[:].indirect(offsets[:]))
-        nc.scalar.dma_start(pick_s1[0:112, :].bitcast(I32), pick_s0[16:P, :].bitcast(I32))
+        nc.scalar.dma_start(pick_s1[0:100, :].bitcast(I32), pick_s0[28:P, :].bitcast(I32))
         pick_s = [pick_s0, pick_s1]
 
         def pick_words(h, tag):
@@ -100,11 +104,12 @@ def tile_list_modp_relu2_gateP_kernel(
         parted = [pick_words(0, "both0")]
         wu_p = keep.tile([P, 2, PACK, P], I32, name="wu_p", align_bytes=64)
         nc.vector.tensor_copy(
-            wu_p[:].rearrange("p a t m -> p a m t"), wu_w[:].rearrange("p a (m t) -> p a m t", t=PACK)
+            wu_p[:].rearrange("p a t (c i) -> p a c t i", i=4),
+            wu_w[:].rearrange("p a (c i t) -> p a c t i", i=4, t=PACK),
         )
         ws_p = keep.tile([P, 2, PACK, P], U8, name="ws_p", align_bytes=64)
         nc.vector.tensor_copy(
-            ws_p[:].rearrange("p a t m -> p a m t"), w_s[:].rearrange("p a (m t) -> p a m t", t=PACK)
+            ws_p[:], w_s[:].rearrange("p a (m t) -> p a t m", t=PACK)
         )
         parted.append(pick_words(1, "w_s"))
 
@@ -201,9 +206,11 @@ def tile_list_modp_relu2_gateP_kernel(
         woven = hidden(0, 2, "g3")
         gate[1] = gates(1, 0, J, "gate1")
         wd_p = keep.tile([P, PACK, P], I32, name="wd_p", align_bytes=64)
-        nc.vector.tensor_copy(wd_p[:].rearrange("p t m -> p m t"), wd_w[:].rearrange("p (m t) -> p m t", t=PACK))
+        nc.vector.tensor_copy(
+            wd_p[:].rearrange("p t (c i) -> p c t i", i=4), wd_w[:].rearrange("p (c i t) -> p c t i", i=4, t=PACK)
+        )
         wds_p = keep.tile([P, PACK, P], U8, name="wds_p", align_bytes=64)
-        nc.vector.tensor_copy(wds_p[:].rearrange("p t m -> p m t"), wd_s[:].rearrange("p (m t) -> p m t", t=PACK))
+        nc.vector.tensor_copy(wds_p[:], wd_s[:].rearrange("p (m t) -> p t m", t=PACK))
 
         results0 = down(0, woven)
         gate[0] = gates(0, 0, J, "gate0")
@@ -228,33 +235,35 @@ def tile_list_modp_relu2_gateP_kernel(
 
         o_scales = keep.tile([P, T], U8, name="o_scales", align_bytes=64)
         words_out = out_1[0].rearrange("p c b -> p (c b)").bitcast(I32)
-        chunk_cols = [slice(c * CHUNK, (c + 1) * CHUNK) for c in range(CHUNKS)]
-        woven_o = [keep.tile([P, CHUNK, PACK], BF16, name="woven_o%d" % c, align_bytes=64) for c in range(CHUNKS)]
+        split = T // 2
+        chunks = [(c, HALF) for c in range(0, split, HALF)] + [(c, CHUNK) for c in range(split, T, CHUNK)]
+        woven_o = [keep.tile([P, n, PACK], BF16, name="woven_o%d" % c, align_bytes=64) for c, n in chunks]
         rows_lo = keep.tile([P, 2, T], BF16, name="rows_lo", align_bytes=64)
-        rows_hi = [keep.tile([P, 2, CHUNK], BF16, name="rows_hi%d" % c, align_bytes=64) for c in range(CHUNKS)]
+        rows_v = keep.tile([P, 2, split], BF16, name="rows_v", align_bytes=64)
+        rows_s = keep.tile([P, 2, T - split], BF16, name="rows_s", align_bytes=64)
+        pairs = "p t c -> p c t"
         for t in range(2):
             nc.scalar.copy(rows_lo[:, t, :], page[t][:])
-        for c in range(CHUNKS):
-            nc.scalar.copy(woven_o[c][:, :, 0:2], rows_lo[:, :, chunk_cols[c]].rearrange("p t c -> p c t"))
-        for c in range(CHUNKS):
-            nc.scalar.copy(rows_hi[c][:, 0, :], page[2][:, chunk_cols[c]])
-        half_chunks = CHUNKS // 2
-        for c in range(CHUNKS):
-            copy = nc.vector.tensor_copy if c < half_chunks else nc.scalar.copy
-            copy(rows_hi[c][:, 1, :], page[3][:, chunk_cols[c]])
-        for i in range(half_chunks):
-            for c, copy in ((i, nc.vector.tensor_copy), (half_chunks + i, nc.scalar.copy)):
-                copy(woven_o[c][:, :, 2:4], rows_hi[c][:].rearrange("p t c -> p c t"))
-        for i in range(CHUNKS):
-            c = (i % 2) * half_chunks + i // 2
-            o_codes = keep.tile([P, CHUNK], I32, name="o_codes%d" % c, align_bytes=64)
+        for (c, n), woven in zip(chunks, woven_o):
+            nc.scalar.copy(woven[:, :, 0:2], rows_lo[:, :, c : c + n].rearrange(pairs))
+        nc.scalar.copy(rows_v[:, 0, :], page[2][:, 0:split])
+        nc.scalar.copy(rows_s[:, 0, :], page[2][:, split:T])
+        nc.vector.tensor_copy(rows_v[:, 1, :], page[3][:, 0:split])
+        nc.scalar.copy(rows_s[:, 1, :], page[3][:, split:T])
+        for (c, n), woven in zip(chunks, woven_o):
+            if c < split:
+                nc.vector.tensor_copy(woven[:, :, 2:4], rows_v[:, :, c : c + n].rearrange(pairs))
+            else:
+                nc.scalar.copy(woven[:, :, 2:4], rows_s[:, :, c - split : c - split + n].rearrange(pairs))
+        for (c, n), woven in zip(chunks, woven_o):
+            o_codes = keep.tile([P, n], I32, name="o_codes%d" % c, align_bytes=64)
             nc.vector.quantize_mx(
                 out=o_codes[:].bitcast(FP8X4),
-                scales=o_scales[:, chunk_cols[c]],
-                in_=woven_o[c][:].rearrange("p c t -> p (c t)"),
+                scales=o_scales[:, c : c + n],
+                in_=woven[:].rearrange("p c t -> p (c t)"),
             )
-            nc.sync.dma_start(words_out[:, chunk_cols[c]], o_codes[:])
+            nc.sync.dma_start(words_out[:, c : c + n], o_codes[:])
         for q in range(QUADS):
-            nc.scalar.dma_start(
+            (nc.scalar if q % 2 else nc.sync).dma_start(
                 out_2[0, 4 * q : 4 * q + 4, :].bitcast(I32), o_scales[32 * q : 32 * q + 4, :].bitcast(I32)
             )

@@ -21,6 +21,7 @@ PACK = 4
 QUADS = 4
 HALF = 512
 CHUNK = 256
+PIECES = [(0, 256), (256, 256), (512, 512)]
 
 
 def tile_list_modp_relu2_gateP_kernel(
@@ -35,65 +36,68 @@ def tile_list_modp_relu2_gateP_kernel(
             return offsets[:, start // 16 : (start + count) // 16]
 
         offsets = keep.tile([P, J // 16], U16, name="offsets")
-        tab_s = keep.tile([P, T], U8, name="tab_s", align_bytes=64)
-        tab_w = keep.tile([P, T], I32, name="tab_w", align_bytes=64)
-        w_s = keep.tile([P, 2, R], U8, name="w_s", tag="w_s", align_bytes=64)
-        wu_w = keep.tile([P, 2, R], I32, name="wu_w", align_bytes=64)
-        sm_t = keep.tile([P, PACK], F32, name="sm_t")
-        wgo_t = keep.tile([P, J], F32, name="wgo_t", align_bytes=64)
-        pick_s0 = keep.tile([P, J], U8, name="pick_s0", align_bytes=64)
-        pick_s1 = keep.tile([P, J], U8, name="pick_s1", align_bytes=64)
         g_src = gT.rearrange("(p t) c -> t p c", t=PACK)
 
-        def load_gates(t, tag):
-            rows = keep.tile([P, T], F32, name="g_rows%d" % t, tag=tag, align_bytes=64)
-            nc.sync.dma_start(rows[:], g_src[t])
-            return rows
+        tab_s = keep.tile([P, T], U8, name="tab_s", tag="tab_s", align_bytes=64)[:]
+        tab_w = keep.tile([P, T], I32, name="tab_w", tag="tab_w", align_bytes=64)
+        w_flat = keep.tile([P, 2 * R], U8, name="w_s", align_bytes=64)[:]
+        w_s = w_flat.rearrange("p (a r) -> p a r", a=2)
+        wu_w = keep.tile([P, 2, R], I32, name="wu_w", tag="wu_w", align_bytes=64)
+        pick_s0 = keep.tile([P, J], U8, name="pick_s0", align_bytes=64)
+        pick_s1 = keep.tile([P, J], U8, name="pick_s1", align_bytes=64)
 
-        def clear_page(t, tag, engine):
-            cleared = keep.tile([P, T], F32, name="page%d" % t, tag=tag, align_bytes=64)
+        def clear_page(cleared, engine):
             engine.memset(cleared[:].bitcast(I32), 0)
             return cleared
 
+        nc.vector.memset(w_flat.bitcast(I32), 0)
         wd_s = keep.tile([P, N], U8, name="wd_s", align_bytes=64)
-        wd_w = keep.tile([P, N], I32, name="wd_w", tag="wd_w", align_bytes=64)
-        nc.vector.memset(w_s[:].rearrange("p a r -> p (a r)").bitcast(I32), 0)
         nc.vector.memset(wd_s[:].bitcast(I32), 0)
         nc.vector.memset(pick_s1[:].bitcast(I32), 0)
-        page = [clear_page(0, "page0", nc.vector)]
+        page = [clear_page(keep.tile([P, T], F32, name="page0", align_bytes=64), nc.vector)]
 
         nc.sync.dma_start(offsets[:], offs)
         s_rows = tab_scales.rearrange("a q c -> (a q) c").bitcast(I32)
-        for q in range(QUADS):
-            for e in range(2):
-                first = 4 * q + 4 * e
-                nc.sync.dma_start(
-                    tab_s[32 * q + 16 * e : 32 * q + 16 * e + 16, :].bitcast(I32), s_rows[first : first + 16, :]
-                )
+        for first, rows, source in ((104, 24, 8), (0, 32, 0), (32, 16, 4), (48, 8, 20), (56, 32, 0), (88, 16, 4)):
+            (nc.scalar if rows == 24 else nc.sync).dma_start(
+                tab_s[first : first + rows, :].bitcast(I32), s_rows[source : source + rows, :]
+            )
         nc.sync.dma_start(tab_w[:], tab_words[0].rearrange("p c b -> p (c b)").bitcast(I32))
-        nc.sync.dma_start(wu_w[:], wu_words.rearrange("a p r b -> p a (r b)").bitcast(I32))
         for q in range(QUADS):
             nc.sync.dma_start(
                 w_s[32 * q : 32 * q + 4, :, :].bitcast(I32),
                 wu_scales[:, 4 * q : 4 * q + 4, :].rearrange("a s r -> s a r").bitcast(I32),
             )
+
+        nc.sync.dma_start(wu_w[:], wu_words.rearrange("a p r b -> p a (r b)").bitcast(I32))
+        wgo_t = keep.tile([P, J], F32, name="wgo_t", align_bytes=64)
+        sm_t = keep.tile([P, PACK], F32, name="sm_t", align_bytes=64)
         nc.sync.dma_start(sm_t[:], sm.rearrange("(p t) -> p t", t=PACK))
-        nc.sync.dma_start(wgo_t[:], wgo)
-        g_rows = {t: load_gates(t, "g%d" % t) for t in (3, 1)}
-        nc.sync.dma_start(wd_w[:], wd_words[0].rearrange("p n b -> p (n b)").bitcast(I32))
         for q in range(QUADS):
             nc.sync.dma_start(
                 wd_s[32 * q : 32 * q + 4, :].bitcast(I32), wd_scales[0, 4 * q : 4 * q + 4, :].bitcast(I32)
             )
-        for t in (0, 2):
-            g_rows[t] = load_gates(t, "g%d" % t)
+        nc.sync.dma_start(wgo_t[:], wgo)
 
-        nc.vector.tensor_copy(pick_s0[:], tab_s[:].indirect(offsets[:]))
-        nc.scalar.dma_start(pick_s1[0:100, :].bitcast(I32), pick_s0[28:P, :].bitcast(I32))
+        def load_gates(t):
+            rows = keep.tile([P, T], F32, name="g_rows%d" % t, tag="g_rows%d" % t, align_bytes=64)
+            nc.sync.dma_start(rows[:], g_src[t])
+            return rows
+
+        g_rows = [load_gates(0)]
+        wd_w = keep.tile([P, N], I32, name="wd_w", tag="wd_w", align_bytes=64)
+        nc.sync.dma_start(wd_w[:], wd_words[0].rearrange("p n b -> p (n b)").bitcast(I32))
+        g_rows.extend(load_gates(t) for t in range(1, PACK))
+
+        nc.vector.tensor_copy(pick_s0[:], tab_s.indirect(offsets[:]))
+        for first, source, rows in ((0, 16, 64), (64, 80, 4), (96, 124, 4)):
+            nc.scalar.dma_start(
+                pick_s1[first : first + rows, :].bitcast(I32), pick_s0[source : source + rows, :].bitcast(I32)
+            )
         pick_s = [pick_s0, pick_s1]
 
-        def pick_words(h, tag):
-            both = keep.tile([P, HALF], I32, name="both%d" % h, tag=tag, align_bytes=64)
+
+        def pick_words(h, both):
             nc.vector.tensor_copy(both[:].bitcast(U32), tab_w[:].bitcast(U32).indirect(entries(h * HALF, HALF)))
             parted = keep.tile([P, 2, 2 * HALF], U8, name="parted%d" % h, tag="parted%d" % h, align_bytes=64)
             nc.vector.tensor_copy(
@@ -101,24 +105,30 @@ def tile_list_modp_relu2_gateP_kernel(
             )
             return parted
 
-        parted = [pick_words(0, "both0")]
+        parted = [pick_words(0, keep.tile([P, HALF], I32, name="both0", tag="tab_s", align_bytes=64))]
+        ws_p = keep.tile([P, 2, PACK, P], U8, name="ws_p", align_bytes=64)
+        nc.vector.tensor_copy(ws_p[:], w_s.rearrange("p a (m t) -> p a t m", t=PACK))
         wu_p = keep.tile([P, 2, PACK, P], I32, name="wu_p", align_bytes=64)
         nc.vector.tensor_copy(
             wu_p[:].rearrange("p a t (c i) -> p a c t i", i=4),
             wu_w[:].rearrange("p a (c i t) -> p a c t i", i=4, t=PACK),
         )
-        ws_p = keep.tile([P, 2, PACK, P], U8, name="ws_p", align_bytes=64)
+
+        parted.append(pick_words(1, keep.tile([P, HALF], I32, name="both1", tag="wu_w", align_bytes=64)))
+        wd_p = keep.tile([P, PACK, P], I32, name="wd_p", tag="wu_w", align_bytes=64)
         nc.vector.tensor_copy(
-            ws_p[:], w_s[:].rearrange("p a (m t) -> p a t m", t=PACK)
+            wd_p[:].rearrange("p t (c i) -> p c t i", i=4), wd_w[:].rearrange("p (c i t) -> p c t i", i=4, t=PACK)
         )
-        parted.append(pick_words(1, "w_s"))
+        wds_p = keep.tile([P, PACK, P], U8, name="wds_p", align_bytes=64)
+        nc.vector.tensor_copy(wds_p[:], wd_s[:].rearrange("p (m t) -> p t m", t=PACK))
+        page.append(clear_page(keep.tile([P, T], F32, name="page1", tag="wd_w", align_bytes=64), nc.gpsimd))
 
         def bank(b, shape):
             return psum.tile(shape, F32, name="bank%d" % b, tag="bank%d" % b)
 
-        def up(h):
+        def up(h, planes):
             sums = []
-            for t in range(PACK):
+            for t in planes:
                 acc = bank(PACK * h + t, [P, HALF])
                 for a in range(2):
                     nc.tensor.matmul_mx(
@@ -133,43 +143,39 @@ def tile_list_modp_relu2_gateP_kernel(
                 sums.append(acc)
             return sums
 
-        def hidden(h, on_vector, tag):
-            pos = keep.tile([P, PACK, HALF], F32, name="pos%d" % h, align_bytes=64)
-            sq = keep.tile([P, PACK, HALF], F32, name="sq", tag="sq", align_bytes=64)
-            rows = keep.tile([P, PACK, HALF], BF16, name="rows%d" % h, tag=tag, align_bytes=64)
-            on_scalar = range(PACK - on_vector)
-            for t in range(PACK):
-                nc.scalar.activation(pos[:, t, :], sums[h][t][:], ACT.Relu)
-            for t in on_scalar:
-                nc.scalar.activation(sq[:, t, :], pos[:, t, :], ACT.Square)
-            for t in on_scalar:
-                nc.scalar.activation(rows[:, t, :], sq[:, t, :], ACT.Copy, scale=sm_t[:, t : t + 1])
-            for t in range(PACK - on_vector, PACK):
-                nc.vector.scalar_tensor_tensor(
-                    out=rows[:, t, :],
-                    in0=pos[:, t, :],
-                    scalar=sm_t[:, t : t + 1],
-                    in1=sums[h][t][:],
-                    op0=MULT,
-                    op1=MULT,
-                )
-            woven = keep.tile([P, HALF, PACK], BF16, name="woven%d" % h, tag="woven%d" % h, align_bytes=64)
+        def rectify(c, pos, t):
+            start, count = PIECES[c]
+            h, first = divmod(start, HALF)
+            nc.scalar.activation(pos[:, t, :], sums[h][t][:, first : first + count], ACT.Relu)
+
+        def square(pos, sq, planes):
+            nc.scalar.activation(sq[:, planes, :], pos[:, planes, :], ACT.Square)
+
+        def smooth(sq, rows, t):
+            nc.scalar.activation(rows[:, t, :], sq[:, t, :], ACT.Copy, scale=sm_t[:, t : t + 1])
+
+        def planes_tile(kind, c, dtype, tag):
+            return keep.tile([P, PACK, PIECES[c][1]], dtype, name="%s%d" % (kind, c), tag=tag, align_bytes=64)
+
+        def weave(c, rows):
+            woven = keep.tile([P, PIECES[c][1], PACK], BF16, name="woven%d" % c, tag="woven%d" % c, align_bytes=64)
             nc.scalar.copy(
                 woven[:].rearrange("p (c i) t -> p c t i", i=4), rows[:].rearrange("p t (c i) -> p c t i", i=4)
             )
             return woven
 
-        def down(h, woven):
-            codes = keep.tile([P, HALF], I32, name="h_codes%d" % h, align_bytes=64)
-            scales = keep.tile([P, HALF], U8, name="h_scales%d" % h, tag="h_scales%d" % h, align_bytes=64)
+        def down(c, woven, first_bank, pool, **place):
+            count = PIECES[c][1]
+            codes = pool.tile([P, count], I32, name="h_codes%d" % c, align_bytes=64, **place)
+            scales = keep.tile([P, count], U8, name="h_scales%d" % c, align_bytes=64)
             nc.vector.quantize_mx(
                 out=codes[:].bitcast(FP8X4), scales=scales[:], in_=woven[:].rearrange("p c t -> p (c t)")
             )
-            results = []
+            share = HALF // count
+            banks = [bank(first_bank + b, [P, share, count]) for b in range(PACK // share)]
             for t in range(PACK):
-                acc = bank(PACK * h + t, [P, HALF])
                 nc.tensor.matmul_mx(
-                    out=acc[:],
+                    out=banks[t // share][:, t % share, :],
                     lhsT=wd_p[:, t, :].bitcast(FP8X4),
                     lhsT_scale=wds_p[:, t, :],
                     rhs=codes[:].bitcast(FP8X4),
@@ -177,8 +183,17 @@ def tile_list_modp_relu2_gateP_kernel(
                     start=True,
                     stop=True,
                 )
-                results.append(acc)
-            return results
+            return banks
+
+        def drain(c, banks):
+            count = PIECES[c][1]
+            share = HALF // count
+            y = []
+            for b, acc in enumerate(banks):
+                held = keep.tile([P, share, count], F32, name="y%d_%d" % (c, b), tag="y%d_%d" % (c, b), align_bytes=64)
+                nc.scalar.copy(held[:], acc[:])
+                y.extend(held[:, i, :] for i in range(share))
+            return y
 
         def gates(t, start, count, tag):
             gate = keep.tile([P, count], F32, name="gate_%d_%d" % (t, start), tag=tag, align_bytes=64)
@@ -187,47 +202,66 @@ def tile_list_modp_relu2_gateP_kernel(
             )
             return gate
 
-        def put(t, start, count, y, gate):
-            nc.vector.tensor_tensor(page[t][:].indirect(entries(start, count)), y, gate, MULT)
+        def put(t, c, y, gate, first):
+            start, count = PIECES[c]
+            nc.vector.tensor_tensor(
+                page[t][:].indirect(entries(start, count)), y[t], gate[:, start - first : start - first + count], MULT
+            )
 
-        y = [keep.tile([P, J], F32, name="y%d" % t, align_bytes=64) for t in range(2)]
-        halves = [slice(h * HALF, (h + 1) * HALF) for h in range(2)]
+        sums = [up(0, range(PACK)), up(1, range(2))]
+        gate = [gates(0, 0, J, "gate0"), gates(1, 0, HALF, "gate1")]
 
-        def drain(h, results, t):
-            nc.scalar.copy(y[t][:, halves[h]], results[t][:])
+        pos = planes_tile("pos", 0, F32, "pos0")
+        sq = planes_tile("sq", 0, F32, "sq0")
+        rows = planes_tile("rows", 0, BF16, "rows0")
+        for t in range(PACK):
+            rectify(0, pos, t)
+            square(pos, sq, slice(t, t + 1))
+            smooth(sq, rows, t)
+        banks = down(0, weave(0, rows), 6, keep, tag="h_codes0")
+        y0 = drain(0, banks)
+        sums[1].extend(up(1, range(2, PACK)))
+        gate1_late = gates(1, HALF, HALF, "woven0")
+        gate.append(gates(2, 0, J, "gate2"))
+        page.append(clear_page(keep.tile([P, T], F32, name="page2", tag="h_codes0", align_bytes=64), nc.gpsimd))
+        page.append(clear_page(keep.tile([P, T], F32, name="page3", tag="g_rows2", align_bytes=64), nc.gpsimd))
+        for t in range(3):
+            put(t, 0, y0, gate[t], 0)
 
-        def put_early(h, results):
-            for t in range(2):
-                drain(h, results, t)
-                put(t, h * HALF, HALF, y[t][:, halves[h]], gate[t][:, halves[h]])
+        pos = planes_tile("pos", 1, F32, "rows0")
+        sq = planes_tile("sq", 1, F32, "sq1")
+        rows = planes_tile("rows", 1, BF16, "rows1")
+        for t in range(PACK):
+            rectify(1, pos, t)
+        for pair in range(2):
+            square(pos, sq, slice(2 * pair, 2 * pair + 2))
+        for t in range(PACK):
+            smooth(sq, rows, t)
+        banks = down(1, weave(1, rows), 0, keep, tag="y0_0")
+        gate_last = gates(3, 0, HALF, "woven1")
+        put(3, 0, y0, gate_last, 0)
+        pos = planes_tile("pos", 2, F32, "sq1")
+        sq = planes_tile("sq", 2, F32, "sq2")
+        rows = planes_tile("rows", 2, BF16, "rows2")
+        for t in range(PACK):
+            rectify(2, pos, t)
+        square(pos, sq, slice(0, 1))
+        y1 = drain(1, banks)
+        for t in range(3):
+            put(t, 1, y1, gate[t], 0)
+        put(3, 1, y1, gate_last, 0)
 
-        gate = {3: gates(3, 0, J, "gate3")}
-        sums = [up(0), up(1)]
-        woven = hidden(0, 2, "g3")
-        gate[1] = gates(1, 0, J, "gate1")
-        wd_p = keep.tile([P, PACK, P], I32, name="wd_p", align_bytes=64)
-        nc.vector.tensor_copy(
-            wd_p[:].rearrange("p t (c i) -> p c t i", i=4), wd_w[:].rearrange("p (c i t) -> p c t i", i=4, t=PACK)
-        )
-        wds_p = keep.tile([P, PACK, P], U8, name="wds_p", align_bytes=64)
-        nc.vector.tensor_copy(wds_p[:], wd_s[:].rearrange("p (m t) -> p t m", t=PACK))
-
-        results0 = down(0, woven)
-        gate[0] = gates(0, 0, J, "gate0")
-        page.append(clear_page(1, "g0", nc.gpsimd))
-        put_early(0, results0)
-        woven = hidden(1, 0, "rows1")
-        y.append(keep.tile([P, J], F32, name="y2", tag="rows1", align_bytes=64))
-        results1 = down(1, woven)
-        y.append(keep.tile([P, J], F32, name="y3", tag="h_scales1", align_bytes=64))
-        gate[2] = gates(2, 0, J, "woven1")
-        page.append(clear_page(2, "g2", nc.gpsimd))
-        put_early(1, results1)
-        page.append(clear_page(3, "gate0", nc.gpsimd))
-        for t in range(2, PACK):
-            drain(0, results0, t)
-            drain(1, results1, t)
-            put(t, 0, J, y[t][:], gate[t][:])
+        for t in range(1, PACK):
+            square(pos, sq, slice(t, t + 1))
+        for t in range(PACK):
+            smooth(sq, rows, t)
+        banks = down(2, weave(2, rows), 4, keep, tag="y1_0")
+        gate_last = gates(3, HALF, HALF, "woven2")
+        y2 = drain(2, banks)
+        put(0, 2, y2, gate[0], 0)
+        put(1, 2, y2, gate1_late, HALF)
+        put(2, 2, y2, gate[2], 0)
+        put(3, 2, y2, gate_last, HALF)
 
         out_rows = out_0.rearrange("(p t) c -> t p c", t=PACK)
         for t in range(PACK):
@@ -237,24 +271,22 @@ def tile_list_modp_relu2_gateP_kernel(
         words_out = out_1[0].rearrange("p c b -> p (c b)").bitcast(I32)
         split = T // 2
         chunks = [(c, HALF) for c in range(0, split, HALF)] + [(c, CHUNK) for c in range(split, T, CHUNK)]
-        woven_o = [keep.tile([P, n, PACK], BF16, name="woven_o%d" % c, align_bytes=64) for c, n in chunks]
-        rows_lo = keep.tile([P, 2, T], BF16, name="rows_lo", align_bytes=64)
-        rows_v = keep.tile([P, 2, split], BF16, name="rows_v", align_bytes=64)
-        rows_s = keep.tile([P, 2, T - split], BF16, name="rows_s", align_bytes=64)
-        pairs = "p t c -> p c t"
-        for t in range(2):
-            nc.scalar.copy(rows_lo[:, t, :], page[t][:])
-        for (c, n), woven in zip(chunks, woven_o):
-            nc.scalar.copy(woven[:, :, 0:2], rows_lo[:, :, c : c + n].rearrange(pairs))
-        nc.scalar.copy(rows_v[:, 0, :], page[2][:, 0:split])
-        nc.scalar.copy(rows_s[:, 0, :], page[2][:, split:T])
-        nc.vector.tensor_copy(rows_v[:, 1, :], page[3][:, 0:split])
-        nc.scalar.copy(rows_s[:, 1, :], page[3][:, split:T])
-        for (c, n), woven in zip(chunks, woven_o):
+        rows_v = keep.tile([P, PACK, split], BF16, name="rows_v", align_bytes=64)
+        rows_s = keep.tile([P, PACK, T - split], BF16, name="rows_s", align_bytes=64)
+        for t in range(3):
+            nc.scalar.copy(rows_v[:, t, :], page[t][:, 0:split])
+            nc.scalar.copy(rows_s[:, t, :], page[t][:, split:T])
+        nc.vector.tensor_copy(rows_v[:, 3, :], page[3][:, 0:split])
+        nc.scalar.copy(rows_s[:, 3, :], page[3][:, split:T])
+        woven_o = []
+        for c, n in chunks:
+            woven = keep.tile([P, n, PACK], BF16, name="woven_o%d" % c, align_bytes=64)
+            dst = woven[:].rearrange("p (c i) t -> p c t i", i=4)
             if c < split:
-                nc.vector.tensor_copy(woven[:, :, 2:4], rows_v[:, :, c : c + n].rearrange(pairs))
+                nc.vector.tensor_copy(dst, rows_v[:, :, c : c + n].rearrange("p t (c i) -> p c t i", i=4))
             else:
-                nc.scalar.copy(woven[:, :, 2:4], rows_s[:, :, c - split : c - split + n].rearrange(pairs))
+                nc.scalar.copy(dst, rows_s[:, :, c - split : c - split + n].rearrange("p t (c i) -> p c t i", i=4))
+            woven_o.append(woven)
         for (c, n), woven in zip(chunks, woven_o):
             o_codes = keep.tile([P, n], I32, name="o_codes%d" % c, align_bytes=64)
             nc.vector.quantize_mx(

@@ -30,6 +30,7 @@ def tile_list_modp_relu2_gateP_kernel(
     nc = tc.nc
     with ExitStack() as ctx:
         keep = ctx.enter_context(tc.tile_pool(name="keep", bufs=1))
+        laid = ctx.enter_context(tc.tile_pool(name="laid", bufs=1))
         psum = ctx.enter_context(tc.psum_pool(name="psum", bufs=1))
 
         def entries(start, count):
@@ -38,12 +39,12 @@ def tile_list_modp_relu2_gateP_kernel(
         offsets = keep.tile([P, J // 16], U16, name="offsets")
         g_src = gT.rearrange("(p t) c -> t p c", t=PACK)
 
-        tab_s = keep.tile([P, T], U8, name="tab_s", tag="tab_s", align_bytes=64)[:]
+        at_g = [None] + [5 * N + 4 * T * t for t in range(PACK - 1)]
+        tab_s = keep.tile([P, T], U8, name="tab_s", align_bytes=64)[:]
         tab_w = keep.tile([P, T], I32, name="tab_w", tag="tab_w", align_bytes=64)
-        w_flat = keep.tile([P, 2 * R], U8, name="w_s", align_bytes=64)[:]
+        w_flat = laid.tile([P, at_g[-1] + 4 * T], U8, name="w_s", align_bytes=64, offset=0)[:, 0 : 2 * R]
         w_s = w_flat.rearrange("p (a r) -> p a r", a=2)
         wu_w = keep.tile([P, 2, R], I32, name="wu_w", tag="wu_w", align_bytes=64)
-        pick_s0 = keep.tile([P, J], U8, name="pick_s0", align_bytes=64)
         pick_s1 = keep.tile([P, J], U8, name="pick_s1", align_bytes=64)
 
         def clear_page(cleared, engine):
@@ -51,17 +52,20 @@ def tile_list_modp_relu2_gateP_kernel(
             return cleared
 
         nc.vector.memset(w_flat.bitcast(I32), 0)
-        wd_s = keep.tile([P, N], U8, name="wd_s", align_bytes=64)
-        nc.vector.memset(wd_s[:].bitcast(I32), 0)
         nc.vector.memset(pick_s1[:].bitcast(I32), 0)
         page = [clear_page(keep.tile([P, T], F32, name="page0", align_bytes=64), nc.vector)]
 
         nc.sync.dma_start(offsets[:], offs)
         s_rows = tab_scales.rearrange("a q c -> (a q) c").bitcast(I32)
-        for first, rows, source in ((104, 24, 8), (0, 32, 0), (32, 16, 4), (48, 8, 20), (56, 32, 0), (88, 16, 4)):
-            (nc.scalar if rows == 24 else nc.sync).dma_start(
-                tab_s[first : first + rows, :].bitcast(I32), s_rows[source : source + rows, :]
-            )
+        for queue, first, rows, source in (
+            (nc.scalar, 56, 28, 0),
+            (nc.sync, 116, 12, 0),
+            (nc.sync, 0, 32, 0),
+            (nc.sync, 84, 32, 0),
+            (nc.sync, 32, 16, 4),
+            (nc.sync, 48, 8, 20),
+        ):
+            queue.dma_start(tab_s[first : first + rows, :].bitcast(I32), s_rows[source : source + rows, :])
         nc.sync.dma_start(tab_w[:], tab_words[0].rearrange("p c b -> p (c b)").bitcast(I32))
         for q in range(QUADS):
             nc.sync.dma_start(
@@ -72,81 +76,85 @@ def tile_list_modp_relu2_gateP_kernel(
         nc.sync.dma_start(wu_w[:], wu_words.rearrange("a p r b -> p a (r b)").bitcast(I32))
         wgo_t = keep.tile([P, J], F32, name="wgo_t", align_bytes=64)
         sm_t = keep.tile([P, PACK], F32, name="sm_t", align_bytes=64)
-        nc.sync.dma_start(sm_t[:], sm.rearrange("(p t) -> p t", t=PACK))
-        for q in range(QUADS):
-            nc.sync.dma_start(
-                wd_s[32 * q : 32 * q + 4, :].bitcast(I32), wd_scales[0, 4 * q : 4 * q + 4, :].bitcast(I32)
-            )
         nc.sync.dma_start(wgo_t[:], wgo)
+        g_rows = [keep.tile([P, T], F32, name="g_rows0", align_bytes=64)]
+        nc.sync.dma_start(g_rows[0][:], g_src[0])
+        nc.sync.dma_start(sm_t[:], sm.rearrange("(p t) -> p t", t=PACK))
 
-        def load_gates(t):
-            rows = keep.tile([P, T], F32, name="g_rows%d" % t, tag="g_rows%d" % t, align_bytes=64)
-            nc.sync.dma_start(rows[:], g_src[t])
-            return rows
+        def pick_scales(start, count):
+            picked = keep.tile([P, count], U8, name="pick_s0_%d" % start, align_bytes=64)
+            nc.vector.tensor_copy(picked[:], tab_s.indirect(entries(start, count)))
+            moved = pick_s1[:, start : start + count]
+            nc.scalar.dma_start(moved[0:112, :].bitcast(I32), picked[16:P, :].bitcast(I32))
+            return [picked[:], moved]
 
-        g_rows = [load_gates(0)]
-        wd_w = keep.tile([P, N], I32, name="wd_w", tag="wd_w", align_bytes=64)
-        nc.sync.dma_start(wd_w[:], wd_words[0].rearrange("p n b -> p (n b)").bitcast(I32))
-        g_rows.extend(load_gates(t) for t in range(1, PACK))
+        pick_s = [pick_scales(0, CHUNK), pick_scales(CHUNK, J - CHUNK)]
 
-        nc.vector.tensor_copy(pick_s0[:], tab_s.indirect(offsets[:]))
-        for first, source, rows in ((0, 16, 64), (64, 80, 4), (96, 124, 4)):
-            nc.scalar.dma_start(
-                pick_s1[first : first + rows, :].bitcast(I32), pick_s0[source : source + rows, :].bitcast(I32)
-            )
-        pick_s = [pick_s0, pick_s1]
-
-
-        def pick_words(h, both):
-            nc.vector.tensor_copy(both[:].bitcast(U32), tab_w[:].bitcast(U32).indirect(entries(h * HALF, HALF)))
-            parted = keep.tile([P, 2, 2 * HALF], U8, name="parted%d" % h, tag="parted%d" % h, align_bytes=64)
+        def pick_words(start, count, tag):
+            both = keep.tile([P, count], I32, name="both%d" % start, tag=tag, align_bytes=64)
+            nc.vector.tensor_copy(both[:].bitcast(U32), tab_w[:].bitcast(U32).indirect(entries(start, count)))
+            parted = keep.tile([P, 2, 2 * count], U8, name="parted%d" % start, align_bytes=64)
             nc.vector.tensor_copy(
                 parted[:].bitcast(U16), both[:].bitcast(U16).rearrange("p (j d) -> p d j", d=2)
             )
             return parted
 
-        parted = [pick_words(0, keep.tile([P, HALF], I32, name="both0", tag="tab_s", align_bytes=64))]
+        parted = [pick_words(0, CHUNK, "both0")]
         ws_p = keep.tile([P, 2, PACK, P], U8, name="ws_p", align_bytes=64)
         nc.vector.tensor_copy(ws_p[:], w_s.rearrange("p a (m t) -> p a t m", t=PACK))
+        def load_gates(t):
+            rows = laid.tile([P, T], F32, name="g_rows%d" % t, align_bytes=64, offset=at_g[t])
+            nc.sync.dma_start(rows[:], g_src[t])
+            return rows
+
+        g_rows.append(load_gates(1))
+        wd_w = laid.tile([P, N], I32, name="wd_w", align_bytes=64, offset=0)
+        nc.sync.dma_start(wd_w[:], wd_words[0].rearrange("p n b -> p (n b)").bitcast(I32))
+        wd_s = laid.tile([P, N], U8, name="wd_s", align_bytes=64, offset=4 * N)
+        nc.gpsimd.memset(wd_s[:].bitcast(I32), 0)
+        for q in range(QUADS):
+            nc.sync.dma_start(
+                wd_s[32 * q : 32 * q + 4, :].bitcast(I32), wd_scales[0, 4 * q : 4 * q + 4, :].bitcast(I32)
+            )
+        g_rows.append(load_gates(2))
+        g_rows.append(load_gates(3))
+
         wu_p = keep.tile([P, 2, PACK, P], I32, name="wu_p", align_bytes=64)
         nc.vector.tensor_copy(
             wu_p[:].rearrange("p a t (c i) -> p a c t i", i=4),
             wu_w[:].rearrange("p a (c i t) -> p a c t i", i=4, t=PACK),
         )
 
-        parted.append(pick_words(1, keep.tile([P, HALF], I32, name="both1", tag="wu_w", align_bytes=64)))
-        wd_p = keep.tile([P, PACK, P], I32, name="wd_p", tag="wu_w", align_bytes=64)
-        nc.vector.tensor_copy(
-            wd_p[:].rearrange("p t (c i) -> p c t i", i=4), wd_w[:].rearrange("p (c i t) -> p c t i", i=4, t=PACK)
-        )
-        wds_p = keep.tile([P, PACK, P], U8, name="wds_p", align_bytes=64)
-        nc.vector.tensor_copy(wds_p[:], wd_s[:].rearrange("p (m t) -> p t m", t=PACK))
-        page.append(clear_page(keep.tile([P, T], F32, name="page1", tag="wd_w", align_bytes=64), nc.gpsimd))
+        parted.append(pick_words(CHUNK, J - CHUNK, "wu_w"))
+        page.append(clear_page(keep.tile([P, T], F32, name="page1", tag="wu_w", align_bytes=64), nc.gpsimd))
 
         def bank(b, shape):
             return psum.tile(shape, F32, name="bank%d" % b, tag="bank%d" % b)
 
-        def up(h, planes):
-            sums = []
-            for t in planes:
-                acc = bank(PACK * h + t, [P, HALF])
-                for a in range(2):
-                    nc.tensor.matmul_mx(
-                        out=acc[:],
-                        lhsT=wu_p[:, a, t, :].bitcast(FP8X4),
-                        lhsT_scale=ws_p[:, a, t, :],
-                        rhs=parted[h][:, a, :].bitcast(FP4X4),
-                        rhs_scale=pick_s[a][:, h * HALF : (h + 1) * HALF],
-                        start=(a == 0),
-                        stop=(a == 1),
-                    )
-                sums.append(acc)
-            return sums
-
-        def rectify(c, pos, t):
+        def up(c, first_bank):
             start, count = PIECES[c]
-            h, first = divmod(start, HALF)
-            nc.scalar.activation(pos[:, t, :], sums[h][t][:, first : first + count], ACT.Relu)
+            part, first = (0, 0) if c == 0 else (1, start - CHUNK)
+            width = count if count == HALF else P
+            share = HALF // count
+            banks = [bank(first_bank + b, [P, share, count]) for b in range(PACK // share)]
+            for t in range(PACK):
+                for lo in range(0, count, width):
+                    for a in range(2):
+                        nc.tensor.matmul_mx(
+                            out=banks[t // share][:, t % share, lo : lo + width],
+                            lhsT=wu_p[:, a, t, :].bitcast(FP8X4),
+                            lhsT_scale=ws_p[:, a, t, :],
+                            rhs=parted[part][:, a, 2 * (first + lo) : 2 * (first + lo + width)].bitcast(FP4X4),
+                            rhs_scale=pick_s[part][a][:, first + lo : first + lo + width],
+                            start=(a == 0),
+                            stop=(a == 1),
+                        )
+            return banks
+
+        def rectify(sums, pos):
+            share = PACK // len(sums)
+            for b, acc in enumerate(sums):
+                nc.scalar.activation(pos[:, share * b : share * (b + 1), :], acc[:], ACT.Relu)
 
         def square(pos, sq, planes):
             nc.scalar.activation(sq[:, planes, :], pos[:, planes, :], ACT.Square)
@@ -164,10 +172,10 @@ def tile_list_modp_relu2_gateP_kernel(
             )
             return woven
 
-        def down(c, woven, first_bank, pool, **place):
+        def down(c, woven, first_bank, codes_tag, scales_tag):
             count = PIECES[c][1]
-            codes = pool.tile([P, count], I32, name="h_codes%d" % c, align_bytes=64, **place)
-            scales = keep.tile([P, count], U8, name="h_scales%d" % c, align_bytes=64)
+            codes = keep.tile([P, count], I32, name="h_codes%d" % c, tag=codes_tag, align_bytes=64)
+            scales = keep.tile([P, count], U8, name="h_scales%d" % c, tag=scales_tag, align_bytes=64)
             nc.vector.quantize_mx(
                 out=codes[:].bitcast(FP8X4), scales=scales[:], in_=woven[:].rearrange("p c t -> p (c t)")
             )
@@ -185,15 +193,10 @@ def tile_list_modp_relu2_gateP_kernel(
                 )
             return banks
 
-        def drain(c, banks):
-            count = PIECES[c][1]
-            share = HALF // count
-            y = []
-            for b, acc in enumerate(banks):
-                held = keep.tile([P, share, count], F32, name="y%d_%d" % (c, b), tag="y%d_%d" % (c, b), align_bytes=64)
-                nc.scalar.copy(held[:], acc[:])
-                y.extend(held[:, i, :] for i in range(share))
-            return y
+        def drain(name, acc):
+            held = keep.tile(acc.shape, F32, name=name, tag=name, align_bytes=64)
+            nc.scalar.copy(held[:], acc[:])
+            return held
 
         def gates(t, start, count, tag):
             gate = keep.tile([P, count], F32, name="gate_%d_%d" % (t, start), tag=tag, align_bytes=64)
@@ -202,66 +205,71 @@ def tile_list_modp_relu2_gateP_kernel(
             )
             return gate
 
-        def put(t, c, y, gate, first):
-            start, count = PIECES[c]
-            nc.vector.tensor_tensor(
-                page[t][:].indirect(entries(start, count)), y[t], gate[:, start - first : start - first + count], MULT
-            )
+        def put(t, start, count, y, gate):
+            nc.vector.tensor_tensor(page[t][:].indirect(entries(start, count)), y, gate, MULT)
 
-        sums = [up(0, range(PACK)), up(1, range(2))]
+        sums = [up(0, 0), up(1, 2), up(2, 4)]
         gate = [gates(0, 0, J, "gate0"), gates(1, 0, HALF, "gate1")]
+        wd_p = keep.tile([P, PACK, P], I32, name="wd_p", align_bytes=64)
+        nc.vector.tensor_copy(
+            wd_p[:].rearrange("p t (c i) -> p c t i", i=4), wd_w[:].rearrange("p (c i t) -> p c t i", i=4, t=PACK)
+        )
+        wds_p = keep.tile([P, PACK, P], U8, name="wds_p", align_bytes=64)
+        nc.vector.tensor_copy(wds_p[:], wd_s[:].rearrange("p (m t) -> p t m", t=PACK))
 
         pos = planes_tile("pos", 0, F32, "pos0")
         sq = planes_tile("sq", 0, F32, "sq0")
         rows = planes_tile("rows", 0, BF16, "rows0")
-        for t in range(PACK):
-            rectify(0, pos, t)
-            square(pos, sq, slice(t, t + 1))
-            smooth(sq, rows, t)
-        banks = down(0, weave(0, rows), 6, keep, tag="h_codes0")
-        y0 = drain(0, banks)
-        sums[1].extend(up(1, range(2, PACK)))
-        gate1_late = gates(1, HALF, HALF, "woven0")
-        gate.append(gates(2, 0, J, "gate2"))
-        page.append(clear_page(keep.tile([P, T], F32, name="page2", tag="h_codes0", align_bytes=64), nc.gpsimd))
-        page.append(clear_page(keep.tile([P, T], F32, name="page3", tag="g_rows2", align_bytes=64), nc.gpsimd))
-        for t in range(3):
-            put(t, 0, y0, gate[t], 0)
-
-        pos = planes_tile("pos", 1, F32, "rows0")
-        sq = planes_tile("sq", 1, F32, "sq1")
-        rows = planes_tile("rows", 1, BF16, "rows1")
-        for t in range(PACK):
-            rectify(1, pos, t)
+        rectify(sums[0], pos)
         for pair in range(2):
             square(pos, sq, slice(2 * pair, 2 * pair + 2))
         for t in range(PACK):
             smooth(sq, rows, t)
-        banks = down(1, weave(1, rows), 0, keep, tag="y0_0")
-        gate_last = gates(3, 0, HALF, "woven1")
-        put(3, 0, y0, gate_last, 0)
+        banks = down(0, weave(0, rows), 0, "h_codes0", "h_scales0")
+        y_low = drain("y0_0", banks[0])
+        y_high = keep.tile([P, 2, HALF], F32, name="y_high", align_bytes=64)
+        nc.scalar.copy(y_high[:, :, 0:CHUNK], banks[1][:])
+        gate1_late = gates(1, HALF, HALF, "woven0")
+        gate.append(gates(2, 0, CHUNK, "gate2"))
+        page.append(clear_page(keep.tile([P, T], F32, name="page2", tag="h_codes0", align_bytes=64), nc.gpsimd))
+        for t in range(2):
+            put(t, 0, CHUNK, y_low[:, t, :], gate[t][:, 0:CHUNK])
+        put(2, 0, CHUNK, y_high[:, 0, 0:CHUNK], gate[2][:])
+
+        pos = planes_tile("pos", 1, F32, "rows0")
+        sq = planes_tile("sq", 1, F32, "sq1")
+        rows = planes_tile("rows", 1, BF16, "rows1")
+        rectify(sums[1], pos)
+        for pair in range(2):
+            square(pos, sq, slice(2 * pair, 2 * pair + 2))
+        for t in range(PACK):
+            smooth(sq, rows, t)
+        banks = down(1, weave(1, rows), 2, "h_codes1", "y0_0")
+        gate2_late = gates(2, CHUNK, J - CHUNK, "woven1")
         pos = planes_tile("pos", 2, F32, "sq1")
         sq = planes_tile("sq", 2, F32, "sq2")
         rows = planes_tile("rows", 2, BF16, "rows2")
-        for t in range(PACK):
-            rectify(2, pos, t)
-        square(pos, sq, slice(0, 1))
-        y1 = drain(1, banks)
-        for t in range(3):
-            put(t, 1, y1, gate[t], 0)
-        put(3, 1, y1, gate_last, 0)
+        rectify(sums[2], pos)
+        square(pos, sq, slice(0, 2))
+        y_low = drain("y1_0", banks[0])
+        nc.scalar.copy(y_high[:, :, CHUNK:HALF], banks[1][:])
+        for t in range(2):
+            put(t, CHUNK, CHUNK, y_low[:, t, :], gate[t][:, CHUNK:HALF])
+        put(2, CHUNK, CHUNK, y_high[:, 0, CHUNK:HALF], gate2_late[:, 0:CHUNK])
 
-        for t in range(1, PACK):
-            square(pos, sq, slice(t, t + 1))
+        page.append(clear_page(keep.tile([P, T], F32, name="page3", tag="h_codes1", align_bytes=64), nc.gpsimd))
+        put(3, 0, HALF, y_high[:, 1, :], gates(3, 0, HALF, "y1_0")[:])
+
+        square(pos, sq, slice(2, 4))
         for t in range(PACK):
             smooth(sq, rows, t)
-        banks = down(2, weave(2, rows), 4, keep, tag="y1_0")
-        gate_last = gates(3, HALF, HALF, "woven2")
-        y2 = drain(2, banks)
-        put(0, 2, y2, gate[0], 0)
-        put(1, 2, y2, gate1_late, HALF)
-        put(2, 2, y2, gate[2], 0)
-        put(3, 2, y2, gate_last, HALF)
+        banks = down(2, weave(2, rows), 4, "h_codes2", "h_scales2")
+        gate3_late = gates(3, HALF, HALF, "woven2")
+        late = [gate[0][:, HALF:J], gate1_late[:], gate2_late[:, CHUNK:]]
+        y_late = [drain("y2_%d" % t, banks[t]) for t in range(PACK)]
+        for t in range(3):
+            put(t, HALF, HALF, y_late[t][:, 0, :], late[t])
+        put(3, HALF, HALF, y_late[3][:, 0, :], gate3_late[:])
 
         out_rows = out_0.rearrange("(p t) c -> t p c", t=PACK)
         for t in range(PACK):
@@ -269,8 +277,8 @@ def tile_list_modp_relu2_gateP_kernel(
 
         o_scales = keep.tile([P, T], U8, name="o_scales", align_bytes=64)
         words_out = out_1[0].rearrange("p c b -> p (c b)").bitcast(I32)
-        split = T // 2
-        chunks = [(c, HALF) for c in range(0, split, HALF)] + [(c, CHUNK) for c in range(split, T, CHUNK)]
+        split = T // 2 + P
+        chunks = [(c, HALF) for c in range(0, T // 2, HALF)] + [(c, CHUNK) for c in range(T // 2, T, CHUNK)]
         rows_v = keep.tile([P, PACK, split], BF16, name="rows_v", align_bytes=64)
         rows_s = keep.tile([P, PACK, T - split], BF16, name="rows_s", align_bytes=64)
         for t in range(3):
@@ -281,11 +289,17 @@ def tile_list_modp_relu2_gateP_kernel(
         woven_o = []
         for c, n in chunks:
             woven = keep.tile([P, n, PACK], BF16, name="woven_o%d" % c, align_bytes=64)
-            dst = woven[:].rearrange("p (c i) t -> p c t i", i=4)
-            if c < split:
-                nc.vector.tensor_copy(dst, rows_v[:, :, c : c + n].rearrange("p t (c i) -> p c t i", i=4))
-            else:
-                nc.scalar.copy(dst, rows_s[:, :, c - split : c - split + n].rearrange("p t (c i) -> p c t i", i=4))
+            mid = min(max(split, c), c + n)
+            if mid > c:
+                nc.vector.tensor_copy(
+                    woven[:, 0 : mid - c, :].rearrange("p (c i) t -> p c t i", i=4),
+                    rows_v[:, :, c:mid].rearrange("p t (c i) -> p c t i", i=4),
+                )
+            if mid < c + n:
+                nc.scalar.copy(
+                    woven[:, mid - c : n, :].rearrange("p (c i) t -> p c t i", i=4),
+                    rows_s[:, :, mid - split : c + n - split].rearrange("p t (c i) -> p c t i", i=4),
+                )
             woven_o.append(woven)
         for (c, n), woven in zip(chunks, woven_o):
             o_codes = keep.tile([P, n], I32, name="o_codes%d" % c, align_bytes=64)

@@ -39,10 +39,11 @@ def tile_list_modp_relu2_gateP_kernel(
         offsets = keep.tile([P, J // 16], U16, name="offsets")
         g_src = gT.rearrange("(p t) c -> t p c", t=PACK)
 
-        at_g = [None] + [5 * N + 4 * T * t for t in range(PACK - 1)]
+        at_tab_w = 8 * T
+        at_g = [None, 4 * T, at_tab_w, at_tab_w + 4 * T]
         tab_s = keep.tile([P, T], U8, name="tab_s", align_bytes=64)[:]
-        tab_w = keep.tile([P, T], I32, name="tab_w", tag="tab_w", align_bytes=64)
-        w_flat = laid.tile([P, at_g[-1] + 4 * T], U8, name="w_s", align_bytes=64, offset=0)[:, 0 : 2 * R]
+        tab_w = laid.tile([P, 2 * T], I32, name="tab_w", align_bytes=64, offset=at_tab_w)[:, 0:T]
+        w_flat = laid.tile([P, at_tab_w], U8, name="w_s", align_bytes=64, offset=0)[:, 0 : 2 * R]
         w_s = w_flat.rearrange("p (a r) -> p a r", a=2)
         wu_w = keep.tile([P, 2, R], I32, name="wu_w", tag="wu_w", align_bytes=64)
         pick_s1 = keep.tile([P, J], U8, name="pick_s1", align_bytes=64)
@@ -66,7 +67,7 @@ def tile_list_modp_relu2_gateP_kernel(
             (nc.sync, 48, 8, 20),
         ):
             queue.dma_start(tab_s[first : first + rows, :].bitcast(I32), s_rows[source : source + rows, :])
-        nc.sync.dma_start(tab_w[:], tab_words[0].rearrange("p c b -> p (c b)").bitcast(I32))
+        nc.sync.dma_start(tab_w, tab_words[0].rearrange("p c b -> p (c b)").bitcast(I32))
         for q in range(QUADS):
             nc.sync.dma_start(
                 w_s[32 * q : 32 * q + 4, :, :].bitcast(I32),
@@ -92,7 +93,7 @@ def tile_list_modp_relu2_gateP_kernel(
 
         def pick_words(start, count, tag):
             both = keep.tile([P, count], I32, name="both%d" % start, tag=tag, align_bytes=64)
-            nc.vector.tensor_copy(both[:].bitcast(U32), tab_w[:].bitcast(U32).indirect(entries(start, count)))
+            nc.vector.tensor_copy(both[:].bitcast(U32), tab_w.bitcast(U32).indirect(entries(start, count)))
             parted = keep.tile([P, 2, 2 * count], U8, name="parted%d" % start, align_bytes=64)
             nc.vector.tensor_copy(
                 parted[:].bitcast(U16), both[:].bitcast(U16).rearrange("p (j d) -> p d j", d=2)
@@ -110,14 +111,6 @@ def tile_list_modp_relu2_gateP_kernel(
         g_rows.append(load_gates(1))
         wd_w = laid.tile([P, N], I32, name="wd_w", align_bytes=64, offset=0)
         nc.sync.dma_start(wd_w[:], wd_words[0].rearrange("p n b -> p (n b)").bitcast(I32))
-        wd_s = laid.tile([P, N], U8, name="wd_s", align_bytes=64, offset=4 * N)
-        nc.gpsimd.memset(wd_s[:].bitcast(I32), 0)
-        for q in range(QUADS):
-            nc.sync.dma_start(
-                wd_s[32 * q : 32 * q + 4, :].bitcast(I32), wd_scales[0, 4 * q : 4 * q + 4, :].bitcast(I32)
-            )
-        g_rows.append(load_gates(2))
-        g_rows.append(load_gates(3))
 
         wu_p = keep.tile([P, 2, PACK, P], I32, name="wu_p", align_bytes=64)
         nc.vector.tensor_copy(
@@ -125,7 +118,14 @@ def tile_list_modp_relu2_gateP_kernel(
             wu_w[:].rearrange("p a (c i t) -> p a c t i", i=4, t=PACK),
         )
 
+        wd_s = keep.tile([P, N], U8, name="wd_s", tag="both0", align_bytes=64)
+        nc.gpsimd.memset(wd_s[:].bitcast(I32), 0)
+        for q in range(QUADS):
+            nc.sync.dma_start(
+                wd_s[32 * q : 32 * q + 4, :].bitcast(I32), wd_scales[0, 4 * q : 4 * q + 4, :].bitcast(I32)
+            )
         parted.append(pick_words(CHUNK, J - CHUNK, "wu_w"))
+        g_rows.extend(load_gates(t) for t in range(2, PACK))
         page.append(clear_page(keep.tile([P, T], F32, name="page1", tag="wu_w", align_bytes=64), nc.gpsimd))
 
         def bank(b, shape):
@@ -172,9 +172,8 @@ def tile_list_modp_relu2_gateP_kernel(
             )
             return woven
 
-        def down(c, woven, first_bank, codes_tag, scales_tag):
+        def down(c, woven, first_bank, codes, scales_tag):
             count = PIECES[c][1]
-            codes = keep.tile([P, count], I32, name="h_codes%d" % c, tag=codes_tag, align_bytes=64)
             scales = keep.tile([P, count], U8, name="h_scales%d" % c, tag=scales_tag, align_bytes=64)
             nc.vector.quantize_mx(
                 out=codes[:].bitcast(FP8X4), scales=scales[:], in_=woven[:].rearrange("p c t -> p (c t)")
@@ -225,51 +224,53 @@ def tile_list_modp_relu2_gateP_kernel(
             square(pos, sq, slice(2 * pair, 2 * pair + 2))
         for t in range(PACK):
             smooth(sq, rows, t)
-        banks = down(0, weave(0, rows), 0, "h_codes0", "h_scales0")
+        banks = down(0, weave(0, rows), 0, laid.tile([P, CHUNK], I32, name="h_codes0", align_bytes=64, offset=0), "both0")
         y_low = drain("y0_0", banks[0])
-        y_high = keep.tile([P, 2, HALF], F32, name="y_high", align_bytes=64)
+        y_high = keep.tile([P, 2, J], F32, name="y_high", align_bytes=64)
         nc.scalar.copy(y_high[:, :, 0:CHUNK], banks[1][:])
         gate1_late = gates(1, HALF, HALF, "woven0")
         gate.append(gates(2, 0, CHUNK, "gate2"))
-        page.append(clear_page(keep.tile([P, T], F32, name="page2", tag="h_codes0", align_bytes=64), nc.gpsimd))
+        page.append(clear_page(keep.tile([P, T], F32, name="page2", tag="both0", align_bytes=64), nc.gpsimd))
         for t in range(2):
             put(t, 0, CHUNK, y_low[:, t, :], gate[t][:, 0:CHUNK])
         put(2, 0, CHUNK, y_high[:, 0, 0:CHUNK], gate[2][:])
 
         pos = planes_tile("pos", 1, F32, "rows0")
-        sq = planes_tile("sq", 1, F32, "sq1")
+        sq = laid.tile([P, PACK, CHUNK], F32, name="sq1", align_bytes=64, offset=0)
         rows = planes_tile("rows", 1, BF16, "rows1")
         rectify(sums[1], pos)
         for pair in range(2):
             square(pos, sq, slice(2 * pair, 2 * pair + 2))
         for t in range(PACK):
             smooth(sq, rows, t)
-        banks = down(1, weave(1, rows), 2, "h_codes1", "y0_0")
+        banks = down(1, weave(1, rows), 2, keep.tile([P, CHUNK], I32, name="h_codes1", tag="gate2", align_bytes=64), "y0_0")
         gate2_late = gates(2, CHUNK, J - CHUNK, "woven1")
-        pos = planes_tile("pos", 2, F32, "sq1")
+        pos = laid.tile([P, PACK, HALF], F32, name="pos2", align_bytes=64, offset=0)
         sq = planes_tile("sq", 2, F32, "sq2")
         rows = planes_tile("rows", 2, BF16, "rows2")
         rectify(sums[2], pos)
-        square(pos, sq, slice(0, 2))
         y_low = drain("y1_0", banks[0])
         nc.scalar.copy(y_high[:, :, CHUNK:HALF], banks[1][:])
         for t in range(2):
             put(t, CHUNK, CHUNK, y_low[:, t, :], gate[t][:, CHUNK:HALF])
         put(2, CHUNK, CHUNK, y_high[:, 0, CHUNK:HALF], gate2_late[:, 0:CHUNK])
 
-        page.append(clear_page(keep.tile([P, T], F32, name="page3", tag="h_codes1", align_bytes=64), nc.gpsimd))
-        put(3, 0, HALF, y_high[:, 1, :], gates(3, 0, HALF, "y1_0")[:])
+        page.append(clear_page(keep.tile([P, T], F32, name="page3", tag="gate2", align_bytes=64), nc.gpsimd))
+        put(3, 0, CHUNK, y_high[:, 1, 0:CHUNK], gates(3, 0, CHUNK, "y1_0")[:])
 
-        square(pos, sq, slice(2, 4))
+        for pair in range(2):
+            square(pos, sq, slice(2 * pair, 2 * pair + 2))
         for t in range(PACK):
             smooth(sq, rows, t)
-        banks = down(2, weave(2, rows), 4, "h_codes2", "h_scales2")
-        gate3_late = gates(3, HALF, HALF, "woven2")
-        late = [gate[0][:, HALF:J], gate1_late[:], gate2_late[:, CHUNK:]]
-        y_late = [drain("y2_%d" % t, banks[t]) for t in range(PACK)]
-        for t in range(3):
-            put(t, HALF, HALF, y_late[t][:, 0, :], late[t])
-        put(3, HALF, HALF, y_late[3][:, 0, :], gate3_late[:])
+        banks = down(2, weave(2, rows), 4, keep.tile([P, HALF], I32, name="h_codes2", align_bytes=64), "h_scales2")
+        gate3_late = gates(3, CHUNK, J - CHUNK, "woven2")
+        y_late = [drain("y2_%d" % t, banks[t])[:, 0, :] for t in range(2)]
+        for t in range(2):
+            nc.scalar.copy(y_high[:, t, HALF:J], banks[2 + t][:, 0, :])
+        put(0, HALF, HALF, y_late[0], gate[0][:, HALF:J])
+        put(1, HALF, HALF, y_late[1], gate1_late[:])
+        put(2, HALF, HALF, y_high[:, 0, HALF:J], gate2_late[:, CHUNK:])
+        put(3, CHUNK, J - CHUNK, y_high[:, 1, CHUNK:J], gate3_late[:])
 
         out_rows = out_0.rearrange("(p t) c -> t p c", t=PACK)
         for t in range(PACK):
@@ -284,31 +285,39 @@ def tile_list_modp_relu2_gateP_kernel(
         for t in range(3):
             nc.scalar.copy(rows_v[:, t, :], page[t][:, 0:split])
             nc.scalar.copy(rows_s[:, t, :], page[t][:, split:T])
-        nc.vector.tensor_copy(rows_v[:, 3, :], page[3][:, 0:split])
-        nc.scalar.copy(rows_s[:, 3, :], page[3][:, split:T])
-        woven_o = []
-        for c, n in chunks:
-            woven = keep.tile([P, n, PACK], BF16, name="woven_o%d" % c, align_bytes=64)
-            mid = min(max(split, c), c + n)
-            if mid > c:
-                nc.vector.tensor_copy(
-                    woven[:, 0 : mid - c, :].rearrange("p (c i) t -> p c t i", i=4),
-                    rows_v[:, :, c:mid].rearrange("p t (c i) -> p c t i", i=4),
-                )
-            if mid < c + n:
-                nc.scalar.copy(
-                    woven[:, mid - c : n, :].rearrange("p (c i) t -> p c t i", i=4),
-                    rows_s[:, :, mid - split : c + n - split].rearrange("p t (c i) -> p c t i", i=4),
-                )
-            woven_o.append(woven)
-        for (c, n), woven in zip(chunks, woven_o):
-            o_codes = keep.tile([P, n], I32, name="o_codes%d" % c, align_bytes=64)
-            nc.vector.quantize_mx(
-                out=o_codes[:].bitcast(FP8X4),
-                scales=o_scales[:, c : c + n],
-                in_=woven[:].rearrange("p c t -> p (c t)"),
+        woven_o = [keep.tile([P, n, PACK], BF16, name="woven_o%d" % c, align_bytes=64) for c, n in chunks]
+        o_codes = keep.tile([P, T], I32, name="o_codes", align_bytes=64)
+
+        def weave_out(engine_copy, k, rows, first, lo, hi):
+            c = chunks[k][0]
+            engine_copy(
+                woven_o[k][:, lo - c : hi - c, :].rearrange("p (c i) t -> p c t i", i=4),
+                rows[:, :, lo - first : hi - first].rearrange("p t (c i) -> p c t i", i=4),
             )
-            nc.sync.dma_start(words_out[:, c : c + n], o_codes[:])
+
+        def planes(k):
+            c, n = chunks[k]
+            nc.vector.quantize_mx(
+                out=o_codes[:, c : c + n].bitcast(FP8X4),
+                scales=o_scales[:, c : c + n],
+                in_=woven_o[k][:].rearrange("p c t -> p (c t)"),
+            )
+            nc.sync.dma_start(words_out[:, c : c + n], o_codes[:, c : c + n])
+
+        nc.scalar.copy(rows_s[:, 3, :], page[3][:, split:T])
+        for k in (3, 4, 2, 5):
+            c, n = chunks[k]
+            weave_out(nc.scalar.copy, k, rows_s, split, max(c, split), c + n)
+        nc.vector.tensor_copy(rows_v[:, 3, 0:HALF], page[3][:, 0:HALF])
+        weave_out(nc.vector.tensor_copy, 0, rows_v, 0, 0, HALF)
+        nc.vector.tensor_copy(rows_v[:, 3, HALF:split], page[3][:, HALF:split])
+        planes(0)
+        weave_out(nc.vector.tensor_copy, 1, rows_v, 0, HALF, 2 * HALF)
+        planes(3)
+        planes(1)
+        weave_out(nc.vector.tensor_copy, 2, rows_v, 0, 2 * HALF, split)
+        for k in (4, 2, 5):
+            planes(k)
         for q in range(QUADS):
             (nc.scalar if q % 2 else nc.sync).dma_start(
                 out_2[0, 4 * q : 4 * q + 4, :].bitcast(I32), o_scales[32 * q : 32 * q + 4, :].bitcast(I32)

@@ -1,6 +1,7 @@
 from contextlib import ExitStack
 
 import concourse.mybir as mybir
+from concourse.masks import make_identity
 
 K, R, N, T, J = 1024, 512, 512, 2048, 1024
 FLOPS = 2 * K * R * J + 2 * R * N * J
@@ -21,7 +22,7 @@ PACK = 4
 QUADS = 4
 HALF = 512
 CHUNK = 256
-PIECES = [(0, 256), (256, 256), (512, 512)]
+PIECES = J // CHUNK
 
 
 def tile_list_modp_relu2_gateP_kernel(
@@ -39,22 +40,33 @@ def tile_list_modp_relu2_gateP_kernel(
         offsets = keep.tile([P, J // 16], U16, name="offsets")
         g_src = gT.rearrange("(p t) c -> t p c", t=PACK)
 
-        at_tab_w = 8 * T
-        at_g = [None, 4 * T, at_tab_w, at_tab_w + 4 * T]
-        tab_s = keep.tile([P, T], U8, name="tab_s", align_bytes=64)[:]
-        tab_w = laid.tile([P, 2 * T], I32, name="tab_w", align_bytes=64, offset=at_tab_w)[:, 0:T]
-        w_flat = laid.tile([P, at_tab_w], U8, name="w_s", align_bytes=64, offset=0)[:, 0 : 2 * R]
-        w_s = w_flat.rearrange("p (a r) -> p a r", a=2)
-        wu_w = keep.tile([P, 2, R], I32, name="wu_w", tag="wu_w", align_bytes=64)
+        at_wd_w = T + 8 * T
+        at_g = [None, T, T + 4 * T, at_wd_w + 4 * N]
+        at_both = at_g[3] + 4 * T
+        at_wd_s = at_both + 4 * T
+        tab_s = laid.tile([P, at_both], U8, name="tab_s", align_bytes=64, offset=0)[:, 0:T]
+        tab_w = keep.tile([P, T], I32, name="tab_w", align_bytes=64)[:]
+        w_s = keep.tile([P, 2, R], U8, name="w_s", align_bytes=64)
+        wd_s = laid.tile([P, N], U8, name="wd_s", align_bytes=64, offset=at_wd_s)
+        wu_w = keep.tile([P, 2, R], I32, name="wu_w", align_bytes=64)
         pick_s1 = keep.tile([P, J], U8, name="pick_s1", align_bytes=64)
+        ident = keep.tile([P, P], F32, name="ident", align_bytes=64)
 
         def clear_page(cleared, engine):
             engine.memset(cleared[:].bitcast(I32), 0)
             return cleared
 
-        nc.vector.memset(w_flat.bitcast(I32), 0)
+        nc.vector.memset(w_s[:].rearrange("p a r -> p (a r)").bitcast(I32), 0)
         nc.vector.memset(pick_s1[:].bitcast(I32), 0)
         page = [clear_page(keep.tile([P, T], F32, name="page0", align_bytes=64), nc.vector)]
+        nc.gpsimd.memset(wd_s[:].bitcast(I32), 0)
+        make_identity(nc, ident[:])
+        sm_t = keep.tile([P, PACK], F32, name="sm_t", align_bytes=64)
+        nc.gpsimd.dma_start(sm_t[:], sm.rearrange("(p t) -> p t", t=PACK))
+        for q in range(QUADS):
+            nc.gpsimd.dma_start(
+                wd_s[32 * q : 32 * q + 4, :].bitcast(I32), wd_scales[0, 4 * q : 4 * q + 4, :].bitcast(I32)
+            )
 
         nc.sync.dma_start(offsets[:], offs)
         s_rows = tab_scales.rearrange("a q c -> (a q) c").bitcast(I32)
@@ -73,14 +85,9 @@ def tile_list_modp_relu2_gateP_kernel(
                 w_s[32 * q : 32 * q + 4, :, :].bitcast(I32),
                 wu_scales[:, 4 * q : 4 * q + 4, :].rearrange("a s r -> s a r").bitcast(I32),
             )
-
         nc.sync.dma_start(wu_w[:], wu_words.rearrange("a p r b -> p a (r b)").bitcast(I32))
         wgo_t = keep.tile([P, J], F32, name="wgo_t", align_bytes=64)
-        sm_t = keep.tile([P, PACK], F32, name="sm_t", align_bytes=64)
         nc.sync.dma_start(wgo_t[:], wgo)
-        g_rows = [keep.tile([P, T], F32, name="g_rows0", align_bytes=64)]
-        nc.sync.dma_start(g_rows[0][:], g_src[0])
-        nc.sync.dma_start(sm_t[:], sm.rearrange("(p t) -> p t", t=PACK))
 
         def pick_scales(start, count):
             picked = keep.tile([P, count], U8, name="pick_s0_%d" % start, align_bytes=64)
@@ -91,8 +98,19 @@ def tile_list_modp_relu2_gateP_kernel(
 
         pick_s = [pick_scales(0, CHUNK), pick_scales(CHUNK, J - CHUNK)]
 
-        def pick_words(start, count, tag):
-            both = keep.tile([P, count], I32, name="both%d" % start, tag=tag, align_bytes=64)
+        def load_gates(t, rows):
+            nc.sync.dma_start(rows[:], g_src[t])
+            return rows
+
+        g_rows = [load_gates(0, keep.tile([P, T], F32, name="g_rows0", tag="g_rows0", align_bytes=64))]
+        g_rows.append(load_gates(1, laid.tile([P, T], F32, name="g_rows1", align_bytes=64, offset=at_g[1])))
+        g_rows.append(load_gates(2, laid.tile([P, T], F32, name="g_rows2", align_bytes=64, offset=at_g[2])))
+        wd_w = laid.tile([P, N], I32, name="wd_w", align_bytes=64, offset=at_wd_w)
+        nc.sync.dma_start(wd_w[:], wd_words[0].rearrange("p n b -> p (n b)").bitcast(I32))
+        g_rows.append(load_gates(3, laid.tile([P, T], F32, name="g_rows3", align_bytes=64, offset=at_g[3])))
+
+        def pick_words(start, both):
+            count = both.shape[1]
             nc.vector.tensor_copy(both[:].bitcast(U32), tab_w.bitcast(U32).indirect(entries(start, count)))
             parted = keep.tile([P, 2, 2 * count], U8, name="parted%d" % start, align_bytes=64)
             nc.vector.tensor_copy(
@@ -100,177 +118,147 @@ def tile_list_modp_relu2_gateP_kernel(
             )
             return parted
 
-        parted = [pick_words(0, CHUNK, "both0")]
-        ws_p = keep.tile([P, 2, PACK, P], U8, name="ws_p", align_bytes=64)
-        nc.vector.tensor_copy(ws_p[:], w_s.rearrange("p a (m t) -> p a t m", t=PACK))
-        def load_gates(t):
-            rows = laid.tile([P, T], F32, name="g_rows%d" % t, align_bytes=64, offset=at_g[t])
-            nc.sync.dma_start(rows[:], g_src[t])
-            return rows
+        parted = [
+            pick_words(0, keep.tile([P, CHUNK], I32, name="both0", align_bytes=64)),
+            pick_words(CHUNK, laid.tile([P, J - CHUNK], I32, name="both1", align_bytes=64, offset=at_both)),
+        ]
+        page.append(clear_page(laid.tile([P, T], F32, name="page1", align_bytes=64, offset=at_both), nc.gpsimd))
 
-        g_rows.append(load_gates(1))
-        wd_w = laid.tile([P, N], I32, name="wd_w", align_bytes=64, offset=0)
-        nc.sync.dma_start(wd_w[:], wd_words[0].rearrange("p n b -> p (n b)").bitcast(I32))
+        def gates(t, tag):
+            gate = keep.tile([P, J], F32, name="gate%d" % t, tag=tag, align_bytes=64)
+            nc.vector.tensor_tensor(gate[:], g_rows[t][:].indirect(offsets[:]), wgo_t[:], MULT)
+            return gate
 
-        wu_p = keep.tile([P, 2, PACK, P], I32, name="wu_p", align_bytes=64)
+        gate = [gates(0, "gate0")]
+        page.append(clear_page(keep.tile([P, T], F32, name="page2", tag="g_rows0", align_bytes=64), nc.gpsimd))
+        gate.extend(gates(t, "gate%d" % t) for t in (1, 2))
+        wds_p = laid.tile([P, PACK, P], U8, name="wds_p", align_bytes=64, offset=at_g[2])
+        nc.vector.tensor_copy(wds_p[:], wd_s[:].rearrange("p (m t) -> p t m", t=PACK))
+        wd_p = keep.tile([P, PACK, P], I32, name="wd_p", align_bytes=64)
         nc.vector.tensor_copy(
-            wu_p[:].rearrange("p a t (c i) -> p a c t i", i=4),
-            wu_w[:].rearrange("p a (c i t) -> p a c t i", i=4, t=PACK),
+            wd_p[:].rearrange("p t (c i) -> p c t i", i=4), wd_w[:].rearrange("p (c i t) -> p c t i", i=4, t=PACK)
         )
 
-        wd_s = keep.tile([P, N], U8, name="wd_s", tag="both0", align_bytes=64)
-        nc.gpsimd.memset(wd_s[:].bitcast(I32), 0)
-        for q in range(QUADS):
-            nc.sync.dma_start(
-                wd_s[32 * q : 32 * q + 4, :].bitcast(I32), wd_scales[0, 4 * q : 4 * q + 4, :].bitcast(I32)
-            )
-        parted.append(pick_words(CHUNK, J - CHUNK, "wu_w"))
-        g_rows.extend(load_gates(t) for t in range(2, PACK))
-        page.append(clear_page(keep.tile([P, T], F32, name="page1", tag="wu_w", align_bytes=64), nc.gpsimd))
+        def bank(tag, shape):
+            return psum.tile(shape, F32, name=tag, tag=tag)
 
-        def bank(b, shape):
-            return psum.tile(shape, F32, name="bank%d" % b, tag="bank%d" % b)
+        def squares(k):
+            sq = keep.tile([P, PACK, CHUNK], F32, name="sq%d" % k, tag="sq%d" % k, align_bytes=64)
+            part, first = (0, 0) if k == 0 else (1, CHUNK * (k - 1))
+            turned = []
+            for b in range(2):
+                lo = first + P * b
+                sums = bank("up%d" % b, [P, R])
+                for a in range(2):
+                    nc.tensor.matmul_mx(
+                        out=sums[:],
+                        lhsT=parted[part][:, a, 2 * lo : 2 * (lo + P)].bitcast(FP4X4),
+                        lhsT_scale=pick_s[part][a][:, lo : lo + P],
+                        rhs=wu_w[:, a, :].bitcast(FP8X4),
+                        rhs_scale=w_s[:, a, :],
+                        start=(a == 0),
+                        stop=(a == 1),
+                    )
+                pos = keep.tile([P, PACK, P], F32, name="pos%d" % b, tag="pos%d" % b, align_bytes=64)
+                nc.scalar.activation(pos[:], sums[:].rearrange("p (m t) -> p t m", t=PACK), ACT.Relu)
+                turned.append(bank("turn%d_%d" % (k % 2, b), [P, PACK, P]))
+                for t in range(PACK):
+                    nc.tensor.transpose(turned[b][:, t, :], pos[:, t, :], ident[:])
+            for b in range(2):
+                nc.scalar.activation(sq[:, :, P * b : P * (b + 1)], turned[b][:], ACT.Square)
+            return sq
 
-        def up(c, first_bank):
-            start, count = PIECES[c]
-            part, first = (0, 0) if c == 0 else (1, start - CHUNK)
-            width = count if count == HALF else P
-            share = HALF // count
-            banks = [bank(first_bank + b, [P, share, count]) for b in range(PACK // share)]
+        def smooth(k, sq):
+            rows = keep.tile([P, PACK, CHUNK], BF16, name="rows%d" % k, tag="rows%d" % k, align_bytes=64)
             for t in range(PACK):
-                for lo in range(0, count, width):
-                    for a in range(2):
-                        nc.tensor.matmul_mx(
-                            out=banks[t // share][:, t % share, lo : lo + width],
-                            lhsT=wu_p[:, a, t, :].bitcast(FP8X4),
-                            lhsT_scale=ws_p[:, a, t, :],
-                            rhs=parted[part][:, a, 2 * (first + lo) : 2 * (first + lo + width)].bitcast(FP4X4),
-                            rhs_scale=pick_s[part][a][:, first + lo : first + lo + width],
-                            start=(a == 0),
-                            stop=(a == 1),
-                        )
-            return banks
+                nc.scalar.activation(rows[:, t, :], sq[:, t, :], ACT.Copy, scale=sm_t[:, t : t + 1])
+            return rows
 
-        def rectify(sums, pos):
-            share = PACK // len(sums)
-            for b, acc in enumerate(sums):
-                nc.scalar.activation(pos[:, share * b : share * (b + 1), :], acc[:], ACT.Relu)
-
-        def square(pos, sq, planes):
-            nc.scalar.activation(sq[:, planes, :], pos[:, planes, :], ACT.Square)
-
-        def smooth(sq, rows, t):
-            nc.scalar.activation(rows[:, t, :], sq[:, t, :], ACT.Copy, scale=sm_t[:, t : t + 1])
-
-        def planes_tile(kind, c, dtype, tag):
-            return keep.tile([P, PACK, PIECES[c][1]], dtype, name="%s%d" % (kind, c), tag=tag, align_bytes=64)
-
-        def weave(c, rows):
-            woven = keep.tile([P, PIECES[c][1], PACK], BF16, name="woven%d" % c, tag="woven%d" % c, align_bytes=64)
+        def weave(rows, woven):
             nc.scalar.copy(
                 woven[:].rearrange("p (c i) t -> p c t i", i=4), rows[:].rearrange("p t (c i) -> p c t i", i=4)
             )
             return woven
 
-        def down(c, woven, first_bank, codes, scales_tag):
-            count = PIECES[c][1]
-            scales = keep.tile([P, count], U8, name="h_scales%d" % c, tag=scales_tag, align_bytes=64)
+        def quantise(woven, codes, scales):
             nc.vector.quantize_mx(
                 out=codes[:].bitcast(FP8X4), scales=scales[:], in_=woven[:].rearrange("p c t -> p (c t)")
             )
-            share = HALF // count
-            banks = [bank(first_bank + b, [P, share, count]) for b in range(PACK // share)]
+            return codes, scales
+
+        def h_tiles(k):
+            return (
+                keep.tile([P, CHUNK], I32, name="h_codes%d" % k, tag="h_codes%d" % k, align_bytes=64),
+                keep.tile([P, CHUNK], U8, name="h_scales%d" % k, align_bytes=64),
+            )
+
+        def woven_tile(k, tag):
+            return keep.tile([P, CHUNK, PACK], BF16, name="woven%d" % k, tag=tag, align_bytes=64)
+
+        def down(h, kind):
+            banks = [bank("%s%d" % (kind, b), [P, 2, CHUNK]) for b in range(2)]
             for t in range(PACK):
                 nc.tensor.matmul_mx(
-                    out=banks[t // share][:, t % share, :],
+                    out=banks[t // 2][:, t % 2, :],
                     lhsT=wd_p[:, t, :].bitcast(FP8X4),
                     lhsT_scale=wds_p[:, t, :],
-                    rhs=codes[:].bitcast(FP8X4),
-                    rhs_scale=scales[:],
+                    rhs=h[0][:].bitcast(FP8X4),
+                    rhs_scale=h[1][:],
                     start=True,
                     stop=True,
                 )
             return banks
 
-        def drain(name, acc):
-            held = keep.tile(acc.shape, F32, name=name, tag=name, align_bytes=64)
+        def drain(name, tag, acc):
+            held = keep.tile([P, 2, CHUNK], F32, name=name, tag=tag, align_bytes=64)
             nc.scalar.copy(held[:], acc[:])
             return held
 
-        def gates(t, start, count, tag):
-            gate = keep.tile([P, count], F32, name="gate_%d_%d" % (t, start), tag=tag, align_bytes=64)
+        def put(t, start, count, y):
             nc.vector.tensor_tensor(
-                gate[:], g_rows[t][:].indirect(entries(start, count)), wgo_t[:, start : start + count], MULT
+                page[t][:].indirect(entries(start, count)), y, gate[t][:, start : start + count], MULT
             )
-            return gate
 
-        def put(t, start, count, y, gate):
-            nc.vector.tensor_tensor(page[t][:].indirect(entries(start, count)), y, gate, MULT)
-
-        sums = [up(0, 0), up(1, 2), up(2, 4)]
-        gate = [gates(0, 0, J, "gate0"), gates(1, 0, HALF, "gate1")]
-        wd_p = keep.tile([P, PACK, P], I32, name="wd_p", align_bytes=64)
-        nc.vector.tensor_copy(
-            wd_p[:].rearrange("p t (c i) -> p c t i", i=4), wd_w[:].rearrange("p (c i t) -> p c t i", i=4, t=PACK)
-        )
-        wds_p = keep.tile([P, PACK, P], U8, name="wds_p", align_bytes=64)
-        nc.vector.tensor_copy(wds_p[:], wd_s[:].rearrange("p (m t) -> p t m", t=PACK))
-
-        pos = planes_tile("pos", 0, F32, "pos0")
-        sq = planes_tile("sq", 0, F32, "sq0")
-        rows = planes_tile("rows", 0, BF16, "rows0")
-        rectify(sums[0], pos)
-        for pair in range(2):
-            square(pos, sq, slice(2 * pair, 2 * pair + 2))
-        for t in range(PACK):
-            smooth(sq, rows, t)
-        banks = down(0, weave(0, rows), 0, laid.tile([P, CHUNK], I32, name="h_codes0", align_bytes=64, offset=0), "both0")
-        y_low = drain("y0_0", banks[0])
-        y_high = keep.tile([P, 2, J], F32, name="y_high", align_bytes=64)
-        nc.scalar.copy(y_high[:, :, 0:CHUNK], banks[1][:])
-        gate1_late = gates(1, HALF, HALF, "woven0")
-        gate.append(gates(2, 0, CHUNK, "gate2"))
-        page.append(clear_page(keep.tile([P, T], F32, name="page2", tag="both0", align_bytes=64), nc.gpsimd))
-        for t in range(2):
-            put(t, 0, CHUNK, y_low[:, t, :], gate[t][:, 0:CHUNK])
-        put(2, 0, CHUNK, y_high[:, 0, 0:CHUNK], gate[2][:])
-
-        pos = planes_tile("pos", 1, F32, "rows0")
-        sq = laid.tile([P, PACK, CHUNK], F32, name="sq1", align_bytes=64, offset=0)
-        rows = planes_tile("rows", 1, BF16, "rows1")
-        rectify(sums[1], pos)
-        for pair in range(2):
-            square(pos, sq, slice(2 * pair, 2 * pair + 2))
-        for t in range(PACK):
-            smooth(sq, rows, t)
-        banks = down(1, weave(1, rows), 2, keep.tile([P, CHUNK], I32, name="h_codes1", tag="gate2", align_bytes=64), "y0_0")
-        gate2_late = gates(2, CHUNK, J - CHUNK, "woven1")
-        pos = laid.tile([P, PACK, HALF], F32, name="pos2", align_bytes=64, offset=0)
-        sq = planes_tile("sq", 2, F32, "sq2")
-        rows = planes_tile("rows", 2, BF16, "rows2")
-        rectify(sums[2], pos)
-        y_low = drain("y1_0", banks[0])
-        nc.scalar.copy(y_high[:, :, CHUNK:HALF], banks[1][:])
-        for t in range(2):
-            put(t, CHUNK, CHUNK, y_low[:, t, :], gate[t][:, CHUNK:HALF])
-        put(2, CHUNK, CHUNK, y_high[:, 0, CHUNK:HALF], gate2_late[:, 0:CHUNK])
-
-        page.append(clear_page(keep.tile([P, T], F32, name="page3", tag="gate2", align_bytes=64), nc.gpsimd))
-        put(3, 0, CHUNK, y_high[:, 1, 0:CHUNK], gates(3, 0, CHUNK, "y1_0")[:])
-
-        for pair in range(2):
-            square(pos, sq, slice(2 * pair, 2 * pair + 2))
-        for t in range(PACK):
-            smooth(sq, rows, t)
-        banks = down(2, weave(2, rows), 4, keep.tile([P, HALF], I32, name="h_codes2", align_bytes=64), "h_scales2")
-        gate3_late = gates(3, CHUNK, J - CHUNK, "woven2")
-        y_late = [drain("y2_%d" % t, banks[t])[:, 0, :] for t in range(2)]
-        for t in range(2):
-            nc.scalar.copy(y_high[:, t, HALF:J], banks[2 + t][:, 0, :])
-        put(0, HALF, HALF, y_late[0], gate[0][:, HALF:J])
-        put(1, HALF, HALF, y_late[1], gate1_late[:])
-        put(2, HALF, HALF, y_high[:, 0, HALF:J], gate2_late[:, CHUNK:])
-        put(3, CHUNK, J - CHUNK, y_high[:, 1, CHUNK:J], gate3_late[:])
+        codes = laid.tile([P, CHUNK], I32, name="h_codes0", align_bytes=64, offset=at_wd_w - 2 * CHUNK)
+        scales = laid.tile([P, CHUNK], U8, name="h_scales0", align_bytes=64, offset=at_wd_s)
+        h = quantise(weave(smooth(0, squares(0)), woven_tile(0, "woven0")), codes, scales)
+        gate.append(gates(3, "woven0"))
+        for k in (1, 2):
+            done = CHUNK * (k - 1)
+            sq = squares(k)
+            banks = down(h, "turn%d_" % (k % 2))
+            if k == 1:
+                page.append(
+                    clear_page(laid.tile([P, T], F32, name="page3", align_bytes=64, offset=at_wd_s), nc.gpsimd)
+                )
+            rows = smooth(k, sq)
+            y = drain("y%da" % k, "sq%d" % k, banks[0])
+            if k == 1:
+                woven = laid.tile([P, CHUNK, PACK], BF16, name="woven1", align_bytes=64, offset=at_wd_w - 2 * CHUNK)
+            else:
+                woven = woven_tile(k, "h_codes1")
+            weave(rows, woven)
+            for t in range(2):
+                put(t, done, CHUNK, y[:, t, :])
+            h = quantise(woven, *h_tiles(k))
+            y = drain("y%db" % k, "rows%d" % k, banks[1])
+            for t in range(2):
+                put(2 + t, done, CHUNK, y[:, t, :])
+        sq = squares(3)
+        banks = down(h, "turn1_")
+        h = quantise(weave(smooth(3, sq), woven_tile(3, "woven3")), *h_tiles(3))
+        y = keep.tile([P, PACK, HALF], F32, name="y_late", tag="rows3", align_bytes=64)
+        for b in range(2):
+            nc.scalar.copy(y[:, 2 * b : 2 * b + 2, 0:CHUNK], banks[b][:])
+        for t in (1, 2):
+            put(t, HALF, CHUNK, y[:, t, 0:CHUNK])
+        banks = down(h, "up")
+        for b in range(2):
+            nc.scalar.copy(y[:, 2 * b : 2 * b + 2, CHUNK:HALF], banks[b][:])
+        put(0, HALF, HALF, y[:, 0, :])
+        for t in (1, 2):
+            put(t, J - CHUNK, CHUNK, y[:, t, CHUNK:HALF])
+        put(3, HALF, HALF, y[:, 3, :])
 
         out_rows = out_0.rearrange("(p t) c -> t p c", t=PACK)
         for t in range(PACK):

@@ -43,11 +43,11 @@ def tile_list_modp_relu2_gateP_kernel(
         at_wd_w = T + 8 * T
         at_g = [None, T, T + 4 * T, at_wd_w + 4 * N]
         at_both = at_g[3] + 4 * T
-        at_wd_s = at_both + 4 * T
+        at_wd_s = at_both
+        at_woven = at_both + 4 * T
         tab_s = laid.tile([P, at_both], U8, name="tab_s", align_bytes=64, offset=0)[:, 0:T]
         tab_w = keep.tile([P, T], I32, name="tab_w", align_bytes=64)[:]
         w_s = keep.tile([P, 2, R], U8, name="w_s", align_bytes=64)
-        wd_s = laid.tile([P, N], U8, name="wd_s", align_bytes=64, offset=at_wd_s)
         wu_w = keep.tile([P, 2, R], I32, name="wu_w", align_bytes=64)
         pick_s1 = keep.tile([P, J], U8, name="pick_s1", align_bytes=64)
         ident = keep.tile([P, P], F32, name="ident", align_bytes=64)
@@ -59,14 +59,11 @@ def tile_list_modp_relu2_gateP_kernel(
         nc.vector.memset(w_s[:].rearrange("p a r -> p (a r)").bitcast(I32), 0)
         nc.vector.memset(pick_s1[:].bitcast(I32), 0)
         page = [clear_page(keep.tile([P, T], F32, name="page0", align_bytes=64), nc.vector)]
-        nc.gpsimd.memset(wd_s[:].bitcast(I32), 0)
-        make_identity(nc, ident[:])
+        wgo_c = keep.tile([P, 2 * PACK], F32, name="wgo_c", align_bytes=64)
+        nc.gpsimd.dma_start(wgo_c[:], wgo[0].rearrange("(p i) -> p i", p=P))
         sm_t = keep.tile([P, PACK], F32, name="sm_t", align_bytes=64)
         nc.gpsimd.dma_start(sm_t[:], sm.rearrange("(p t) -> p t", t=PACK))
-        for q in range(QUADS):
-            nc.gpsimd.dma_start(
-                wd_s[32 * q : 32 * q + 4, :].bitcast(I32), wd_scales[0, 4 * q : 4 * q + 4, :].bitcast(I32)
-            )
+        make_identity(nc, ident[:])
 
         nc.sync.dma_start(offsets[:], offs)
         s_rows = tab_scales.rearrange("a q c -> (a q) c").bitcast(I32)
@@ -87,7 +84,14 @@ def tile_list_modp_relu2_gateP_kernel(
             )
         nc.sync.dma_start(wu_w[:], wu_words.rearrange("a p r b -> p a (r b)").bitcast(I32))
         wgo_t = keep.tile([P, J], F32, name="wgo_t", align_bytes=64)
-        nc.sync.dma_start(wgo_t[:], wgo)
+        for b in range(2):
+            spread = psum.tile([P, PACK, P], F32, name="spread%d" % b)
+            for i in range(PACK):
+                column = wgo_c[:, PACK * b + i : PACK * b + i + 1]
+                nc.tensor.transpose(spread[:, i, :], column.to_broadcast([P, P]), ident[:])
+            nc.scalar.copy(
+                wgo_t[:].rearrange("c (p b i) -> c b p i", b=2, i=PACK)[:, b], spread[:].rearrange("c i p -> c p i")
+            )
 
         def pick_scales(start, count):
             picked = keep.tile([P, count], U8, name="pick_s0_%d" % start, align_bytes=64)
@@ -122,16 +126,20 @@ def tile_list_modp_relu2_gateP_kernel(
             pick_words(0, keep.tile([P, CHUNK], I32, name="both0", align_bytes=64)),
             pick_words(CHUNK, laid.tile([P, J - CHUNK], I32, name="both1", align_bytes=64, offset=at_both)),
         ]
-        page.append(clear_page(laid.tile([P, T], F32, name="page1", align_bytes=64, offset=at_both), nc.gpsimd))
+        wd_s = laid.tile([P, N], U8, name="wd_s", align_bytes=64, offset=at_wd_s)
+        nc.gpsimd.memset(wd_s[:].bitcast(I32), 0)
+        for q in range(QUADS):
+            nc.gpsimd.dma_start(
+                wd_s[32 * q : 32 * q + 4, :].bitcast(I32), wd_scales[0, 4 * q : 4 * q + 4, :].bitcast(I32)
+            )
 
-        def gates(t, tag):
-            gate = keep.tile([P, J], F32, name="gate%d" % t, tag=tag, align_bytes=64)
+        def gates(t, gate):
             nc.vector.tensor_tensor(gate[:], g_rows[t][:].indirect(offsets[:]), wgo_t[:], MULT)
             return gate
 
-        gate = [gates(0, "gate0")]
-        page.append(clear_page(keep.tile([P, T], F32, name="page2", tag="g_rows0", align_bytes=64), nc.gpsimd))
-        gate.extend(gates(t, "gate%d" % t) for t in (1, 2))
+        gate = [gates(0, keep.tile([P, J], F32, name="gate0", align_bytes=64))]
+        page.append(clear_page(keep.tile([P, T], F32, name="page1", tag="g_rows0", align_bytes=64), nc.gpsimd))
+        gate.extend(gates(t, keep.tile([P, J], F32, name="gate%d" % t, align_bytes=64)) for t in (1, 2))
         wds_p = laid.tile([P, PACK, P], U8, name="wds_p", align_bytes=64, offset=at_g[2])
         nc.vector.tensor_copy(wds_p[:], wd_s[:].rearrange("p (m t) -> p t m", t=PACK))
         wd_p = keep.tile([P, PACK, P], I32, name="wd_p", align_bytes=64)
@@ -221,16 +229,16 @@ def tile_list_modp_relu2_gateP_kernel(
 
         codes = laid.tile([P, CHUNK], I32, name="h_codes0", align_bytes=64, offset=at_wd_w - 2 * CHUNK)
         scales = laid.tile([P, CHUNK], U8, name="h_scales0", align_bytes=64, offset=at_wd_s)
-        h = quantise(weave(smooth(0, squares(0)), woven_tile(0, "woven0")), codes, scales)
-        gate.append(gates(3, "woven0"))
+        woven = laid.tile([P, (J + 2 * T) // 2, PACK], BF16, name="woven0", align_bytes=64, offset=at_woven)[:, 0:CHUNK, :]
+        h = quantise(weave(smooth(0, squares(0)), woven), codes, scales)
+        gate.append(gates(3, laid.tile([P, J], F32, name="gate3", align_bytes=64, offset=at_woven)))
+        for t in (2, 3):
+            at_page = at_woven + 4 * J + 4 * T * (t - 2)
+            page.append(clear_page(laid.tile([P, T], F32, name="page%d" % t, align_bytes=64, offset=at_page), nc.gpsimd))
         for k in (1, 2):
             done = CHUNK * (k - 1)
             sq = squares(k)
             banks = down(h, "turn%d_" % (k % 2))
-            if k == 1:
-                page.append(
-                    clear_page(laid.tile([P, T], F32, name="page3", align_bytes=64, offset=at_wd_s), nc.gpsimd)
-                )
             rows = smooth(k, sq)
             y = drain("y%da" % k, "sq%d" % k, banks[0])
             if k == 1:
@@ -296,17 +304,18 @@ def tile_list_modp_relu2_gateP_kernel(
         for k in (3, 4, 2, 5):
             c, n = chunks[k]
             weave_out(nc.scalar.copy, k, rows_s, split, max(c, split), c + n)
+        def store_scales(lo, hi):
+            for q in range(QUADS):
+                (nc.scalar if q % 2 else nc.sync).dma_start(
+                    out_2[0, 4 * q : 4 * q + 4, lo:hi].bitcast(I32), o_scales[32 * q : 32 * q + 4, lo:hi].bitcast(I32)
+                )
+
         nc.vector.tensor_copy(rows_v[:, 3, 0:HALF], page[3][:, 0:HALF])
-        weave_out(nc.vector.tensor_copy, 0, rows_v, 0, 0, HALF)
         nc.vector.tensor_copy(rows_v[:, 3, HALF:split], page[3][:, HALF:split])
+        weave_out(nc.vector.tensor_copy, 0, rows_v, 0, 0, HALF)
+        weave_out(nc.vector.tensor_copy, 2, rows_v, 0, 2 * HALF, split)
         planes(0)
         weave_out(nc.vector.tensor_copy, 1, rows_v, 0, HALF, 2 * HALF)
-        planes(3)
-        planes(1)
-        weave_out(nc.vector.tensor_copy, 2, rows_v, 0, 2 * HALF, split)
-        for k in (4, 2, 5):
+        for k in (3, 1, 4, 2, 5):
             planes(k)
-        for q in range(QUADS):
-            (nc.scalar if q % 2 else nc.sync).dma_start(
-                out_2[0, 4 * q : 4 * q + 4, :].bitcast(I32), o_scales[32 * q : 32 * q + 4, :].bitcast(I32)
-            )
+        store_scales(0, T)

@@ -57,7 +57,6 @@ def tile_list_modp_relu2_gateP_kernel(
             return cleared
 
         nc.vector.memset(w_s[:].rearrange("p a r -> p (a r)").bitcast(I32), 0)
-        nc.vector.memset(pick_s1[:].bitcast(I32), 0)
         page = [clear_page(keep.tile([P, T], F32, name="page0", align_bytes=64), nc.vector)]
         wgo_c = keep.tile([P, 2 * PACK], F32, name="wgo_c", align_bytes=64)
         nc.gpsimd.dma_start(wgo_c[:], wgo[0].rearrange("(p i) -> p i", p=P))
@@ -68,12 +67,12 @@ def tile_list_modp_relu2_gateP_kernel(
         nc.sync.dma_start(offsets[:], offs)
         s_rows = tab_scales.rearrange("a q c -> (a q) c").bitcast(I32)
         for queue, first, rows, source in (
-            (nc.scalar, 56, 28, 0),
-            (nc.sync, 116, 12, 0),
+            (nc.scalar, 32, 24, 4),
             (nc.sync, 0, 32, 0),
-            (nc.sync, 84, 32, 0),
-            (nc.sync, 32, 16, 4),
-            (nc.sync, 48, 8, 20),
+            (nc.sync, 56, 32, 0),
+            (nc.sync, 88, 16, 4),
+            (nc.sync, 104, 16, 16),
+            (nc.sync, 120, 8, 0),
         ):
             queue.dma_start(tab_s[first : first + rows, :].bitcast(I32), s_rows[source : source + rows, :])
         nc.sync.dma_start(tab_w, tab_words[0].rearrange("p c b -> p (c b)").bitcast(I32))
@@ -97,7 +96,10 @@ def tile_list_modp_relu2_gateP_kernel(
             picked = keep.tile([P, count], U8, name="pick_s0_%d" % start, align_bytes=64)
             nc.vector.tensor_copy(picked[:], tab_s.indirect(entries(start, count)))
             moved = pick_s1[:, start : start + count]
-            nc.scalar.dma_start(moved[0:112, :].bitcast(I32), picked[16:P, :].bitcast(I32))
+            for first, source in ((0, 16), (64, 52)):
+                nc.scalar.dma_start(
+                    moved[first : first + 64, :].bitcast(I32), picked[source : source + 64, :].bitcast(I32)
+                )
             return [picked[:], moved]
 
         pick_s = [pick_scales(0, CHUNK), pick_scales(CHUNK, J - CHUNK)]
@@ -150,10 +152,9 @@ def tile_list_modp_relu2_gateP_kernel(
         def bank(tag, shape):
             return psum.tile(shape, F32, name=tag, tag=tag)
 
-        def squares(k):
-            sq = keep.tile([P, PACK, CHUNK], F32, name="sq%d" % k, tag="sq%d" % k, align_bytes=64)
+        def turn(k):
             part, first = (0, 0) if k == 0 else (1, CHUNK * (k - 1))
-            turned = []
+            turned = [bank("turn%d_%d" % (k % 2, b), [P, 2, CHUNK]) for b in range(2)]
             for b in range(2):
                 lo = first + P * b
                 sums = bank("up%d" % b, [P, R])
@@ -169,17 +170,16 @@ def tile_list_modp_relu2_gateP_kernel(
                     )
                 pos = keep.tile([P, PACK, P], F32, name="pos%d" % b, tag="pos%d" % b, align_bytes=64)
                 nc.scalar.activation(pos[:], sums[:].rearrange("p (m t) -> p t m", t=PACK), ACT.Relu)
-                turned.append(bank("turn%d_%d" % (k % 2, b), [P, PACK, P]))
+                sq = keep.tile([P, PACK, P], F32, name="sq%d" % b, tag="sq%d" % b, align_bytes=64)
+                nc.scalar.activation(sq[:], pos[:], ACT.Square)
                 for t in range(PACK):
-                    nc.tensor.transpose(turned[b][:, t, :], pos[:, t, :], ident[:])
-            for b in range(2):
-                nc.scalar.activation(sq[:, :, P * b : P * (b + 1)], turned[b][:], ACT.Square)
-            return sq
+                    nc.tensor.transpose(turned[t // 2][:, t % 2, P * b : P * (b + 1)], sq[:, t, :], ident[:])
+            return turned
 
-        def smooth(k, sq):
+        def smooth(k, turned):
             rows = keep.tile([P, PACK, CHUNK], BF16, name="rows%d" % k, tag="rows%d" % k, align_bytes=64)
             for t in range(PACK):
-                nc.scalar.activation(rows[:, t, :], sq[:, t, :], ACT.Copy, scale=sm_t[:, t : t + 1])
+                nc.scalar.activation(rows[:, t, :], turned[t // 2][:, t % 2, :], ACT.Copy, scale=sm_t[:, t : t + 1])
             return rows
 
         def weave(rows, woven):
@@ -227,95 +227,114 @@ def tile_list_modp_relu2_gateP_kernel(
                 page[t][:].indirect(entries(start, count)), y, gate[t][:, start : start + count], MULT
             )
 
+        turned = [turn(0), turn(1)]
         codes = laid.tile([P, CHUNK], I32, name="h_codes0", align_bytes=64, offset=at_wd_w - 2 * CHUNK)
         scales = laid.tile([P, CHUNK], U8, name="h_scales0", align_bytes=64, offset=at_wd_s)
         woven = laid.tile([P, (J + 2 * T) // 2, PACK], BF16, name="woven0", align_bytes=64, offset=at_woven)[:, 0:CHUNK, :]
-        h = quantise(weave(smooth(0, squares(0)), woven), codes, scales)
+        h = quantise(weave(smooth(0, turned[0]), woven), codes, scales)
         gate.append(gates(3, laid.tile([P, J], F32, name="gate3", align_bytes=64, offset=at_woven)))
         for t in (2, 3):
             at_page = at_woven + 4 * J + 4 * T * (t - 2)
             page.append(clear_page(laid.tile([P, T], F32, name="page%d" % t, align_bytes=64, offset=at_page), nc.gpsimd))
-        for k in (1, 2):
-            done = CHUNK * (k - 1)
-            sq = squares(k)
-            banks = down(h, "turn%d_" % (k % 2))
-            rows = smooth(k, sq)
-            y = drain("y%da" % k, "sq%d" % k, banks[0])
-            if k == 1:
-                woven = laid.tile([P, CHUNK, PACK], BF16, name="woven1", align_bytes=64, offset=at_wd_w - 2 * CHUNK)
-            else:
-                woven = woven_tile(k, "h_codes1")
-            weave(rows, woven)
-            for t in range(2):
-                put(t, done, CHUNK, y[:, t, :])
-            h = quantise(woven, *h_tiles(k))
-            y = drain("y%db" % k, "rows%d" % k, banks[1])
-            for t in range(2):
-                put(2 + t, done, CHUNK, y[:, t, :])
-        sq = squares(3)
+        def y_tile(name, tag, planes, count):
+            return keep.tile([P, planes, count], F32, name=name, tag=tag, align_bytes=64)
+
+        rows = smooth(1, turned[1])
         banks = down(h, "turn1_")
-        h = quantise(weave(smooth(3, sq), woven_tile(3, "woven3")), *h_tiles(3))
-        y = keep.tile([P, PACK, HALF], F32, name="y_late", tag="rows3", align_bytes=64)
-        for b in range(2):
-            nc.scalar.copy(y[:, 2 * b : 2 * b + 2, 0:CHUNK], banks[b][:])
-        for t in (1, 2):
-            put(t, HALF, CHUNK, y[:, t, 0:CHUNK])
+        y = drain("y0a", "y0a", banks[0])
+        turned.append(turn(2))
+        woven = laid.tile([P, CHUNK, PACK], BF16, name="woven1", align_bytes=64, offset=at_wd_w - 2 * CHUNK)
+        weave(rows, woven)
+        for t in range(2):
+            put(t, 0, CHUNK, y[:, t, :])
+        h = quantise(woven, *h_tiles(1))
+        y = drain("y0b", "rows1", banks[1])
+        for t in range(2):
+            put(2 + t, 0, CHUNK, y[:, t, :])
+
+        rows = smooth(2, turned[2])
+        banks = down(h, "turn0_")
+        y = drain("y1a", "y1a", banks[0])
+        turned.append(turn(3))
+        woven = weave(rows, woven_tile(2, "h_codes1"))
+        for t in range(2):
+            put(t, CHUNK, CHUNK, y[:, t, :])
+        h = quantise(woven, *h_tiles(2))
+        y_high = y_tile("y_high", "rows2", 2, J - CHUNK)
+        nc.scalar.copy(y_high[:, :, 0:CHUNK], banks[1][:])
+        put(2, CHUNK, CHUNK, y_high[:, 0, 0:CHUNK])
+
+        rows = smooth(3, turned[3])
+        banks = down(h, "turn1_")
+        y = y_tile("y2_0", "y2_0", 1, CHUNK)
+        nc.scalar.copy(y[:, 0, :], banks[0][:, 0, :])
+        woven = weave(rows, woven_tile(3, "h_codes2"))
+        put(0, HALF, CHUNK, y[:, 0, :])
+        h = quantise(woven, *h_tiles(3))
+        y = y_tile("y2_1", "rows3", 1, CHUNK)
+        nc.scalar.copy(y[:, 0, :], banks[0][:, 1, :])
+        nc.scalar.copy(y_high[:, :, CHUNK:HALF], banks[1][:])
+        put(1, HALF, CHUNK, y[:, 0, :])
+
         banks = down(h, "up")
-        for b in range(2):
-            nc.scalar.copy(y[:, 2 * b : 2 * b + 2, CHUNK:HALF], banks[b][:])
-        put(0, HALF, HALF, y[:, 0, :])
-        for t in (1, 2):
-            put(t, J - CHUNK, CHUNK, y[:, t, CHUNK:HALF])
-        put(3, HALF, HALF, y[:, 3, :])
+        y = y_tile("y3a", "y3a", 2, CHUNK)
+        for t in range(2):
+            nc.scalar.copy(y[:, t, :], banks[0][:, t, :])
+        nc.scalar.copy(y_high[:, :, HALF : J - CHUNK], banks[1][:])
+        for t in range(2):
+            put(t, J - CHUNK, CHUNK, y[:, t, :])
+        put(2, HALF, HALF, y_high[:, 0, CHUNK : J - CHUNK])
+        put(3, CHUNK, J - CHUNK, y_high[:, 1, :])
 
         out_rows = out_0.rearrange("(p t) c -> t p c", t=PACK)
         for t in range(PACK):
             nc.sync.dma_start(out_rows[t], page[t][:])
 
         o_scales = keep.tile([P, T], U8, name="o_scales", align_bytes=64)
+        o_codes = keep.tile([P, T], I32, name="o_codes", align_bytes=64)
         words_out = out_1[0].rearrange("p c b -> p (c b)").bitcast(I32)
         split = T // 2 + P
+        spans = [(0, split), (split, HALF - P), (T - HALF, HALF)]
         chunks = [(c, HALF) for c in range(0, T // 2, HALF)] + [(c, CHUNK) for c in range(T // 2, T, CHUNK)]
-        rows_v = keep.tile([P, PACK, split], BF16, name="rows_v", align_bytes=64)
-        rows_s = keep.tile([P, PACK, T - split], BF16, name="rows_s", align_bytes=64)
+        woven_o = [keep.tile([P, n, 2], U32, name="woven_o%d" % c, align_bytes=64) for c, n in chunks]
+        pairs = [keep.tile([P, 2, n, 2], BF16, name="pairs%d" % c, align_bytes=64) for c, n in spans]
         for t in range(3):
-            nc.scalar.copy(rows_v[:, t, :], page[t][:, 0:split])
-            nc.scalar.copy(rows_s[:, t, :], page[t][:, split:T])
-        woven_o = [keep.tile([P, n, PACK], BF16, name="woven_o%d" % c, align_bytes=64) for c, n in chunks]
-        o_codes = keep.tile([P, T], I32, name="o_codes", align_bytes=64)
+            for (c, n), pair in zip(spans, pairs):
+                if t == 2 and c < split:
+                    both_halves = page[t][:, c : c + n].unsqueeze(2).to_broadcast([P, n, 2])
+                    nc.scalar.copy(pair[:, 1, :, :], both_halves)
+                else:
+                    nc.scalar.copy(pair[:, t // 2, :, t % 2], page[t][:, c : c + n])
 
-        def weave_out(engine_copy, k, rows, first, lo, hi):
-            c = chunks[k][0]
-            engine_copy(
-                woven_o[k][:, lo - c : hi - c, :].rearrange("p (c i) t -> p c t i", i=4),
-                rows[:, :, lo - first : hi - first].rearrange("p t (c i) -> p c t i", i=4),
-            )
+        def weave_out(engine_copy, s, k):
+            (first, count), (c, n) = spans[s], chunks[k]
+            lo, hi = max(first, c), min(first + count, c + n)
+            words = pairs[s][:].rearrange("p u c e -> p (u c e)").bitcast(U32).rearrange("p (u c) -> p c u", u=2)
+            engine_copy(woven_o[k][:, lo - c : hi - c, :], words[:, lo - first : hi - first, :])
 
         def planes(k):
             c, n = chunks[k]
             nc.vector.quantize_mx(
                 out=o_codes[:, c : c + n].bitcast(FP8X4),
                 scales=o_scales[:, c : c + n],
-                in_=woven_o[k][:].rearrange("p c t -> p (c t)"),
+                in_=woven_o[k][:].rearrange("p c u -> p (c u)").bitcast(BF16),
             )
-            nc.sync.dma_start(words_out[:, c : c + n], o_codes[:, c : c + n])
+            if (c + n) % HALF == 0:
+                nc.sync.dma_start(words_out[:, c + n - HALF : c + n], o_codes[:, c + n - HALF : c + n])
 
-        nc.scalar.copy(rows_s[:, 3, :], page[3][:, split:T])
-        for k in (3, 4, 2, 5):
-            c, n = chunks[k]
-            weave_out(nc.scalar.copy, k, rows_s, split, max(c, split), c + n)
-        def store_scales(lo, hi):
-            for q in range(QUADS):
-                (nc.scalar if q % 2 else nc.sync).dma_start(
-                    out_2[0, 4 * q : 4 * q + 4, lo:hi].bitcast(I32), o_scales[32 * q : 32 * q + 4, lo:hi].bitcast(I32)
-                )
-
-        nc.vector.tensor_copy(rows_v[:, 3, 0:HALF], page[3][:, 0:HALF])
-        nc.vector.tensor_copy(rows_v[:, 3, HALF:split], page[3][:, HALF:split])
-        weave_out(nc.vector.tensor_copy, 0, rows_v, 0, 0, HALF)
-        weave_out(nc.vector.tensor_copy, 2, rows_v, 0, 2 * HALF, split)
+        for s, ks in ((1, (2, 3)), (2, (4, 5))):
+            c, n = spans[s]
+            nc.scalar.copy(pairs[s][:, 1, :, 1], page[3][:, c : c + n])
+            for k in ks:
+                weave_out(nc.scalar.copy, s, k)
+        nc.vector.tensor_copy(pairs[0][:, 1, :, 1], page[3][:, 0:split])
+        weave_out(nc.vector.tensor_copy, 0, 0)
+        weave_out(nc.vector.tensor_copy, 0, 1)
         planes(0)
-        weave_out(nc.vector.tensor_copy, 1, rows_v, 0, HALF, 2 * HALF)
-        for k in (3, 1, 4, 2, 5):
+        weave_out(nc.vector.tensor_copy, 0, 2)
+        for k in range(1, len(chunks)):
             planes(k)
-        store_scales(0, T)
+        for q in range(QUADS):
+            (nc.scalar if q % 2 else nc.sync).dma_start(
+                out_2[0, 4 * q : 4 * q + 4, :].bitcast(I32), o_scales[32 * q : 32 * q + 4, :].bitcast(I32)
+            )

@@ -45,7 +45,7 @@ def tile_list_modp_relu2_gateP_kernel(
         at_both = at_g[3] + 4 * T
         at_wd_s = at_both
         at_woven = at_both + 4 * T
-        tab_s = laid.tile([P, at_both], U8, name="tab_s", align_bytes=64, offset=0)[:, 0:T]
+        tab_s = keep.tile([P, T], U8, name="tab_s", align_bytes=64)[:]
         tab_w = keep.tile([P, T], I32, name="tab_w", align_bytes=64)[:]
         w_s = keep.tile([P, 2, R], U8, name="w_s", align_bytes=64)
         wu_w = keep.tile([P, 2, R], I32, name="wu_w", align_bytes=64)
@@ -56,13 +56,14 @@ def tile_list_modp_relu2_gateP_kernel(
             engine.memset(cleared[:].bitcast(I32), 0)
             return cleared
 
-        nc.vector.memset(w_s[:].rearrange("p a r -> p (a r)").bitcast(I32), 0)
         page = [clear_page(keep.tile([P, T], F32, name="page0", align_bytes=64), nc.vector)]
-        wgo_c = keep.tile([P, 2 * PACK], F32, name="wgo_c", align_bytes=64)
-        nc.gpsimd.dma_start(wgo_c[:], wgo[0].rearrange("(p i) -> p i", p=P))
-        sm_t = keep.tile([P, PACK], F32, name="sm_t", align_bytes=64)
-        nc.gpsimd.dma_start(sm_t[:], sm.rearrange("(p t) -> p t", t=PACK))
         make_identity(nc, ident[:])
+        nc.gpsimd.memset(w_s[:].rearrange("p a r -> p (a r)").bitcast(I32), 0)
+        for q in range(QUADS):
+            nc.gpsimd.dma_start(
+                w_s[32 * q : 32 * q + 4, :, :].bitcast(I32),
+                wu_scales[:, 4 * q : 4 * q + 4, :].rearrange("a s r -> s a r").bitcast(I32),
+            )
 
         nc.sync.dma_start(offsets[:], offs)
         s_rows = tab_scales.rearrange("a q c -> (a q) c").bitcast(I32)
@@ -76,12 +77,17 @@ def tile_list_modp_relu2_gateP_kernel(
         ):
             queue.dma_start(tab_s[first : first + rows, :].bitcast(I32), s_rows[source : source + rows, :])
         nc.sync.dma_start(tab_w, tab_words[0].rearrange("p c b -> p (c b)").bitcast(I32))
-        for q in range(QUADS):
-            nc.sync.dma_start(
-                w_s[32 * q : 32 * q + 4, :, :].bitcast(I32),
-                wu_scales[:, 4 * q : 4 * q + 4, :].rearrange("a s r -> s a r").bitcast(I32),
-            )
+        wgo_c = keep.tile([P, 2 * PACK], F32, name="wgo_c", align_bytes=64)
+        nc.sync.dma_start(wgo_c[:], wgo[0].rearrange("(p i) -> p i", p=P))
         nc.sync.dma_start(wu_w[:], wu_words.rearrange("a p r b -> p a (r b)").bitcast(I32))
+
+        def load_gates(t, rows):
+            nc.sync.dma_start(rows[:], g_src[t])
+            return rows
+
+        g_rows = [load_gates(0, keep.tile([P, T], F32, name="g_rows0", tag="g_rows0", align_bytes=64))]
+        sm_t = keep.tile([P, PACK], F32, name="sm_t", align_bytes=64)
+        nc.sync.dma_start(sm_t[:], sm.rearrange("(p t) -> p t", t=PACK))
         wgo_t = keep.tile([P, J], F32, name="wgo_t", align_bytes=64)
         for b in range(2):
             spread = psum.tile([P, PACK, P], F32, name="spread%d" % b)
@@ -104,17 +110,6 @@ def tile_list_modp_relu2_gateP_kernel(
 
         pick_s = [pick_scales(0, CHUNK), pick_scales(CHUNK, J - CHUNK)]
 
-        def load_gates(t, rows):
-            nc.sync.dma_start(rows[:], g_src[t])
-            return rows
-
-        g_rows = [load_gates(0, keep.tile([P, T], F32, name="g_rows0", tag="g_rows0", align_bytes=64))]
-        g_rows.append(load_gates(1, laid.tile([P, T], F32, name="g_rows1", align_bytes=64, offset=at_g[1])))
-        g_rows.append(load_gates(2, laid.tile([P, T], F32, name="g_rows2", align_bytes=64, offset=at_g[2])))
-        wd_w = laid.tile([P, N], I32, name="wd_w", align_bytes=64, offset=at_wd_w)
-        nc.sync.dma_start(wd_w[:], wd_words[0].rearrange("p n b -> p (n b)").bitcast(I32))
-        g_rows.append(load_gates(3, laid.tile([P, T], F32, name="g_rows3", align_bytes=64, offset=at_g[3])))
-
         def pick_words(start, both):
             count = both.shape[1]
             nc.vector.tensor_copy(both[:].bitcast(U32), tab_w.bitcast(U32).indirect(entries(start, count)))
@@ -125,9 +120,14 @@ def tile_list_modp_relu2_gateP_kernel(
             return parted
 
         parted = [
-            pick_words(0, keep.tile([P, CHUNK], I32, name="both0", align_bytes=64)),
+            pick_words(0, laid.tile([P, at_both // 4], I32, name="both0", align_bytes=64, offset=0)[:, 0:CHUNK]),
             pick_words(CHUNK, laid.tile([P, J - CHUNK], I32, name="both1", align_bytes=64, offset=at_both)),
         ]
+        g_rows.append(load_gates(1, laid.tile([P, T], F32, name="g_rows1", align_bytes=64, offset=at_g[1])))
+        g_rows.append(load_gates(2, laid.tile([P, T], F32, name="g_rows2", align_bytes=64, offset=at_g[2])))
+        wd_w = laid.tile([P, N], I32, name="wd_w", align_bytes=64, offset=at_wd_w)
+        nc.sync.dma_start(wd_w[:], wd_words[0].rearrange("p n b -> p (n b)").bitcast(I32))
+        g_rows.append(load_gates(3, laid.tile([P, T], F32, name="g_rows3", align_bytes=64, offset=at_g[3])))
         wd_s = laid.tile([P, N], U8, name="wd_s", align_bytes=64, offset=at_wd_s)
         nc.gpsimd.memset(wd_s[:].bitcast(I32), 0)
         for q in range(QUADS):

@@ -77,9 +77,9 @@ def tile_list_modp_relu2_gateP_kernel(
         ):
             queue.dma_start(tab_s[first : first + rows, :].bitcast(I32), s_rows[source : source + rows, :])
         nc.sync.dma_start(tab_w, tab_words[0].rearrange("p c b -> p (c b)").bitcast(I32))
+        nc.sync.dma_start(wu_w[:], wu_words.rearrange("a p r b -> p a (r b)").bitcast(I32))
         wgo_c = keep.tile([P, 2 * PACK], F32, name="wgo_c", align_bytes=64)
         nc.sync.dma_start(wgo_c[:], wgo[0].rearrange("(p i) -> p i", p=P))
-        nc.sync.dma_start(wu_w[:], wu_words.rearrange("a p r b -> p a (r b)").bitcast(I32))
 
         def load_gates(t, rows):
             nc.sync.dma_start(rows[:], g_src[t])

@@ -56,7 +56,9 @@ def tile_list_modp_relu2_gateP_kernel(
             engine.memset(cleared[:].bitcast(I32), 0)
             return cleared
 
-        page = [clear_page(keep.tile([P, T], F32, name="page0", align_bytes=64), nc.vector)]
+        page = [keep.tile([P, T], F32, name="page0", align_bytes=64)]
+        for first, last in ((0, T // 2 - 1), (T // 2 - 1, T)):
+            nc.vector.memset(page[0][:, first:last].bitcast(I32), 0)
         make_identity(nc, ident[:])
         nc.gpsimd.memset(w_s[:].rearrange("p a r -> p (a r)").bitcast(I32), 0)
         for q in range(QUADS):
@@ -90,7 +92,7 @@ def tile_list_modp_relu2_gateP_kernel(
         nc.sync.dma_start(sm_t[:], sm.rearrange("(p t) -> p t", t=PACK))
         wgo_t = keep.tile([P, J], F32, name="wgo_t", align_bytes=64)
         for b in range(2):
-            spread = psum.tile([P, PACK, P], F32, name="spread%d" % b)
+            spread = psum.tile([P, PACK, P], F32, name="spread%d" % b, tag="spread%d" % b)
             for i in range(PACK):
                 column = wgo_c[:, PACK * b + i : PACK * b + i + 1]
                 nc.tensor.transpose(spread[:, i, :], column.to_broadcast([P, P]), ident[:])
@@ -152,29 +154,32 @@ def tile_list_modp_relu2_gateP_kernel(
         def bank(tag, shape):
             return psum.tile(shape, F32, name=tag, tag=tag)
 
-        def turn(k):
+        def turn_banks(k):
+            return [bank("turn%d_%d" % (k % 2, b), [P, 2, CHUNK]) for b in range(2)]
+
+        def rectify(k, b):
             part, first = (0, 0) if k == 0 else (1, CHUNK * (k - 1))
-            turned = [bank("turn%d_%d" % (k % 2, b), [P, 2, CHUNK]) for b in range(2)]
-            for b in range(2):
-                lo = first + P * b
-                sums = bank("up%d" % b, [P, R])
-                for a in range(2):
-                    nc.tensor.matmul_mx(
-                        out=sums[:],
-                        lhsT=parted[part][:, a, 2 * lo : 2 * (lo + P)].bitcast(FP4X4),
-                        lhsT_scale=pick_s[part][a][:, lo : lo + P],
-                        rhs=wu_w[:, a, :].bitcast(FP8X4),
-                        rhs_scale=w_s[:, a, :],
-                        start=(a == 0),
-                        stop=(a == 1),
-                    )
-                pos = keep.tile([P, PACK, P], F32, name="pos%d" % b, tag="pos%d" % b, align_bytes=64)
-                nc.scalar.activation(pos[:], sums[:].rearrange("p (m t) -> p t m", t=PACK), ACT.Relu)
-                sq = keep.tile([P, PACK, P], F32, name="sq%d" % b, tag="sq%d" % b, align_bytes=64)
-                nc.scalar.activation(sq[:], pos[:], ACT.Square)
-                for t in range(PACK):
-                    nc.tensor.transpose(turned[t // 2][:, t % 2, P * b : P * (b + 1)], sq[:, t, :], ident[:])
-            return turned
+            lo = first + P * b
+            sums = bank("up%d" % b, [P, R])
+            for a in range(2):
+                nc.tensor.matmul_mx(
+                    out=sums[:],
+                    lhsT=parted[part][:, a, 2 * lo : 2 * (lo + P)].bitcast(FP4X4),
+                    lhsT_scale=pick_s[part][a][:, lo : lo + P],
+                    rhs=wu_w[:, a, :].bitcast(FP8X4),
+                    rhs_scale=w_s[:, a, :],
+                    start=(a == 0),
+                    stop=(a == 1),
+                )
+            pos = keep.tile([P, PACK, P], F32, name="pos%d_%d" % (k, b), tag="pos%d_%d" % (k % 2, b), align_bytes=64)
+            nc.scalar.activation(pos[:], sums[:].rearrange("p (m t) -> p t m", t=PACK), ACT.Relu)
+            return pos
+
+        def turn(b, pos, turned):
+            sq = keep.tile([P, PACK, P], F32, name="sq%d" % b, tag="sq%d" % b, align_bytes=64)
+            nc.scalar.activation(sq[:], pos[:], ACT.Square)
+            for t in range(PACK):
+                nc.tensor.transpose(turned[t // 2][:, t % 2, P * b : P * (b + 1)], sq[:, t, :], ident[:])
 
         def smooth(k, turned):
             rows = keep.tile([P, PACK, CHUNK], BF16, name="rows%d" % k, tag="rows%d" % k, align_bytes=64)
@@ -227,64 +232,73 @@ def tile_list_modp_relu2_gateP_kernel(
                 page[t][:].indirect(entries(start, count)), y, gate[t][:, start : start + count], MULT
             )
 
-        turned = [turn(0), turn(1)]
+        def y_tile(name, tag, planes, count):
+            return keep.tile([P, planes, count], F32, name=name, tag=tag, align_bytes=64)
+
+        def later_page(t):
+            at_page = at_woven + 4 * J + 4 * T * (t - 2)
+            return clear_page(laid.tile([P, T], F32, name="page%d" % t, align_bytes=64, offset=at_page), nc.gpsimd)
+
+        turned = [turn_banks(k) for k in range(2)]
+        for k in range(2):
+            for b in range(2):
+                turn(b, rectify(k, b), turned[k])
         codes = laid.tile([P, CHUNK], I32, name="h_codes0", align_bytes=64, offset=at_wd_w - 2 * CHUNK)
         scales = laid.tile([P, CHUNK], U8, name="h_scales0", align_bytes=64, offset=at_wd_s)
         woven = laid.tile([P, (J + 2 * T) // 2, PACK], BF16, name="woven0", align_bytes=64, offset=at_woven)[:, 0:CHUNK, :]
         h = quantise(weave(smooth(0, turned[0]), woven), codes, scales)
         gate.append(gates(3, laid.tile([P, J], F32, name="gate3", align_bytes=64, offset=at_woven)))
-        for t in (2, 3):
-            at_page = at_woven + 4 * J + 4 * T * (t - 2)
-            page.append(clear_page(laid.tile([P, T], F32, name="page%d" % t, align_bytes=64, offset=at_page), nc.gpsimd))
-        def y_tile(name, tag, planes, count):
-            return keep.tile([P, planes, count], F32, name=name, tag=tag, align_bytes=64)
-
+        page.extend(later_page(t) for t in (2, 3))
         rows = smooth(1, turned[1])
         banks = down(h, "turn1_")
+        pos = [rectify(2, 0)]
         y = drain("y0a", "y0a", banks[0])
-        turned.append(turn(2))
-        woven = laid.tile([P, CHUNK, PACK], BF16, name="woven1", align_bytes=64, offset=at_wd_w - 2 * CHUNK)
-        weave(rows, woven)
         for t in range(2):
             put(t, 0, CHUNK, y[:, t, :])
-        h = quantise(woven, *h_tiles(1))
-        y = drain("y0b", "rows1", banks[1])
-        for t in range(2):
-            put(2 + t, 0, CHUNK, y[:, t, :])
+        h = quantise(weave(rows, woven_tile(1, "woven1")), *h_tiles(1))
 
-        rows = smooth(2, turned[2])
-        banks = down(h, "turn0_")
-        y = drain("y1a", "y1a", banks[0])
-        turned.append(turn(3))
-        woven = weave(rows, woven_tile(2, "h_codes1"))
+        pos.append(rectify(2, 1))
+        turned.append(turn_banks(2))
+        turn(0, pos[0], turned[2])
+        y_high = y_tile("y_high", "pos0_0", 2, J)
+        nc.scalar.copy(y_high[:, :, 0:CHUNK], banks[1][:])
+        turn(1, pos[1], turned[2])
+        for t in range(2):
+            put(2 + t, 0, CHUNK, y_high[:, t, 0:CHUNK])
+        banks = down(h, "spread")
+        y = drain("y1a", "pos0_1", banks[0])
         for t in range(2):
             put(t, CHUNK, CHUNK, y[:, t, :])
-        h = quantise(woven, *h_tiles(2))
-        y_high = y_tile("y_high", "rows2", 2, J - CHUNK)
-        nc.scalar.copy(y_high[:, :, 0:CHUNK], banks[1][:])
-        put(2, CHUNK, CHUNK, y_high[:, 0, 0:CHUNK])
+        rows = smooth(2, turned[2])
+        pos = [rectify(3, 0)]
+        h = quantise(weave(rows, woven_tile(2, "woven2")), *h_tiles(2))
 
+        pos.append(rectify(3, 1))
+        turned.append(turn_banks(3))
+        turn(0, pos[0], turned[3])
+        turn(1, pos[1], turned[3])
+        nc.scalar.copy(y_high[:, :, CHUNK:HALF], banks[1][:])
+        for t in range(2):
+            put(2 + t, CHUNK, CHUNK, y_high[:, t, CHUNK:HALF])
         rows = smooth(3, turned[3])
         banks = down(h, "turn1_")
-        y = y_tile("y2_0", "y2_0", 1, CHUNK)
-        nc.scalar.copy(y[:, 0, :], banks[0][:, 0, :])
-        woven = weave(rows, woven_tile(3, "h_codes2"))
-        put(0, HALF, CHUNK, y[:, 0, :])
+        y_low = y_tile("y_low", "pos1_1", 2, HALF)
+        woven = weave(rows, woven_tile(3, "woven3"))
         h = quantise(woven, *h_tiles(3))
-        y = y_tile("y2_1", "rows3", 1, CHUNK)
-        nc.scalar.copy(y[:, 0, :], banks[0][:, 1, :])
-        nc.scalar.copy(y_high[:, :, CHUNK:HALF], banks[1][:])
-        put(1, HALF, CHUNK, y[:, 0, :])
+        y = y_tile("y2_0", "rows3", 1, CHUNK)
+        nc.scalar.copy(y[:, 0, :], banks[0][:, 0, :])
+        put(0, HALF, CHUNK, y[:, 0, :])
+        nc.scalar.copy(y_low[:, 1, 0:CHUNK], banks[0][:, 1, :])
+        nc.scalar.copy(y_high[:, :, HALF : J - CHUNK], banks[1][:])
 
         banks = down(h, "up")
-        y = y_tile("y3a", "y3a", 2, CHUNK)
         for t in range(2):
-            nc.scalar.copy(y[:, t, :], banks[0][:, t, :])
-        nc.scalar.copy(y_high[:, :, HALF : J - CHUNK], banks[1][:])
+            nc.scalar.copy(y_low[:, t, CHUNK:HALF], banks[0][:, t, :])
+        nc.scalar.copy(y_high[:, :, J - CHUNK : J], banks[1][:])
+        put(0, J - CHUNK, CHUNK, y_low[:, 0, CHUNK:HALF])
+        put(1, HALF, HALF, y_low[:, 1, :])
         for t in range(2):
-            put(t, J - CHUNK, CHUNK, y[:, t, :])
-        put(2, HALF, HALF, y_high[:, 0, CHUNK : J - CHUNK])
-        put(3, CHUNK, J - CHUNK, y_high[:, 1, :])
+            put(2 + t, HALF, HALF, y_high[:, t, HALF:J])
 
         out_rows = out_0.rearrange("(p t) c -> t p c", t=PACK)
         for t in range(PACK):

@@ -56,9 +56,6 @@ def tile_list_modp_relu2_gateP_kernel(
             engine.memset(cleared[:].bitcast(I32), 0)
             return cleared
 
-        page = [keep.tile([P, T], F32, name="page0", align_bytes=64)]
-        for first, last in ((0, T // 2 - 1), (T // 2 - 1, T)):
-            nc.vector.memset(page[0][:, first:last].bitcast(I32), 0)
         make_identity(nc, ident[:])
         nc.gpsimd.memset(w_s[:].rearrange("p a r -> p (a r)").bitcast(I32), 0)
         for q in range(QUADS):
@@ -142,7 +139,7 @@ def tile_list_modp_relu2_gateP_kernel(
             return gate
 
         gate = [gates(0, keep.tile([P, J], F32, name="gate0", align_bytes=64))]
-        page.append(clear_page(keep.tile([P, T], F32, name="page1", tag="g_rows0", align_bytes=64), nc.gpsimd))
+        page = [clear_page(keep.tile([P, T], F32, name="page0", tag="g_rows0", align_bytes=64), nc.gpsimd)]
         gate.extend(gates(t, keep.tile([P, J], F32, name="gate%d" % t, align_bytes=64)) for t in (1, 2))
         wds_p = laid.tile([P, PACK, P], U8, name="wds_p", align_bytes=64, offset=at_g[2])
         nc.vector.tensor_copy(wds_p[:], wd_s[:].rearrange("p (m t) -> p t m", t=PACK))
@@ -236,7 +233,7 @@ def tile_list_modp_relu2_gateP_kernel(
             return keep.tile([P, planes, count], F32, name=name, tag=tag, align_bytes=64)
 
         def later_page(t):
-            at_page = at_woven + 4 * J + 4 * T * (t - 2)
+            at_page = at_woven + 4 * J + 4 * T * (t - 1)
             return clear_page(laid.tile([P, T], F32, name="page%d" % t, align_bytes=64, offset=at_page), nc.gpsimd)
 
         turned = [turn_banks(k) for k in range(2)]
@@ -248,11 +245,11 @@ def tile_list_modp_relu2_gateP_kernel(
         woven = laid.tile([P, (J + 2 * T) // 2, PACK], BF16, name="woven0", align_bytes=64, offset=at_woven)[:, 0:CHUNK, :]
         h = quantise(weave(smooth(0, turned[0]), woven), codes, scales)
         gate.append(gates(3, laid.tile([P, J], F32, name="gate3", align_bytes=64, offset=at_woven)))
-        page.extend(later_page(t) for t in (2, 3))
+        page.extend(later_page(t) for t in (1, 2))
         rows = smooth(1, turned[1])
         banks = down(h, "turn1_")
         pos = [rectify(2, 0)]
-        y = drain("y0a", "y0a", banks[0])
+        y = drain("y0a", "h_codes1", banks[0])
         for t in range(2):
             put(t, 0, CHUNK, y[:, t, :])
         h = quantise(weave(rows, woven_tile(1, "woven1")), *h_tiles(1))
@@ -263,12 +260,13 @@ def tile_list_modp_relu2_gateP_kernel(
         y_high = y_tile("y_high", "pos0_0", 2, J)
         nc.scalar.copy(y_high[:, :, 0:CHUNK], banks[1][:])
         turn(1, pos[1], turned[2])
-        for t in range(2):
-            put(2 + t, 0, CHUNK, y_high[:, t, 0:CHUNK])
+        put(2, 0, CHUNK, y_high[:, 0, 0:CHUNK])
         banks = down(h, "spread")
         y = drain("y1a", "pos0_1", banks[0])
         for t in range(2):
             put(t, CHUNK, CHUNK, y[:, t, :])
+        page.append(clear_page(keep.tile([P, T], F32, name="page3", tag="h_codes1", align_bytes=64), nc.gpsimd))
+        put(3, 0, CHUNK, y_high[:, 1, 0:CHUNK])
         rows = smooth(2, turned[2])
         pos = [rectify(3, 0)]
         h = quantise(weave(rows, woven_tile(2, "woven2")), *h_tiles(2))

@@ -42,8 +42,8 @@ def tile_list_modp_relu2_gateP_kernel(
 
         at_wd_w = T + 8 * T
         at_g = [None, T, T + 4 * T, at_wd_w + 4 * N]
-        at_both = at_g[3] + 4 * T
-        at_wd_s = at_both
+        at_wd_s = at_g[3] + 4 * T
+        at_both = at_wd_s + N
         at_woven = at_both + 4 * T
         tab_s = keep.tile([P, T], U8, name="tab_s", align_bytes=64)[:]
         tab_w = keep.tile([P, T], I32, name="tab_w", align_bytes=64)[:]
@@ -57,7 +57,7 @@ def tile_list_modp_relu2_gateP_kernel(
             return cleared
 
         make_identity(nc, ident[:])
-        nc.gpsimd.memset(w_s[:].rearrange("p a r -> p (a r)").bitcast(I32), 0)
+        nc.vector.memset(w_s[:].rearrange("p a r -> p (a r)").bitcast(I32), 0)
         for q in range(QUADS):
             nc.gpsimd.dma_start(
                 w_s[32 * q : 32 * q + 4, :, :].bitcast(I32),
@@ -66,15 +66,9 @@ def tile_list_modp_relu2_gateP_kernel(
 
         nc.sync.dma_start(offsets[:], offs)
         s_rows = tab_scales.rearrange("a q c -> (a q) c").bitcast(I32)
-        for queue, first, rows, source in (
-            (nc.scalar, 32, 24, 4),
-            (nc.sync, 0, 32, 0),
-            (nc.sync, 56, 32, 0),
-            (nc.sync, 88, 16, 4),
-            (nc.sync, 104, 16, 16),
-            (nc.sync, 120, 8, 0),
-        ):
-            queue.dma_start(tab_s[first : first + rows, :].bitcast(I32), s_rows[source : source + rows, :])
+        nc.scalar.dma_start(tab_s[96:128, :].bitcast(I32), s_rows[12:16, :].unsqueeze(0).to_broadcast([8, 4, T // 4]))
+        for first, rows, source in ((0, 32, 0), (56, 32, 0), (32, 16, 4), (48, 8, 20), (88, 8, 4)):
+            nc.sync.dma_start(tab_s[first : first + rows, :].bitcast(I32), s_rows[source : source + rows, :])
         nc.sync.dma_start(tab_w, tab_words[0].rearrange("p c b -> p (c b)").bitcast(I32))
         nc.sync.dma_start(wu_w[:], wu_words.rearrange("a p r b -> p a (r b)").bitcast(I32))
         wgo_c = keep.tile([P, 2 * PACK], F32, name="wgo_c", align_bytes=64)
@@ -97,17 +91,13 @@ def tile_list_modp_relu2_gateP_kernel(
                 wgo_t[:].rearrange("c (p b i) -> c b p i", b=2, i=PACK)[:, b], spread[:].rearrange("c i p -> c p i")
             )
 
-        def pick_scales(start, count):
-            picked = keep.tile([P, count], U8, name="pick_s0_%d" % start, align_bytes=64)
-            nc.vector.tensor_copy(picked[:], tab_s.indirect(entries(start, count)))
-            moved = pick_s1[:, start : start + count]
-            for first, source in ((0, 16), (64, 52)):
-                nc.scalar.dma_start(
-                    moved[first : first + 64, :].bitcast(I32), picked[source : source + 64, :].bitcast(I32)
-                )
-            return [picked[:], moved]
-
-        pick_s = [pick_scales(0, CHUNK), pick_scales(CHUNK, J - CHUNK)]
+        pick_s0 = keep.tile([P, J], U8, name="pick_s0", align_bytes=64)
+        nc.vector.tensor_copy(pick_s0[:], tab_s.indirect(offsets[:]))
+        for first, source in ((0, 16), (64, 52)):
+            nc.scalar.dma_start(
+                pick_s1[first : first + 64, :].bitcast(I32), pick_s0[source : source + 64, :].bitcast(I32)
+            )
+        pick_s = [pick_s0, pick_s1]
 
         def pick_words(start, both):
             count = both.shape[1]
@@ -162,7 +152,7 @@ def tile_list_modp_relu2_gateP_kernel(
                 nc.tensor.matmul_mx(
                     out=sums[:],
                     lhsT=parted[part][:, a, 2 * lo : 2 * (lo + P)].bitcast(FP4X4),
-                    lhsT_scale=pick_s[part][a][:, lo : lo + P],
+                    lhsT_scale=pick_s[a][:, CHUNK * k + P * b : CHUNK * k + P * (b + 1)],
                     rhs=wu_w[:, a, :].bitcast(FP8X4),
                     rhs_scale=w_s[:, a, :],
                     start=(a == 0),
@@ -256,47 +246,41 @@ def tile_list_modp_relu2_gateP_kernel(
 
         pos.append(rectify(2, 1))
         turned.append(turn_banks(2))
-        turn(0, pos[0], turned[2])
-        y_high = y_tile("y_high", "pos0_0", 2, J)
+        for b in range(2):
+            turn(b, pos[b], turned[2])
+        y_high = y_tile("y_high", "pos0_1", 2, J)
         nc.scalar.copy(y_high[:, :, 0:CHUNK], banks[1][:])
-        turn(1, pos[1], turned[2])
         put(2, 0, CHUNK, y_high[:, 0, 0:CHUNK])
-        banks = down(h, "spread")
-        y = drain("y1a", "pos0_1", banks[0])
+        rows = smooth(2, turned[2])
+        banks = down(h, "turn0_")
+        y = drain("y1a", "y1a", banks[0])
         for t in range(2):
             put(t, CHUNK, CHUNK, y[:, t, :])
         page.append(clear_page(keep.tile([P, T], F32, name="page3", tag="h_codes1", align_bytes=64), nc.gpsimd))
         put(3, 0, CHUNK, y_high[:, 1, 0:CHUNK])
-        rows = smooth(2, turned[2])
-        pos = [rectify(3, 0)]
         h = quantise(weave(rows, woven_tile(2, "woven2")), *h_tiles(2))
 
-        pos.append(rectify(3, 1))
+        pos = [rectify(3, b) for b in range(2)]
         turned.append(turn_banks(3))
-        turn(0, pos[0], turned[3])
-        turn(1, pos[1], turned[3])
+        for b in range(2):
+            turn(b, pos[b], turned[3])
         nc.scalar.copy(y_high[:, :, CHUNK:HALF], banks[1][:])
-        for t in range(2):
-            put(2 + t, CHUNK, CHUNK, y_high[:, t, CHUNK:HALF])
+        put(2, CHUNK, CHUNK, y_high[:, 0, CHUNK:HALF])
         rows = smooth(3, turned[3])
         banks = down(h, "turn1_")
-        y_low = y_tile("y_low", "pos1_1", 2, HALF)
-        woven = weave(rows, woven_tile(3, "woven3"))
-        h = quantise(woven, *h_tiles(3))
-        y = y_tile("y2_0", "rows3", 1, CHUNK)
-        nc.scalar.copy(y[:, 0, :], banks[0][:, 0, :])
-        put(0, HALF, CHUNK, y[:, 0, :])
-        nc.scalar.copy(y_low[:, 1, 0:CHUNK], banks[0][:, 1, :])
+        h = quantise(weave(rows, woven_tile(3, "woven3")), *h_tiles(3))
+        y = drain("y2a", "rows3", banks[0])
+        for t in range(2):
+            put(t, HALF, CHUNK, y[:, t, :])
         nc.scalar.copy(y_high[:, :, HALF : J - CHUNK], banks[1][:])
 
         banks = down(h, "up")
-        for t in range(2):
-            nc.scalar.copy(y_low[:, t, CHUNK:HALF], banks[0][:, t, :])
+        y = drain("y3a", "y3a", banks[0])
         nc.scalar.copy(y_high[:, :, J - CHUNK : J], banks[1][:])
-        put(0, J - CHUNK, CHUNK, y_low[:, 0, CHUNK:HALF])
-        put(1, HALF, HALF, y_low[:, 1, :])
         for t in range(2):
-            put(2 + t, HALF, HALF, y_high[:, t, HALF:J])
+            put(t, J - CHUNK, CHUNK, y[:, t, :])
+        put(2, HALF, HALF, y_high[:, 0, HALF:J])
+        put(3, CHUNK, J - CHUNK, y_high[:, 1, CHUNK:J])
 
         out_rows = out_0.rearrange("(p t) c -> t p c", t=PACK)
         for t in range(PACK):

@@ -42,10 +42,11 @@ def tile_list_modp_relu2_gateP_kernel(
 
         at_wd_w = T + 8 * T
         at_g = [None, T, T + 4 * T, at_wd_w + 4 * N]
-        at_wd_s = at_g[3] + 4 * T
+        at_both0 = at_g[3] + 4 * T
+        at_wd_s = at_both0 + 4 * CHUNK
         at_both = at_wd_s + N
         at_woven = at_both + 4 * T
-        tab_s = keep.tile([P, T], U8, name="tab_s", align_bytes=64)[:]
+        tab_s = laid.tile([P, at_both0], U8, name="tab_s", align_bytes=64, offset=0)[:, 0:T]
         tab_w = keep.tile([P, T], I32, name="tab_w", align_bytes=64)[:]
         w_s = keep.tile([P, 2, R], U8, name="w_s", align_bytes=64)
         wu_w = keep.tile([P, 2, R], I32, name="wu_w", align_bytes=64)
@@ -58,11 +59,15 @@ def tile_list_modp_relu2_gateP_kernel(
 
         make_identity(nc, ident[:])
         nc.vector.memset(w_s[:].rearrange("p a r -> p (a r)").bitcast(I32), 0)
-        for q in range(QUADS):
-            nc.gpsimd.dma_start(
-                w_s[32 * q : 32 * q + 4, :, :].bitcast(I32),
-                wu_scales[:, 4 * q : 4 * q + 4, :].rearrange("a s r -> s a r").bitcast(I32),
-            )
+
+        def load_wu_scales(queue, quads):
+            for q in quads:
+                queue.dma_start(
+                    w_s[32 * q : 32 * q + 4, :, :].bitcast(I32),
+                    wu_scales[:, 4 * q : 4 * q + 4, :].rearrange("a s r -> s a r").bitcast(I32),
+                )
+
+        load_wu_scales(nc.gpsimd, (0, 1))
 
         nc.sync.dma_start(offsets[:], offs)
         s_rows = tab_scales.rearrange("a q c -> (a q) c").bitcast(I32)
@@ -71,6 +76,7 @@ def tile_list_modp_relu2_gateP_kernel(
             nc.sync.dma_start(tab_s[first : first + rows, :].bitcast(I32), s_rows[source : source + rows, :])
         nc.sync.dma_start(tab_w, tab_words[0].rearrange("p c b -> p (c b)").bitcast(I32))
         nc.sync.dma_start(wu_w[:], wu_words.rearrange("a p r b -> p a (r b)").bitcast(I32))
+        load_wu_scales(nc.sync, (2, 3))
         wgo_c = keep.tile([P, 2 * PACK], F32, name="wgo_c", align_bytes=64)
         nc.sync.dma_start(wgo_c[:], wgo[0].rearrange("(p i) -> p i", p=P))
 
@@ -79,8 +85,6 @@ def tile_list_modp_relu2_gateP_kernel(
             return rows
 
         g_rows = [load_gates(0, keep.tile([P, T], F32, name="g_rows0", tag="g_rows0", align_bytes=64))]
-        sm_t = keep.tile([P, PACK], F32, name="sm_t", align_bytes=64)
-        nc.sync.dma_start(sm_t[:], sm.rearrange("(p t) -> p t", t=PACK))
         wgo_t = keep.tile([P, J], F32, name="wgo_t", align_bytes=64)
         for b in range(2):
             spread = psum.tile([P, PACK, P], F32, name="spread%d" % b, tag="spread%d" % b)
@@ -91,13 +95,18 @@ def tile_list_modp_relu2_gateP_kernel(
                 wgo_t[:].rearrange("c (p b i) -> c b p i", b=2, i=PACK)[:, b], spread[:].rearrange("c i p -> c p i")
             )
 
-        pick_s0 = keep.tile([P, J], U8, name="pick_s0", align_bytes=64)
-        nc.vector.tensor_copy(pick_s0[:], tab_s.indirect(offsets[:]))
-        for first, source in ((0, 16), (64, 52)):
-            nc.scalar.dma_start(
-                pick_s1[first : first + 64, :].bitcast(I32), pick_s0[source : source + 64, :].bitcast(I32)
-            )
-        pick_s = [pick_s0, pick_s1]
+        def pick_scales(start):
+            picked = keep.tile([P, HALF], U8, name="pick_s0_%d" % start, align_bytes=64)
+            nc.vector.tensor_copy(picked[:], tab_s.indirect(entries(start, HALF)))
+            return [picked[:], pick_s1[:, start : start + HALF]]
+
+        def move_scales(queue, picked, moved):
+            for first, source in ((0, 16), (64, 52)):
+                queue.dma_start(moved[first : first + 64, :].bitcast(I32), picked[source : source + 64, :].bitcast(I32))
+
+        pick_s = [pick_scales(0)]
+        move_scales(nc.scalar, *pick_s[0])
+        pick_s.append(pick_scales(HALF))
 
         def pick_words(start, both):
             count = both.shape[1]
@@ -109,20 +118,23 @@ def tile_list_modp_relu2_gateP_kernel(
             return parted
 
         parted = [
-            pick_words(0, laid.tile([P, at_both // 4], I32, name="both0", align_bytes=64, offset=0)[:, 0:CHUNK]),
+            pick_words(0, laid.tile([P, CHUNK + N // 4], I32, name="both0", align_bytes=64, offset=at_both0)[:, 0:CHUNK]),
             pick_words(CHUNK, laid.tile([P, J - CHUNK], I32, name="both1", align_bytes=64, offset=at_both)),
         ]
         g_rows.append(load_gates(1, laid.tile([P, T], F32, name="g_rows1", align_bytes=64, offset=at_g[1])))
         g_rows.append(load_gates(2, laid.tile([P, T], F32, name="g_rows2", align_bytes=64, offset=at_g[2])))
+        move_scales(nc.sync, *pick_s[1])
+        sm_t = laid.tile([P, PACK], F32, name="sm_t", align_bytes=64, offset=0)
+        nc.sync.dma_start(sm_t[:], sm.rearrange("(p t) -> p t", t=PACK))
         wd_w = laid.tile([P, N], I32, name="wd_w", align_bytes=64, offset=at_wd_w)
         nc.sync.dma_start(wd_w[:], wd_words[0].rearrange("p n b -> p (n b)").bitcast(I32))
-        g_rows.append(load_gates(3, laid.tile([P, T], F32, name="g_rows3", align_bytes=64, offset=at_g[3])))
         wd_s = laid.tile([P, N], U8, name="wd_s", align_bytes=64, offset=at_wd_s)
         nc.gpsimd.memset(wd_s[:].bitcast(I32), 0)
         for q in range(QUADS):
-            nc.gpsimd.dma_start(
+            (nc.gpsimd if q < 2 else nc.sync).dma_start(
                 wd_s[32 * q : 32 * q + 4, :].bitcast(I32), wd_scales[0, 4 * q : 4 * q + 4, :].bitcast(I32)
             )
+        g_rows.append(load_gates(3, laid.tile([P, T], F32, name="g_rows3", align_bytes=64, offset=at_g[3])))
 
         def gates(t, gate):
             nc.vector.tensor_tensor(gate[:], g_rows[t][:].indirect(offsets[:]), wgo_t[:], MULT)
@@ -142,17 +154,17 @@ def tile_list_modp_relu2_gateP_kernel(
             return psum.tile(shape, F32, name=tag, tag=tag)
 
         def turn_banks(k):
-            return [bank("turn%d_%d" % (k % 2, b), [P, 2, CHUNK]) for b in range(2)]
+            return [bank("%s%d" % (("turn0_", "turn1_", "spread", "turn1_")[k], b), [P, 2, CHUNK]) for b in range(2)]
 
         def rectify(k, b):
             part, first = (0, 0) if k == 0 else (1, CHUNK * (k - 1))
             lo = first + P * b
-            sums = bank("up%d" % b, [P, R])
+            sums = bank("%s%d" % ("up" if k < 2 else "turn0_", b), [P, R])
             for a in range(2):
                 nc.tensor.matmul_mx(
                     out=sums[:],
                     lhsT=parted[part][:, a, 2 * lo : 2 * (lo + P)].bitcast(FP4X4),
-                    lhsT_scale=pick_s[a][:, CHUNK * k + P * b : CHUNK * k + P * (b + 1)],
+                    lhsT_scale=pick_s[k // 2][a][:, CHUNK * (k % 2) + P * b : CHUNK * (k % 2) + P * (b + 1)],
                     rhs=wu_w[:, a, :].bitcast(FP8X4),
                     rhs_scale=w_s[:, a, :],
                     start=(a == 0),
@@ -252,7 +264,7 @@ def tile_list_modp_relu2_gateP_kernel(
         nc.scalar.copy(y_high[:, :, 0:CHUNK], banks[1][:])
         put(2, 0, CHUNK, y_high[:, 0, 0:CHUNK])
         rows = smooth(2, turned[2])
-        banks = down(h, "turn0_")
+        banks = down(h, "spread")
         y = drain("y1a", "y1a", banks[0])
         for t in range(2):
             put(t, CHUNK, CHUNK, y[:, t, :])

@@ -226,6 +226,11 @@ def tile_list_modp_relu2_gateP_kernel(
             nc.scalar.copy(held[:], acc[:])
             return held
 
+        def drain_plane(name, tag, acc, plane):
+            held = keep.tile([P, CHUNK], F32, name=name, tag=tag, align_bytes=64)
+            nc.scalar.copy(held[:], acc[:, plane, :])
+            return held[:]
+
         def put(t, start, count, y):
             nc.vector.tensor_tensor(
                 page[t][:].indirect(entries(start, count)), y, gate[t][:, start : start + count], MULT
@@ -239,24 +244,27 @@ def tile_list_modp_relu2_gateP_kernel(
             return clear_page(laid.tile([P, T], F32, name="page%d" % t, align_bytes=64, offset=at_page), nc.gpsimd)
 
         turned = [turn_banks(k) for k in range(2)]
-        for k in range(2):
-            for b in range(2):
-                turn(b, rectify(k, b), turned[k])
+        for b in range(2):
+            turn(b, rectify(0, b), turned[0])
+        pos = rectify(1, 0)
+        rows = smooth(0, turned[0])
+        turn(0, pos, turned[1])
         codes = laid.tile([P, CHUNK], I32, name="h_codes0", align_bytes=64, offset=at_wd_w - 2 * CHUNK)
         scales = laid.tile([P, CHUNK], U8, name="h_scales0", align_bytes=64, offset=at_wd_s)
         woven = laid.tile([P, (J + 2 * T) // 2, PACK], BF16, name="woven0", align_bytes=64, offset=at_woven)[:, 0:CHUNK, :]
-        h = quantise(weave(smooth(0, turned[0]), woven), codes, scales)
+        h = quantise(weave(rows, woven), codes, scales)
+        turn(1, rectify(1, 1), turned[1])
         gate.append(gates(3, laid.tile([P, J], F32, name="gate3", align_bytes=64, offset=at_woven)))
         page.extend(later_page(t) for t in (1, 2))
-        rows = smooth(1, turned[1])
-        banks = down(h, "turn1_")
+        banks = down(h, "up")
         pos = [rectify(2, 0)]
         y = drain("y0a", "h_codes1", banks[0])
         for t in range(2):
             put(t, 0, CHUNK, y[:, t, :])
+        rows = smooth(1, turned[1])
+        pos.append(rectify(2, 1))
         h = quantise(weave(rows, woven_tile(1, "woven1")), *h_tiles(1))
 
-        pos.append(rectify(2, 1))
         turned.append(turn_banks(2))
         for b in range(2):
             turn(b, pos[b], turned[2])
@@ -265,32 +273,28 @@ def tile_list_modp_relu2_gateP_kernel(
         put(2, 0, CHUNK, y_high[:, 0, 0:CHUNK])
         rows = smooth(2, turned[2])
         banks = down(h, "spread")
-        y = drain("y1a", "y1a", banks[0])
-        for t in range(2):
-            put(t, CHUNK, CHUNK, y[:, t, :])
-        page.append(clear_page(keep.tile([P, T], F32, name="page3", tag="h_codes1", align_bytes=64), nc.gpsimd))
+        put(0, CHUNK, CHUNK, drain_plane("y1_0", "y1_0", banks[0], 0))
+        h = quantise(weave(rows, woven_tile(2, "page3")), *h_tiles(2))
+        page.append(clear_page(keep.tile([P, T], F32, name="page3", tag="page3", align_bytes=64), nc.gpsimd))
+        put(1, CHUNK, CHUNK, drain_plane("y1_1", "rows2", banks[0], 1))
+        nc.scalar.copy(y_high[:, :, CHUNK:HALF], banks[1][:])
+        put(2, CHUNK, CHUNK, y_high[:, 0, CHUNK:HALF])
         put(3, 0, CHUNK, y_high[:, 1, 0:CHUNK])
-        h = quantise(weave(rows, woven_tile(2, "woven2")), *h_tiles(2))
 
+        banks = down(h, "up")
         pos = [rectify(3, b) for b in range(2)]
         turned.append(turn_banks(3))
         for b in range(2):
             turn(b, pos[b], turned[3])
-        nc.scalar.copy(y_high[:, :, CHUNK:HALF], banks[1][:])
-        put(2, CHUNK, CHUNK, y_high[:, 0, CHUNK:HALF])
-        rows = smooth(3, turned[3])
-        banks = down(h, "turn1_")
-        h = quantise(weave(rows, woven_tile(3, "woven3")), *h_tiles(3))
-        y = drain("y2a", "rows3", banks[0])
-        for t in range(2):
-            put(t, HALF, CHUNK, y[:, t, :])
+        put(0, HALF, CHUNK, drain_plane("y2_0", "pos1_1", banks[0], 0))
+        h = quantise(weave(smooth(3, turned[3]), woven_tile(3, "woven3")), *h_tiles(3))
+        put(1, HALF, CHUNK, drain_plane("y2_1", "rows3", banks[0], 1))
         nc.scalar.copy(y_high[:, :, HALF : J - CHUNK], banks[1][:])
 
-        banks = down(h, "up")
-        y = drain("y3a", "y3a", banks[0])
-        nc.scalar.copy(y_high[:, :, J - CHUNK : J], banks[1][:])
+        banks = down(h, "turn0_")
         for t in range(2):
-            put(t, J - CHUNK, CHUNK, y[:, t, :])
+            put(t, J - CHUNK, CHUNK, drain_plane("y3_%d" % t, "y3_%d" % t, banks[0], t))
+        nc.scalar.copy(y_high[:, :, J - CHUNK : J], banks[1][:])
         put(2, HALF, HALF, y_high[:, 0, HALF:J])
         put(3, CHUNK, J - CHUNK, y_high[:, 1, CHUNK:J])
 

@@ -143,7 +143,7 @@ def tile_list_modp_relu2_gateP_kernel(
         gate = [gates(0, keep.tile([P, J], F32, name="gate0", align_bytes=64))]
         page = [clear_page(keep.tile([P, T], F32, name="page0", tag="g_rows0", align_bytes=64), nc.gpsimd)]
         gate.extend(gates(t, keep.tile([P, J], F32, name="gate%d" % t, align_bytes=64)) for t in (1, 2))
-        wds_p = laid.tile([P, PACK, P], U8, name="wds_p", align_bytes=64, offset=at_g[2])
+        wds_p = keep.tile([P, PACK, P], U8, name="wds_p", align_bytes=64)
         nc.vector.tensor_copy(wds_p[:], wd_s[:].rearrange("p (m t) -> p t m", t=PACK))
         wd_p = keep.tile([P, PACK, P], I32, name="wd_p", align_bytes=64)
         nc.vector.tensor_copy(
@@ -240,7 +240,7 @@ def tile_list_modp_relu2_gateP_kernel(
             return keep.tile([P, planes, count], F32, name=name, tag=tag, align_bytes=64)
 
         def later_page(t):
-            at_page = at_woven + 4 * J + 4 * T * (t - 1)
+            at_page = at_woven + 4 * T * (t - 1)
             return clear_page(laid.tile([P, T], F32, name="page%d" % t, align_bytes=64, offset=at_page), nc.gpsimd)
 
         turned = [turn_banks(k) for k in range(2)]
@@ -249,16 +249,14 @@ def tile_list_modp_relu2_gateP_kernel(
         pos = rectify(1, 0)
         rows = smooth(0, turned[0])
         turn(0, pos, turned[1])
-        codes = laid.tile([P, CHUNK], I32, name="h_codes0", align_bytes=64, offset=at_wd_w - 2 * CHUNK)
-        scales = laid.tile([P, CHUNK], U8, name="h_scales0", align_bytes=64, offset=at_wd_s)
-        woven = laid.tile([P, (J + 2 * T) // 2, PACK], BF16, name="woven0", align_bytes=64, offset=at_woven)[:, 0:CHUNK, :]
-        h = quantise(weave(rows, woven), codes, scales)
+        woven = laid.tile([P, T, PACK], BF16, name="woven0", align_bytes=64, offset=at_woven)[:, 0:CHUNK, :]
+        h = quantise(weave(rows, woven), *h_tiles(0))
         turn(1, rectify(1, 1), turned[1])
-        gate.append(gates(3, laid.tile([P, J], F32, name="gate3", align_bytes=64, offset=at_woven)))
+        gate.append(gates(3, keep.tile([P, J], F32, name="gate3", tag="rows0", align_bytes=64)))
         page.extend(later_page(t) for t in (1, 2))
         banks = down(h, "up")
         pos = [rectify(2, 0)]
-        y = drain("y0a", "h_codes1", banks[0])
+        y = drain("y0a", "y0a", banks[0])
         for t in range(2):
             put(t, 0, CHUNK, y[:, t, :])
         rows = smooth(1, turned[1])
@@ -339,7 +337,8 @@ def tile_list_modp_relu2_gateP_kernel(
             nc.scalar.copy(pairs[s][:, 1, :, 1], page[3][:, c : c + n])
             for k in ks:
                 weave_out(nc.scalar.copy, s, k)
-        nc.vector.tensor_copy(pairs[0][:, 1, :, 1], page[3][:, 0:split])
+        for first, last in ((0, HALF), (HALF, split)):
+            nc.vector.tensor_copy(pairs[0][:, 1, first:last, 1], page[3][:, first:last])
         weave_out(nc.vector.tensor_copy, 0, 0)
         weave_out(nc.vector.tensor_copy, 0, 1)
         planes(0)

@@ -304,16 +304,14 @@ def tile_list_modp_relu2_gateP_kernel(
         o_codes = keep.tile([P, T], I32, name="o_codes", align_bytes=64)
         words_out = out_1[0].rearrange("p c b -> p (c b)").bitcast(I32)
         split = T // 2 + P
-        spans = [(0, split), (split, HALF - P), (T - HALF, HALF)]
+        own = HALF + CHUNK
+        spans = [(0, own), (own, split - own), (split, HALF - P), (T - HALF, HALF)]
         chunks = [(c, HALF) for c in range(0, T // 2, HALF)] + [(c, CHUNK) for c in range(T // 2, T, CHUNK)]
         woven_o = [keep.tile([P, n, 2], U32, name="woven_o%d" % c, align_bytes=64) for c, n in chunks]
         pairs = [keep.tile([P, 2, n, 2], BF16, name="pairs%d" % c, align_bytes=64) for c, n in spans]
         for t in range(3):
             for (c, n), pair in zip(spans, pairs):
-                if t == 2 and c < split:
-                    both_halves = page[t][:, c : c + n].unsqueeze(2).to_broadcast([P, n, 2])
-                    nc.scalar.copy(pair[:, 1, :, :], both_halves)
-                else:
+                if t < 2 or c > 0:
                     nc.scalar.copy(pair[:, t // 2, :, t % 2], page[t][:, c : c + n])
 
         def weave_out(engine_copy, s, k):
@@ -332,17 +330,20 @@ def tile_list_modp_relu2_gateP_kernel(
             if (c + n) % HALF == 0:
                 nc.sync.dma_start(words_out[:, c + n - HALF : c + n], o_codes[:, c + n - HALF : c + n])
 
-        for s, ks in ((1, (2, 3)), (2, (4, 5))):
+        nc.scalar.copy(pairs[1][:, 1, :, 1], page[3][:, own:split])
+        for s, ks in ((2, (2, 3)), (3, (4, 5))):
             c, n = spans[s]
             nc.scalar.copy(pairs[s][:, 1, :, 1], page[3][:, c : c + n])
             for k in ks:
                 weave_out(nc.scalar.copy, s, k)
-        for first, last in ((0, HALF), (HALF, split)):
-            nc.vector.tensor_copy(pairs[0][:, 1, first:last, 1], page[3][:, first:last])
+        for t in (2, 3):
+            for first, last in ((0, HALF), (HALF, own)):
+                nc.vector.tensor_copy(pairs[0][:, 1, first:last, t % 2], page[t][:, first:last])
         weave_out(nc.vector.tensor_copy, 0, 0)
         weave_out(nc.vector.tensor_copy, 0, 1)
+        weave_out(nc.vector.tensor_copy, 1, 1)
         planes(0)
-        weave_out(nc.vector.tensor_copy, 0, 2)
+        weave_out(nc.vector.tensor_copy, 1, 2)
         for k in range(1, len(chunks)):
             planes(k)
         for q in range(QUADS):

@@ -109,18 +109,23 @@ def tile_list_modp_relu2_gateP_kernel(
         pick_s.append(pick_scales(HALF))
 
         def pick_words(start, both):
-            count = both.shape[1]
-            nc.vector.tensor_copy(both[:].bitcast(U32), tab_w.bitcast(U32).indirect(entries(start, count)))
-            parted = keep.tile([P, 2, 2 * count], U8, name="parted%d" % start, align_bytes=64)
+            nc.vector.tensor_copy(both[:].bitcast(U32), tab_w.bitcast(U32).indirect(entries(start, both.shape[1])))
+            return both
+
+        def part_words(start, both):
+            parted = keep.tile([P, 2, 2 * both.shape[1]], U8, name="parted%d" % start, align_bytes=64)
             nc.vector.tensor_copy(
                 parted[:].bitcast(U16), both[:].bitcast(U16).rearrange("p (j d) -> p d j", d=2)
             )
             return parted
 
-        parted = [
+        both = [
             pick_words(0, laid.tile([P, CHUNK + N // 4], I32, name="both0", align_bytes=64, offset=at_both0)[:, 0:CHUNK]),
-            pick_words(CHUNK, laid.tile([P, J - CHUNK], I32, name="both1", align_bytes=64, offset=at_both)),
+            pick_words(CHUNK, keep.tile([P, CHUNK], I32, name="both1", align_bytes=64)),
         ]
+        parted = [part_words(0, both[0])]
+        both.append(pick_words(HALF, laid.tile([P, HALF], I32, name="both2", align_bytes=64, offset=at_both)))
+        parted.extend(part_words(start, both[i]) for i, start in ((1, CHUNK), (2, HALF)))
         g_rows.append(load_gates(1, laid.tile([P, T], F32, name="g_rows1", align_bytes=64, offset=at_g[1])))
         g_rows.append(load_gates(2, laid.tile([P, T], F32, name="g_rows2", align_bytes=64, offset=at_g[2])))
         move_scales(nc.sync, *pick_s[1])
@@ -146,9 +151,6 @@ def tile_list_modp_relu2_gateP_kernel(
         wds_p = keep.tile([P, PACK, P], U8, name="wds_p", align_bytes=64)
         nc.vector.tensor_copy(wds_p[:], wd_s[:].rearrange("p (m t) -> p t m", t=PACK))
         wd_p = keep.tile([P, PACK, P], I32, name="wd_p", align_bytes=64)
-        nc.vector.tensor_copy(
-            wd_p[:].rearrange("p t (c i) -> p c t i", i=4), wd_w[:].rearrange("p (c i t) -> p c t i", i=4, t=PACK)
-        )
 
         def bank(tag, shape):
             return psum.tile(shape, F32, name=tag, tag=tag)
@@ -157,7 +159,7 @@ def tile_list_modp_relu2_gateP_kernel(
             return [bank("%s%d" % (("turn0_", "turn1_", "spread", "turn1_")[k], b), [P, 2, CHUNK]) for b in range(2)]
 
         def rectify(k, b):
-            part, first = (0, 0) if k == 0 else (1, CHUNK * (k - 1))
+            part, first = (k, 0) if k < 2 else (2, CHUNK * (k - 2))
             lo = first + P * b
             sums = bank("%s%d" % ("up" if k < 2 else "turn0_", b), [P, R])
             for a in range(2):
@@ -251,6 +253,10 @@ def tile_list_modp_relu2_gateP_kernel(
         turn(0, pos, turned[1])
         woven = laid.tile([P, T, PACK], BF16, name="woven0", align_bytes=64, offset=at_woven)[:, 0:CHUNK, :]
         h = quantise(weave(rows, woven), *h_tiles(0))
+        nc.scalar.copy(
+            wd_p[:].bitcast(U32).rearrange("p t (c i) -> p c t i", i=4),
+            wd_w[:].bitcast(U32).rearrange("p (c i t) -> p c t i", i=4, t=PACK),
+        )
         turn(1, rectify(1, 1), turned[1])
         gate.append(gates(3, keep.tile([P, J], F32, name="gate3", tag="rows0", align_bytes=64)))
         page.extend(later_page(t) for t in (1, 2))

@@ -21,8 +21,8 @@ P = 128
 PACK = 4
 QUADS = 4
 HALF = 512
-CHUNK = 256
-PIECES = J // CHUNK
+PIECE = 256
+KIB = 1024
 
 
 def tile_list_modp_relu2_gateP_kernel(
@@ -34,60 +34,69 @@ def tile_list_modp_relu2_gateP_kernel(
         laid = ctx.enter_context(tc.tile_pool(name="laid", bufs=1))
         psum = ctx.enter_context(tc.psum_pool(name="psum", bufs=1))
 
+        def fresh(name, shape, dtype, tag=None):
+            return keep.tile(shape, dtype, name=name, tag=tag or name, align_bytes=64)
+
+        def placed(name, shape, dtype, kib):
+            return laid.tile(shape, dtype, name=name, align_bytes=64, offset=kib * KIB)
+
+        def bank(tag, shape):
+            return psum.tile(shape, F32, name=tag, tag=tag)
+
         def entries(start, count):
             return offsets[:, start // 16 : (start + count) // 16]
 
+        AT_G1 = 2
+        AT_BOTH0 = 10
+        AT_BOTH2 = 12
+        AT_G2 = 14
+        AT_WD = 22
+        AT_G3 = 30
+        AT_PAGES = 38
+        AT_ROWS1 = 62
+
         offsets = keep.tile([P, J // 16], U16, name="offsets")
-        g_src = gT.rearrange("(p t) c -> t p c", t=PACK)
-
-        at_wd_w = T + 8 * T
-        at_g = [None, T, T + 4 * T, at_wd_w + 4 * N]
-        at_both0 = at_g[3] + 4 * T
-        at_wd_s = at_both0 + 4 * CHUNK
-        at_both = at_wd_s + N
-        at_woven = at_both + 4 * T
-        tab_s = laid.tile([P, at_both0], U8, name="tab_s", align_bytes=64, offset=0)[:, 0:T]
-        tab_w = keep.tile([P, T], I32, name="tab_w", align_bytes=64)[:]
-        w_s = keep.tile([P, 2, R], U8, name="w_s", align_bytes=64)
-        wu_w = keep.tile([P, 2, R], I32, name="wu_w", align_bytes=64)
-        pick_s1 = keep.tile([P, J], U8, name="pick_s1", align_bytes=64)
-        ident = keep.tile([P, P], F32, name="ident", align_bytes=64)
-
-        def clear_page(cleared, engine):
-            engine.memset(cleared[:].bitcast(I32), 0)
-            return cleared
+        tab_s = placed("tab_s", [P, 10 * KIB], U8, 0)[:, 0:T]
+        tab_w = fresh("tab_w", [P, T], I32)
+        wu_s = fresh("wu_s", [P, 2, R], U8)
+        wu_w = fresh("wu_w", [P, 2, R], I32)
+        sm_t = fresh("sm_t", [P, PACK], F32)
+        wgo_c = fresh("wgo_c", [P, 2 * PACK], F32)
+        ident = fresh("ident", [P, P], F32)
 
         make_identity(nc, ident[:])
-        nc.vector.memset(w_s[:].rearrange("p a r -> p (a r)").bitcast(I32), 0)
+        nc.vector.memset(wu_s[:].rearrange("p a r -> p (a r)").bitcast(I32), 0)
 
         def load_wu_scales(queue, quads):
             for q in quads:
                 queue.dma_start(
-                    w_s[32 * q : 32 * q + 4, :, :].bitcast(I32),
+                    wu_s[32 * q : 32 * q + 4, :, :].bitcast(I32),
                     wu_scales[:, 4 * q : 4 * q + 4, :].rearrange("a s r -> s a r").bitcast(I32),
                 )
 
         load_wu_scales(nc.gpsimd, (0, 1))
+        nc.gpsimd.dma_start(sm_t[:], sm.rearrange("(p t) -> p t", t=PACK))
 
         nc.sync.dma_start(offsets[:], offs)
         s_rows = tab_scales.rearrange("a q c -> (a q) c").bitcast(I32)
         nc.scalar.dma_start(tab_s[96:128, :].bitcast(I32), s_rows[12:16, :].unsqueeze(0).to_broadcast([8, 4, T // 4]))
         for first, rows, source in ((0, 32, 0), (56, 32, 0), (32, 16, 4), (48, 8, 20), (88, 8, 4)):
             nc.sync.dma_start(tab_s[first : first + rows, :].bitcast(I32), s_rows[source : source + rows, :])
-        nc.sync.dma_start(tab_w, tab_words[0].rearrange("p c b -> p (c b)").bitcast(I32))
+        nc.sync.dma_start(tab_w[:], tab_words[0].rearrange("p c b -> p (c b)").bitcast(I32))
         nc.sync.dma_start(wu_w[:], wu_words.rearrange("a p r b -> p a (r b)").bitcast(I32))
         load_wu_scales(nc.sync, (2, 3))
-        wgo_c = keep.tile([P, 2 * PACK], F32, name="wgo_c", align_bytes=64)
         nc.sync.dma_start(wgo_c[:], wgo[0].rearrange("(p i) -> p i", p=P))
+
+        g_src = gT.rearrange("(p t) c -> t p c", t=PACK)
 
         def load_gates(t, rows):
             nc.sync.dma_start(rows[:], g_src[t])
             return rows
 
-        g_rows = [load_gates(0, keep.tile([P, T], F32, name="g_rows0", tag="g_rows0", align_bytes=64))]
-        wgo_t = keep.tile([P, J], F32, name="wgo_t", align_bytes=64)
+        g_rows = [load_gates(0, fresh("g_rows0", [P, T], F32))]
+        wgo_t = fresh("wgo_t", [P, J], F32)
         for b in range(2):
-            spread = psum.tile([P, PACK, P], F32, name="spread%d" % b, tag="spread%d" % b)
+            spread = bank("spread%d" % b, [P, PACK, P])
             for i in range(PACK):
                 column = wgo_c[:, PACK * b + i : PACK * b + i + 1]
                 nc.tensor.transpose(spread[:, i, :], column.to_broadcast([P, P]), ident[:])
@@ -95,10 +104,12 @@ def tile_list_modp_relu2_gateP_kernel(
                 wgo_t[:].rearrange("c (p b i) -> c b p i", b=2, i=PACK)[:, b], spread[:].rearrange("c i p -> c p i")
             )
 
+        moved_s = fresh("moved_s", [P, J], U8)
+
         def pick_scales(start):
-            picked = keep.tile([P, HALF], U8, name="pick_s0_%d" % start, align_bytes=64)
+            picked = fresh("picked_s%d" % start, [P, HALF], U8)
             nc.vector.tensor_copy(picked[:], tab_s.indirect(entries(start, HALF)))
-            return [picked[:], pick_s1[:, start : start + HALF]]
+            return [picked[:], moved_s[:, start : start + HALF]]
 
         def move_scales(queue, picked, moved):
             for first, source in ((0, 16), (64, 52)):
@@ -107,200 +118,186 @@ def tile_list_modp_relu2_gateP_kernel(
         pick_s = [pick_scales(0)]
         move_scales(nc.scalar, *pick_s[0])
         pick_s.append(pick_scales(HALF))
+        g_rows.append(load_gates(1, placed("g_rows1", [P, T], F32, AT_G1)))
+        move_scales(nc.sync, *pick_s[1])
 
         def pick_words(start, both):
-            nc.vector.tensor_copy(both[:].bitcast(U32), tab_w.bitcast(U32).indirect(entries(start, both.shape[1])))
+            nc.vector.tensor_copy(both.bitcast(U32), tab_w[:].bitcast(U32).indirect(entries(start, both.shape[1])))
             return both
 
         def part_words(start, both):
-            parted = keep.tile([P, 2, 2 * both.shape[1]], U8, name="parted%d" % start, align_bytes=64)
-            nc.vector.tensor_copy(
-                parted[:].bitcast(U16), both[:].bitcast(U16).rearrange("p (j d) -> p d j", d=2)
-            )
+            parted = fresh("parted%d" % start, [P, 2, 2 * both.shape[1]], U8)
+            nc.vector.tensor_copy(parted[:].bitcast(U16), both.bitcast(U16).rearrange("p (j d) -> p d j", d=2))
             return parted
 
         both = [
-            pick_words(0, laid.tile([P, CHUNK + N // 4], I32, name="both0", align_bytes=64, offset=at_both0)[:, 0:CHUNK]),
-            pick_words(CHUNK, keep.tile([P, CHUNK], I32, name="both1", align_bytes=64)),
+            pick_words(0, placed("both0", [P, 2 * PIECE], I32, AT_BOTH0)[:, 0:PIECE]),
+            pick_words(PIECE, fresh("both1", [P, PIECE], I32)[:]),
         ]
         parted = [part_words(0, both[0])]
-        both.append(pick_words(HALF, laid.tile([P, HALF], I32, name="both2", align_bytes=64, offset=at_both)))
-        parted.extend(part_words(start, both[i]) for i, start in ((1, CHUNK), (2, HALF)))
-        g_rows.append(load_gates(1, laid.tile([P, T], F32, name="g_rows1", align_bytes=64, offset=at_g[1])))
-        g_rows.append(load_gates(2, laid.tile([P, T], F32, name="g_rows2", align_bytes=64, offset=at_g[2])))
-        move_scales(nc.sync, *pick_s[1])
-        sm_t = laid.tile([P, PACK], F32, name="sm_t", align_bytes=64, offset=0)
-        nc.sync.dma_start(sm_t[:], sm.rearrange("(p t) -> p t", t=PACK))
-        wd_w = laid.tile([P, N], I32, name="wd_w", align_bytes=64, offset=at_wd_w)
-        nc.sync.dma_start(wd_w[:], wd_words[0].rearrange("p n b -> p (n b)").bitcast(I32))
-        wd_s = laid.tile([P, N], U8, name="wd_s", align_bytes=64, offset=at_wd_s)
+        both.append(pick_words(HALF, placed("both2", [P, (AT_PAGES - AT_BOTH2) * KIB // 4], I32, AT_BOTH2)[:, 0:HALF]))
+        parted.extend(part_words(start, both[i]) for i, start in ((1, PIECE), (2, HALF)))
+        wd_s = placed("wd_s", [P, N], U8, AT_BOTH0 + 1)
         nc.gpsimd.memset(wd_s[:].bitcast(I32), 0)
         for q in range(QUADS):
             (nc.gpsimd if q < 2 else nc.sync).dma_start(
                 wd_s[32 * q : 32 * q + 4, :].bitcast(I32), wd_scales[0, 4 * q : 4 * q + 4, :].bitcast(I32)
             )
-        g_rows.append(load_gates(3, laid.tile([P, T], F32, name="g_rows3", align_bytes=64, offset=at_g[3])))
+        g_rows.append(load_gates(2, placed("g_rows2", [P, T], F32, AT_G2)))
+        wd_w = placed("wd_w", [P, 4 * N], I32, AT_WD)[:, 0:N]
+        nc.sync.dma_start(wd_w, wd_words[0].rearrange("p n b -> p (n b)").bitcast(I32))
+        g_rows.append(load_gates(3, placed("g_rows3", [P, T], F32, AT_G3)))
 
         def gates(t, gate):
             nc.vector.tensor_tensor(gate[:], g_rows[t][:].indirect(offsets[:]), wgo_t[:], MULT)
             return gate
 
-        gate = [gates(0, keep.tile([P, J], F32, name="gate0", align_bytes=64))]
-        page = [clear_page(keep.tile([P, T], F32, name="page0", tag="g_rows0", align_bytes=64), nc.gpsimd)]
-        gate.extend(gates(t, keep.tile([P, J], F32, name="gate%d" % t, align_bytes=64)) for t in (1, 2))
-        wds_p = keep.tile([P, PACK, P], U8, name="wds_p", align_bytes=64)
+        def cleared(page):
+            nc.gpsimd.memset(page[:].bitcast(I32), 0)
+            return page
+
+        def gate_tile(t):
+            return fresh("gate%d" % t, [P, J], F32)
+
+        gate = [gates(0, gate_tile(0))]
+        page = [cleared(fresh("page0", [P, T], F32, "g_rows0"))]
+        gate.append(gates(1, gate_tile(1)))
+        wds_p = fresh("wds_p", [P, PACK, P], U8)
         nc.vector.tensor_copy(wds_p[:], wd_s[:].rearrange("p (m t) -> p t m", t=PACK))
-        wd_p = keep.tile([P, PACK, P], I32, name="wd_p", align_bytes=64)
 
-        def bank(tag, shape):
-            return psum.tile(shape, F32, name=tag, tag=tag)
-
-        def turn_banks(k):
-            return [bank("%s%d" % (("turn0_", "turn1_", "spread", "turn1_")[k], b), [P, 2, CHUNK]) for b in range(2)]
-
-        def rectify(k, b):
-            part, first = (k, 0) if k < 2 else (2, CHUNK * (k - 2))
+        def rectify(k, b, pos):
+            part, first = (k, 0) if k < 2 else (2, PIECE * (k - 2))
             lo = first + P * b
-            sums = bank("%s%d" % ("up" if k < 2 else "turn0_", b), [P, R])
+            at = PIECE * (k % 2) + P * b
+            sums = bank("%s%d" % ("up" if k < 2 else "even", b), [P, R])
             for a in range(2):
                 nc.tensor.matmul_mx(
                     out=sums[:],
                     lhsT=parted[part][:, a, 2 * lo : 2 * (lo + P)].bitcast(FP4X4),
-                    lhsT_scale=pick_s[k // 2][a][:, CHUNK * (k % 2) + P * b : CHUNK * (k % 2) + P * (b + 1)],
+                    lhsT_scale=pick_s[k // 2][a][:, at : at + P],
                     rhs=wu_w[:, a, :].bitcast(FP8X4),
-                    rhs_scale=w_s[:, a, :],
+                    rhs_scale=wu_s[:, a, :],
                     start=(a == 0),
                     stop=(a == 1),
                 )
-            pos = keep.tile([P, PACK, P], F32, name="pos%d_%d" % (k, b), tag="pos%d_%d" % (k % 2, b), align_bytes=64)
             nc.scalar.activation(pos[:], sums[:].rearrange("p (m t) -> p t m", t=PACK), ACT.Relu)
             return pos
 
-        def turn(b, pos, turned):
-            sq = keep.tile([P, PACK, P], F32, name="sq%d" % b, tag="sq%d" % b, align_bytes=64)
+        def block(name, tag):
+            return fresh(name, [P, PACK, P], F32, tag)
+
+        def turn_banks(kind):
+            return [bank("%s%d" % (kind, b), [P, 2, PIECE]) for b in range(2)]
+
+        def turn(b, pos, turned, sq):
             nc.scalar.activation(sq[:], pos[:], ACT.Square)
             for t in range(PACK):
                 nc.tensor.transpose(turned[t // 2][:, t % 2, P * b : P * (b + 1)], sq[:, t, :], ident[:])
 
-        def smooth(k, turned):
-            rows = keep.tile([P, PACK, CHUNK], BF16, name="rows%d" % k, tag="rows%d" % k, align_bytes=64)
+        def smooth(turned, rows):
             for t in range(PACK):
                 nc.scalar.activation(rows[:, t, :], turned[t // 2][:, t % 2, :], ACT.Copy, scale=sm_t[:, t : t + 1])
             return rows
 
-        def weave(rows, woven):
+        def quantise(k, rows, woven, codes):
             nc.scalar.copy(
-                woven[:].rearrange("p (c i) t -> p c t i", i=4), rows[:].rearrange("p t (c i) -> p c t i", i=4)
+                woven.rearrange("p (c i) t -> p c t i", i=4), rows.rearrange("p t (c i) -> p c t i", i=4)
             )
-            return woven
-
-        def quantise(woven, codes, scales):
-            nc.vector.quantize_mx(
-                out=codes[:].bitcast(FP8X4), scales=scales[:], in_=woven[:].rearrange("p c t -> p (c t)")
-            )
+            scales = fresh("h_scales%d" % k, [P, PIECE], U8)
+            nc.vector.quantize_mx(out=codes.bitcast(FP8X4), scales=scales[:], in_=woven.rearrange("p c t -> p (c t)"))
             return codes, scales
 
-        def h_tiles(k):
-            return (
-                keep.tile([P, CHUNK], I32, name="h_codes%d" % k, tag="h_codes%d" % k, align_bytes=64),
-                keep.tile([P, CHUNK], U8, name="h_scales%d" % k, align_bytes=64),
-            )
-
-        def woven_tile(k, tag):
-            return keep.tile([P, CHUNK, PACK], BF16, name="woven%d" % k, tag=tag, align_bytes=64)
-
-        def down(h, kind):
-            banks = [bank("%s%d" % (kind, b), [P, 2, CHUNK]) for b in range(2)]
+        def down(h, low, high):
+            banks = [bank(tag, [P, 2, PIECE]) for tag in (low, high)]
             for t in range(PACK):
                 nc.tensor.matmul_mx(
                     out=banks[t // 2][:, t % 2, :],
                     lhsT=wd_p[:, t, :].bitcast(FP8X4),
                     lhsT_scale=wds_p[:, t, :],
-                    rhs=h[0][:].bitcast(FP8X4),
+                    rhs=h[0].bitcast(FP8X4),
                     rhs_scale=h[1][:],
                     start=True,
                     stop=True,
                 )
             return banks
 
-        def drain(name, tag, acc):
-            held = keep.tile([P, 2, CHUNK], F32, name=name, tag=tag, align_bytes=64)
-            nc.scalar.copy(held[:], acc[:])
+        def drained(held, acc):
+            nc.scalar.copy(held, acc)
             return held
-
-        def drain_plane(name, tag, acc, plane):
-            held = keep.tile([P, CHUNK], F32, name=name, tag=tag, align_bytes=64)
-            nc.scalar.copy(held[:], acc[:, plane, :])
-            return held[:]
 
         def put(t, start, count, y):
             nc.vector.tensor_tensor(
                 page[t][:].indirect(entries(start, count)), y, gate[t][:, start : start + count], MULT
             )
 
-        def y_tile(name, tag, planes, count):
-            return keep.tile([P, planes, count], F32, name=name, tag=tag, align_bytes=64)
+        def rows_tile(k):
+            return fresh("rows%d" % k, [P, PACK, PIECE], BF16)[:]
 
-        def later_page(t):
-            at_page = at_woven + 4 * T * (t - 1)
-            return clear_page(laid.tile([P, T], F32, name="page%d" % t, align_bytes=64, offset=at_page), nc.gpsimd)
+        def woven_tile(k, tag):
+            return fresh("woven%d" % k, [P, PIECE, PACK], BF16, tag)[:]
 
-        turned = [turn_banks(k) for k in range(2)]
+        def codes_tile(k):
+            return fresh("h_codes%d" % k, [P, PIECE], I32)[:]
+
+        def y_plane(name, tag=None):
+            return fresh(name, [P, PIECE], F32, tag)[:]
+
+        turned = [turn_banks("even"), turn_banks("odd")]
         for b in range(2):
-            turn(b, rectify(0, b), turned[0])
-        pos = rectify(1, 0)
-        rows = smooth(0, turned[0])
-        turn(0, pos, turned[1])
-        woven = laid.tile([P, T, PACK], BF16, name="woven0", align_bytes=64, offset=at_woven)[:, 0:CHUNK, :]
-        h = quantise(weave(rows, woven), *h_tiles(0))
+            turn(b, rectify(0, b, block("pos0_%d" % b, "pos%d" % b)), turned[0], block("sq0_%d" % b, "sq%d" % b))
+        pos = rectify(1, 0, block("pos1_0", "pos2"))
+        rows = smooth(turned[0], rows_tile(0))
+        turn(0, pos, turned[1], block("sq1_0", "sq0"))
+        woven = placed("woven0", [P, 3 * J, PACK], BF16, AT_PAGES)[:, 0:PIECE, :]
+        h = quantise(0, rows, woven, placed("h_codes0", [P, PIECE], I32, AT_G1)[:])
+        gate.append(gates(2, gate_tile(2)))
+        page.extend(cleared(placed("page%d" % t, [P, T], F32, AT_PAGES + 8 * (t - 1))) for t in (1, 2, 3))
+        wd_p = fresh("wd_p", [P, PACK, P], I32)
         nc.scalar.copy(
             wd_p[:].bitcast(U32).rearrange("p t (c i) -> p c t i", i=4),
-            wd_w[:].bitcast(U32).rearrange("p (c i t) -> p c t i", i=4, t=PACK),
+            wd_w.bitcast(U32).rearrange("p (c i t) -> p c t i", i=4, t=PACK),
         )
-        turn(1, rectify(1, 1), turned[1])
-        gate.append(gates(3, keep.tile([P, J], F32, name="gate3", tag="rows0", align_bytes=64)))
-        page.extend(later_page(t) for t in (1, 2))
-        banks = down(h, "up")
-        pos = [rectify(2, 0)]
-        y = drain("y0a", "y0a", banks[0])
+        late = rectify(1, 1, placed("pos1_1", [P, PACK, P], F32, AT_WD + 4))
+        banks = down(h, "up0", "up1")
         for t in range(2):
-            put(t, 0, CHUNK, y[:, t, :])
-        rows = smooth(1, turned[1])
-        pos.append(rectify(2, 1))
-        h = quantise(weave(rows, woven_tile(1, "woven1")), *h_tiles(1))
-
-        turned.append(turn_banks(2))
-        for b in range(2):
-            turn(b, pos[b], turned[2])
-        y_high = y_tile("y_high", "pos0_1", 2, J)
-        nc.scalar.copy(y_high[:, :, 0:CHUNK], banks[1][:])
-        put(2, 0, CHUNK, y_high[:, 0, 0:CHUNK])
-        rows = smooth(2, turned[2])
-        banks = down(h, "spread")
-        put(0, CHUNK, CHUNK, drain_plane("y1_0", "y1_0", banks[0], 0))
-        h = quantise(weave(rows, woven_tile(2, "page3")), *h_tiles(2))
-        page.append(clear_page(keep.tile([P, T], F32, name="page3", tag="page3", align_bytes=64), nc.gpsimd))
-        put(1, CHUNK, CHUNK, drain_plane("y1_1", "rows2", banks[0], 1))
-        nc.scalar.copy(y_high[:, :, CHUNK:HALF], banks[1][:])
-        put(2, CHUNK, CHUNK, y_high[:, 0, CHUNK:HALF])
-        put(3, 0, CHUNK, y_high[:, 1, 0:CHUNK])
-
-        banks = down(h, "up")
-        pos = [rectify(3, b) for b in range(2)]
-        turned.append(turn_banks(3))
-        for b in range(2):
-            turn(b, pos[b], turned[3])
-        put(0, HALF, CHUNK, drain_plane("y2_0", "pos1_1", banks[0], 0))
-        h = quantise(weave(smooth(3, turned[3]), woven_tile(3, "woven3")), *h_tiles(3))
-        put(1, HALF, CHUNK, drain_plane("y2_1", "rows3", banks[0], 1))
-        nc.scalar.copy(y_high[:, :, HALF : J - CHUNK], banks[1][:])
-
-        banks = down(h, "turn0_")
+            put(t, 0, PIECE, drained(y_plane("y0_%d" % t), banks[0][:, t, :]))
+        gate.append(gates(3, gate_tile(3)))
+        turn(1, late, turned[1], block("sq1_1", "sq1"))
+        pos = [rectify(2, 0, placed("pos2_0", [P, PACK, P], F32, AT_WD + 2))]
+        rows = smooth(turned[1], placed("rows1", [P, 6 * PACK, PIECE], BF16, AT_ROWS1)[:, 0:PACK, :])
+        pos.append(rectify(2, 1, placed("pos2_1", [P, PACK, P], F32, AT_WD + 6)))
+        h = quantise(1, rows, woven_tile(1, "woven1"), codes_tile(1))
+        y_high = placed("y_high", [P, 2, J], F32, AT_ROWS1)
+        drained(y_high[:, :, 0:PIECE], banks[1][:])
         for t in range(2):
-            put(t, J - CHUNK, CHUNK, drain_plane("y3_%d" % t, "y3_%d" % t, banks[0], t))
-        nc.scalar.copy(y_high[:, :, J - CHUNK : J], banks[1][:])
+            put(2 + t, 0, PIECE, y_high[:, t, 0:PIECE])
+
+        turned.append(turn_banks("spread"))
+        turn(0, pos[0], turned[2], placed("sq2_0", [P, PACK, P], F32, AT_ROWS1 + 8))
+        turn(1, pos[1], turned[2], block("sq2_1", "sq1"))
+        rows = smooth(turned[2], rows_tile(2))
+        banks = down(h, "spread0", "spread1")
+        put(0, PIECE, PIECE, drained(y_plane("y1_0"), banks[0][:, 0, :]))
+        h = quantise(2, rows, woven_tile(2, "woven2"), codes_tile(2))
+        put(1, PIECE, PIECE, drained(y_plane("y1_1", "rows2"), banks[0][:, 1, :]))
+        put(2, PIECE, PIECE, drained(y_high[:, :, PIECE:HALF], banks[1][:])[:, 0, :])
+
+        banks = down(h, "up0", "up1")
+        pos = [rectify(3, b, block("pos3_%d" % b, "pos%d" % (2 + b))) for b in range(2)]
+        turned.append(turn_banks("odd"))
+        for b in range(2):
+            turn(b, pos[b], turned[3], block("sq3_%d" % b, "sq%d" % b))
+        put(0, HALF, PIECE, drained(y_plane("y2_0", "pos3"), banks[0][:, 0, :]))
+        h = quantise(3, smooth(turned[3], rows_tile(3)), woven_tile(3, "woven3"), codes_tile(3))
+        put(1, HALF, PIECE, drained(y_plane("y2_1", "rows3"), banks[0][:, 1, :]))
+        drained(y_high[:, :, HALF : J - PIECE], banks[1][:])
+
+        banks = down(h, "even0", "even1")
+        for t in range(2):
+            put(t, J - PIECE, PIECE, drained(y_plane("y3_%d" % t), banks[0][:, t, :]))
+        drained(y_high[:, :, J - PIECE : J], banks[1][:])
         put(2, HALF, HALF, y_high[:, 0, HALF:J])
-        put(3, CHUNK, J - CHUNK, y_high[:, 1, CHUNK:J])
+        put(3, PIECE, J - PIECE, y_high[:, 1, PIECE:J])
 
         out_rows = out_0.rearrange("(p t) c -> t p c", t=PACK)
         for t in range(PACK):
@@ -310,9 +307,9 @@ def tile_list_modp_relu2_gateP_kernel(
         o_codes = keep.tile([P, T], I32, name="o_codes", align_bytes=64)
         words_out = out_1[0].rearrange("p c b -> p (c b)").bitcast(I32)
         split = T // 2 + P
-        own = HALF + CHUNK
+        own = HALF + PIECE
         spans = [(0, own), (own, split - own), (split, HALF - P), (T - HALF, HALF)]
-        chunks = [(c, HALF) for c in range(0, T // 2, HALF)] + [(c, CHUNK) for c in range(T // 2, T, CHUNK)]
+        chunks = [(c, HALF) for c in range(0, T // 2, HALF)] + [(c, PIECE) for c in range(T // 2, T, PIECE)]
         woven_o = [keep.tile([P, n, 2], U32, name="woven_o%d" % c, align_bytes=64) for c, n in chunks]
         pairs = [keep.tile([P, 2, n, 2], BF16, name="pairs%d" % c, align_bytes=64) for c, n in spans]
         for t in range(3):

@@ -23,6 +23,7 @@ QUADS = 4
 HALF = 512
 PIECE = 256
 KIB = 1024
+EARLY = 512
 
 
 def tile_list_modp_relu2_gateP_kernel(
@@ -38,7 +39,7 @@ def tile_list_modp_relu2_gateP_kernel(
             return keep.tile(shape, dtype, name=name, tag=tag or name, align_bytes=64)
 
         def placed(name, shape, dtype, kib):
-            return laid.tile(shape, dtype, name=name, align_bytes=64, offset=kib * KIB)
+            return laid.tile(shape, dtype, name=name, align_bytes=64, offset=int(kib * KIB))
 
         def bank(tag, shape):
             return psum.tile(shape, F32, name=tag, tag=tag)
@@ -46,26 +47,27 @@ def tile_list_modp_relu2_gateP_kernel(
         def entries(start, count):
             return offsets[:, start // 16 : (start + count) // 16]
 
-        AT_G1 = 2
-        AT_BOTH0 = 10
-        AT_BOTH2 = 12
-        AT_G2 = 14
-        AT_WD = 22
-        AT_G3 = 30
-        AT_PAGES = 38
-        AT_ROWS1 = 62
+        AT_G0 = 0
+        AT_MOVED = 8
+        AT_G1 = 9
+        AT_WD_S = 17
+        AT_G2 = 18
+        AT_WD = 26
+        AT_ROWS1 = 34
+        AT_G3 = 46
+        AT_PAGES = 54
+        AT_BOTH = 70
+        AT_ROWS2 = 74
 
         offsets = keep.tile([P, J // 16], U16, name="offsets")
-        tab_s = placed("tab_s", [P, 10 * KIB], U8, 0)[:, 0:T]
+        tab_s = fresh("tab_s", [P, T], U8)[:]
         tab_w = fresh("tab_w", [P, T], I32)
         wu_s = fresh("wu_s", [P, 2, R], U8)
         wu_w = fresh("wu_w", [P, 2, R], I32)
-        sm_t = fresh("sm_t", [P, PACK], F32)
-        wgo_c = fresh("wgo_c", [P, 2 * PACK], F32)
+        wgo_c = placed("wgo_c", [P, AT_PAGES * KIB // 4], F32, AT_G0)[:, 0 : 2 * PACK]
         ident = fresh("ident", [P, P], F32)
 
-        make_identity(nc, ident[:])
-        nc.vector.memset(wu_s[:].rearrange("p a r -> p (a r)").bitcast(I32), 0)
+        nc.gpsimd.memset(wu_s[:].rearrange("p a r -> p (a r)").bitcast(I32), 0)
 
         def load_wu_scales(queue, quads):
             for q in quads:
@@ -74,18 +76,18 @@ def tile_list_modp_relu2_gateP_kernel(
                     wu_scales[:, 4 * q : 4 * q + 4, :].rearrange("a s r -> s a r").bitcast(I32),
                 )
 
-        load_wu_scales(nc.gpsimd, (0, 1))
-        nc.gpsimd.dma_start(sm_t[:], sm.rearrange("(p t) -> p t", t=PACK))
+        load_wu_scales(nc.gpsimd, (0,))
+        make_identity(nc, ident[:])
 
         nc.sync.dma_start(offsets[:], offs)
         s_rows = tab_scales.rearrange("a q c -> (a q) c").bitcast(I32)
-        nc.scalar.dma_start(tab_s[96:128, :].bitcast(I32), s_rows[12:16, :].unsqueeze(0).to_broadcast([8, 4, T // 4]))
-        for first, rows, source in ((0, 32, 0), (56, 32, 0), (32, 16, 4), (48, 8, 20), (88, 8, 4)):
+        nc.scalar.dma_start(tab_s[88:128, :].bitcast(I32), s_rows[12:16, :].unsqueeze(0).to_broadcast([10, 4, T // 4]))
+        for first, rows, source in ((0, 32, 0), (56, 32, 0), (32, 16, 4), (48, 8, 20)):
             nc.sync.dma_start(tab_s[first : first + rows, :].bitcast(I32), s_rows[source : source + rows, :])
+        nc.sync.dma_start(wgo_c, wgo[0].rearrange("(p i) -> p i", p=P))
         nc.sync.dma_start(tab_w[:], tab_words[0].rearrange("p c b -> p (c b)").bitcast(I32))
         nc.sync.dma_start(wu_w[:], wu_words.rearrange("a p r b -> p a (r b)").bitcast(I32))
-        load_wu_scales(nc.sync, (2, 3))
-        nc.sync.dma_start(wgo_c[:], wgo[0].rearrange("(p i) -> p i", p=P))
+        load_wu_scales(nc.sync, (1, 2, 3))
 
         g_src = gT.rearrange("(p t) c -> t p c", t=PACK)
 
@@ -93,7 +95,6 @@ def tile_list_modp_relu2_gateP_kernel(
             nc.sync.dma_start(rows[:], g_src[t])
             return rows
 
-        g_rows = [load_gates(0, fresh("g_rows0", [P, T], F32))]
         wgo_t = fresh("wgo_t", [P, J], F32)
         for b in range(2):
             spread = bank("spread%d" % b, [P, PACK, P])
@@ -104,22 +105,25 @@ def tile_list_modp_relu2_gateP_kernel(
                 wgo_t[:].rearrange("c (p b i) -> c b p i", b=2, i=PACK)[:, b], spread[:].rearrange("c i p -> c p i")
             )
 
-        moved_s = fresh("moved_s", [P, J], U8)
+        def pick_scales(start, count):
+            picked = fresh("picked_s%d" % start, [P, count], U8)
+            nc.vector.tensor_copy(picked[:], tab_s.indirect(entries(start, count)))
+            return [picked[:]]
 
-        def pick_scales(start):
-            picked = fresh("picked_s%d" % start, [P, HALF], U8)
-            nc.vector.tensor_copy(picked[:], tab_s.indirect(entries(start, HALF)))
-            return [picked[:], moved_s[:, start : start + HALF]]
-
-        def move_scales(queue, picked, moved):
+        def move_scales(planes, moved):
             for first, source in ((0, 16), (64, 52)):
-                queue.dma_start(moved[first : first + 64, :].bitcast(I32), picked[source : source + 64, :].bitcast(I32))
+                nc.sync.dma_start(
+                    moved[first : first + 64, :].bitcast(I32), planes[0][source : source + 64, :].bitcast(I32)
+                )
+            planes.append(moved[:])
 
-        pick_s = [pick_scales(0)]
-        move_scales(nc.scalar, *pick_s[0])
-        pick_s.append(pick_scales(HALF))
-        g_rows.append(load_gates(1, placed("g_rows1", [P, T], F32, AT_G1)))
-        move_scales(nc.sync, *pick_s[1])
+        pick_s = [pick_scales(0, PIECE)]
+        move_scales(pick_s[0], fresh("moved0", [P, PIECE], U8))
+        g_rows = [load_gates(0, placed("g_rows0", [P, T], F32, AT_G0))]
+        sm_t = placed("sm_t", [P, PACK], F32, AT_MOVED + 0.75)
+        nc.sync.dma_start(sm_t[:], sm.rearrange("(p t) -> p t", t=PACK))
+        pick_s.append(pick_scales(PIECE, J - PIECE))
+        move_scales(pick_s[1], placed("moved1", [P, J - PIECE], U8, AT_MOVED))
 
         def pick_words(start, both):
             nc.vector.tensor_copy(both.bitcast(U32), tab_w[:].bitcast(U32).indirect(entries(start, both.shape[1])))
@@ -131,22 +135,24 @@ def tile_list_modp_relu2_gateP_kernel(
             return parted
 
         both = [
-            pick_words(0, placed("both0", [P, 2 * PIECE], I32, AT_BOTH0)[:, 0:PIECE]),
-            pick_words(PIECE, fresh("both1", [P, PIECE], I32)[:]),
+            pick_words(0, placed("both0", [P, J], I32, AT_BOTH)[:, 0:P]),
+            pick_words(P, fresh("both1", [P, P], I32)[:]),
         ]
-        parted = [part_words(0, both[0])]
-        both.append(pick_words(HALF, placed("both2", [P, (AT_PAGES - AT_BOTH2) * KIB // 4], I32, AT_BOTH2)[:, 0:HALF]))
-        parted.extend(part_words(start, both[i]) for i, start in ((1, PIECE), (2, HALF)))
-        wd_s = placed("wd_s", [P, N], U8, AT_BOTH0 + 1)
-        nc.gpsimd.memset(wd_s[:].bitcast(I32), 0)
-        for q in range(QUADS):
-            (nc.gpsimd if q < 2 else nc.sync).dma_start(
-                wd_s[32 * q : 32 * q + 4, :].bitcast(I32), wd_scales[0, 4 * q : 4 * q + 4, :].bitcast(I32)
-            )
+        parted = [part_words(P * i, both[i]) for i in range(2)]
+        both = [
+            pick_words(PIECE, placed("both2", [P, PIECE], I32, AT_BOTH + 1)[:]),
+            pick_words(HALF, placed("both3", [P, HALF], I32, AT_BOTH + 2)[:]),
+        ]
+        parted.extend(part_words(PIECE * (i + 1), both[i]) for i in range(2))
+        g_rows.append(load_gates(1, placed("g_rows1", [P, T], F32, AT_G1)))
         g_rows.append(load_gates(2, placed("g_rows2", [P, T], F32, AT_G2)))
-        wd_w = placed("wd_w", [P, 4 * N], I32, AT_WD)[:, 0:N]
-        nc.sync.dma_start(wd_w, wd_words[0].rearrange("p n b -> p (n b)").bitcast(I32))
+        wd_s = placed("wd_s", [P, N], U8, AT_WD_S)
+        for q in range(QUADS):
+            rows = wd_scales[0, 4 * q : 4 * q + 4, :].bitcast(I32)
+            nc.sync.dma_start(wd_s[32 * q : 32 * (q + 1), :].bitcast(I32), rows.unsqueeze(0).to_broadcast([8, 4, N // 4]))
         g_rows.append(load_gates(3, placed("g_rows3", [P, T], F32, AT_G3)))
+        wd_w = placed("wd_w", [P, (AT_G3 - AT_WD) * KIB // 4], I32, AT_WD)[:, 0:N]
+        nc.sync.dma_start(wd_w, wd_words[0].rearrange("p n b -> p (n b)").bitcast(I32))
 
         def gates(t, gate):
             nc.vector.tensor_tensor(gate[:], g_rows[t][:].indirect(offsets[:]), wgo_t[:], MULT)
@@ -160,21 +166,22 @@ def tile_list_modp_relu2_gateP_kernel(
             return fresh("gate%d" % t, [P, J], F32)
 
         gate = [gates(0, gate_tile(0))]
-        page = [cleared(fresh("page0", [P, T], F32, "g_rows0"))]
+        page = [cleared(placed("page0", [P, T], F32, AT_G0))]
         gate.append(gates(1, gate_tile(1)))
+        page.append(cleared(placed("page1", [P, T], F32, AT_G1)))
+        gate.append(gates(2, gate_tile(2)))
         wds_p = fresh("wds_p", [P, PACK, P], U8)
         nc.vector.tensor_copy(wds_p[:], wd_s[:].rearrange("p (m t) -> p t m", t=PACK))
 
         def rectify(k, b, pos):
-            part, first = (k, 0) if k < 2 else (2, PIECE * (k - 2))
-            lo = first + P * b
-            at = PIECE * (k % 2) + P * b
+            part, lo = (b, 0) if k == 0 else (min(k, 2) + 1, PIECE * max(k - 2, 0) + P * b)
+            at = PIECE * max(k - 1, 0) + P * b
             sums = bank("%s%d" % ("up" if k < 2 else "even", b), [P, R])
             for a in range(2):
                 nc.tensor.matmul_mx(
                     out=sums[:],
                     lhsT=parted[part][:, a, 2 * lo : 2 * (lo + P)].bitcast(FP4X4),
-                    lhsT_scale=pick_s[k // 2][a][:, at : at + P],
+                    lhsT_scale=pick_s[min(k, 1)][a][:, at : at + P],
                     rhs=wu_w[:, a, :].bitcast(FP8X4),
                     rhs_scale=wu_s[:, a, :],
                     start=(a == 0),
@@ -248,56 +255,62 @@ def tile_list_modp_relu2_gateP_kernel(
         pos = rectify(1, 0, block("pos1_0", "pos2"))
         rows = smooth(turned[0], rows_tile(0))
         turn(0, pos, turned[1], block("sq1_0", "sq0"))
-        woven = placed("woven0", [P, 3 * J, PACK], BF16, AT_PAGES)[:, 0:PIECE, :]
-        h = quantise(0, rows, woven, placed("h_codes0", [P, PIECE], I32, AT_G1)[:])
-        gate.append(gates(2, gate_tile(2)))
-        page.extend(cleared(placed("page%d" % t, [P, T], F32, AT_PAGES + 8 * (t - 1))) for t in (1, 2, 3))
+        woven = placed("woven0", [P, T, PACK], BF16, AT_PAGES)[:, 0:PIECE, :]
+        h = quantise(0, rows, woven, placed("h_codes0", [P, PIECE], I32, AT_G2)[:])
+        gate.append(gates(3, gate_tile(3)))
+        page.extend(cleared(placed("page%d" % t, [P, T], F32, AT_PAGES + 8 * (t - 2))) for t in (2, 3))
+        turn(1, rectify(1, 1, block("pos1_1", "pos3")), turned[1], block("sq1_1", "sq1"))
+        pos = [rectify(2, 0, block("pos2_0", "pos0"))]
         wd_p = fresh("wd_p", [P, PACK, P], I32)
         nc.scalar.copy(
             wd_p[:].bitcast(U32).rearrange("p t (c i) -> p c t i", i=4),
             wd_w.bitcast(U32).rearrange("p (c i t) -> p c t i", i=4, t=PACK),
         )
-        late = rectify(1, 1, placed("pos1_1", [P, PACK, P], F32, AT_WD + 4))
         banks = down(h, "up0", "up1")
         for t in range(2):
             put(t, 0, PIECE, drained(y_plane("y0_%d" % t), banks[0][:, t, :]))
-        gate.append(gates(3, gate_tile(3)))
-        turn(1, late, turned[1], block("sq1_1", "sq1"))
-        pos = [rectify(2, 0, placed("pos2_0", [P, PACK, P], F32, AT_WD + 2))]
-        rows = smooth(turned[1], placed("rows1", [P, 6 * PACK, PIECE], BF16, AT_ROWS1)[:, 0:PACK, :])
-        pos.append(rectify(2, 1, placed("pos2_1", [P, PACK, P], F32, AT_WD + 6)))
+        rows = smooth(turned[1], placed("rows1", [P, 4 * PACK, PIECE], BF16, AT_ROWS1)[:, 0:PACK, :])
+        pos.append(rectify(2, 1, placed("pos2_1", [P, PACK, P], F32, AT_WD + 2)))
         h = quantise(1, rows, woven_tile(1, "woven1"), codes_tile(1))
-        y_high = placed("y_high", [P, 2, J], F32, AT_ROWS1)
-        drained(y_high[:, :, 0:PIECE], banks[1][:])
-        for t in range(2):
-            put(2 + t, 0, PIECE, y_high[:, t, 0:PIECE])
+        y_two = placed("y_two", [P, J], F32, AT_ROWS1)
+        put(2, 0, PIECE, drained(y_two[:, 0:PIECE], banks[1][:, 0, :]))
+        high = [banks[1]]
 
         turned.append(turn_banks("spread"))
-        turn(0, pos[0], turned[2], placed("sq2_0", [P, PACK, P], F32, AT_ROWS1 + 8))
+        turn(0, pos[0], turned[2], placed("sq2_0", [P, PACK, P], F32, AT_ROWS1 + 4))
         turn(1, pos[1], turned[2], block("sq2_1", "sq1"))
-        rows = smooth(turned[2], rows_tile(2))
-        banks = down(h, "spread0", "spread1")
-        put(0, PIECE, PIECE, drained(y_plane("y1_0"), banks[0][:, 0, :]))
+        banks = down(h, "odd0", "odd1")
+        for t in range(2):
+            put(t, PIECE, PIECE, drained(y_plane("y1_%d" % t), banks[0][:, t, :]))
+        put(2, PIECE, PIECE, drained(y_two[:, PIECE:HALF], banks[1][:, 0, :]))
+        high.append(banks[1])
+        rows = smooth(turned[2], placed("rows2", [P, 2 * PACK, PIECE], BF16, AT_ROWS2)[:, 0:PACK, :])
         h = quantise(2, rows, woven_tile(2, "woven2"), codes_tile(2))
-        put(1, PIECE, PIECE, drained(y_plane("y1_1", "rows2"), banks[0][:, 1, :]))
-        put(2, PIECE, PIECE, drained(y_high[:, :, PIECE:HALF], banks[1][:])[:, 0, :])
+        y_three = placed("y_three", [P, J], F32, AT_ROWS2)
+        for k in range(2):
+            drained(y_three[:, PIECE * k : PIECE * (k + 1)], high[k][:, 1, :])
+        put(3, 0, EARLY, y_three[:, 0:EARLY])
 
-        banks = down(h, "up0", "up1")
-        pos = [rectify(3, b, block("pos3_%d" % b, "pos%d" % (2 + b))) for b in range(2)]
-        turned.append(turn_banks("odd"))
+        pos = [rectify(3, 0, block("pos3_0", "pos0")), rectify(3, 1, placed("pos3_1", [P, PACK, P], F32, AT_WD + 2))]
+        turned.append(turn_banks("spread"))
         for b in range(2):
             turn(b, pos[b], turned[3], block("sq3_%d" % b, "sq%d" % b))
-        put(0, HALF, PIECE, drained(y_plane("y2_0", "pos3"), banks[0][:, 0, :]))
-        h = quantise(3, smooth(turned[3], rows_tile(3)), woven_tile(3, "woven3"), codes_tile(3))
+        rows = smooth(turned[3], rows_tile(3))
+        banks = down(h, "spread0", "spread1")
+        put(0, HALF, PIECE, drained(y_plane("y2_0"), banks[0][:, 0, :]))
+        h = quantise(3, rows, woven_tile(3, "woven3"), codes_tile(3))
         put(1, HALF, PIECE, drained(y_plane("y2_1", "rows3"), banks[0][:, 1, :]))
-        drained(y_high[:, :, HALF : J - PIECE], banks[1][:])
+        high = [banks[1]]
 
         banks = down(h, "even0", "even1")
         for t in range(2):
             put(t, J - PIECE, PIECE, drained(y_plane("y3_%d" % t), banks[0][:, t, :]))
-        drained(y_high[:, :, J - PIECE : J], banks[1][:])
-        put(2, HALF, HALF, y_high[:, 0, HALF:J])
-        put(3, PIECE, J - PIECE, y_high[:, 1, PIECE:J])
+        high.append(banks[1])
+        for plane, held in enumerate((y_two, y_three)):
+            for k in range(2):
+                drained(held[:, HALF + PIECE * k : HALF + PIECE * (k + 1)], high[k][:, plane, :])
+        put(2, HALF, HALF, y_two[:, HALF:J])
+        put(3, EARLY, J - EARLY, y_three[:, EARLY:J])
 
         out_rows = out_0.rearrange("(p t) c -> t p c", t=PACK)
         for t in range(PACK):

from contextlib import ExitStack

import concourse.mybir as mybir
from concourse.masks import make_identity

K, R, N, T, J = 1024, 512, 512, 2048, 1024
FLOPS = 2 * K * R * J + 2 * R * N * J

F32 = mybir.dt.float32
BF16 = mybir.dt.bfloat16
I32 = mybir.dt.int32
U32 = mybir.dt.uint32
U16 = mybir.dt.uint16
U8 = mybir.dt.uint8
FP8X4 = mybir.dt.float8_e4m3fn_x4
FP4X4 = mybir.dt.float4_e2m1fn_x4
MULT = mybir.AluOpType.mult
ACT = mybir.ActivationFunctionType

P = 128
PACK = 4
QUADS = 4
HALF = 512
PIECE = 256
KIB = 1024
EARLY = 512


def tile_list_modp_relu2_gateP_kernel(
    tc, tab_words, tab_scales, wu_words, wu_scales, sm, wd_words, wd_scales, gT, wgo, offs, out_0, out_1, out_2
):
    nc = tc.nc
    with ExitStack() as ctx:
        keep = ctx.enter_context(tc.tile_pool(name="keep", bufs=1))
        laid = ctx.enter_context(tc.tile_pool(name="laid", bufs=1))
        psum = ctx.enter_context(tc.psum_pool(name="psum", bufs=1))

        def fresh(name, shape, dtype, tag=None):
            return keep.tile(shape, dtype, name=name, tag=tag or name, align_bytes=64)

        def placed(name, shape, dtype, kib):
            return laid.tile(shape, dtype, name=name, align_bytes=64, offset=int(kib * KIB))

        def bank(tag, shape):
            return psum.tile(shape, F32, name=tag, tag=tag)

        def entries(start, count):
            return offsets[:, start // 16 : (start + count) // 16]

        AT_G0 = 0
        AT_MOVED = 8
        AT_G1 = 9
        AT_WD_S = 17
        AT_G2 = 18
        AT_WD = 26
        AT_ROWS1 = 34
        AT_G3 = 46
        AT_PAGES = 54
        AT_BOTH = 70
        AT_ROWS2 = 74

        offsets = keep.tile([P, J // 16], U16, name="offsets")
        tab_s = fresh("tab_s", [P, T], U8)[:]
        tab_w = fresh("tab_w", [P, T], I32)
        wu_s = fresh("wu_s", [P, 2, R], U8)
        wu_w = fresh("wu_w", [P, 2, R], I32)
        wgo_c = placed("wgo_c", [P, AT_PAGES * KIB // 4], F32, AT_G0)[:, 0 : 2 * PACK]
        ident = fresh("ident", [P, P], F32)

        nc.gpsimd.memset(wu_s[:].rearrange("p a r -> p (a r)").bitcast(I32), 0)

        def load_wu_scales(queue, quads):
            for q in quads:
                queue.dma_start(
                    wu_s[32 * q : 32 * q + 4, :, :].bitcast(I32),
                    wu_scales[:, 4 * q : 4 * q + 4, :].rearrange("a s r -> s a r").bitcast(I32),
                )

        load_wu_scales(nc.gpsimd, (0,))
        make_identity(nc, ident[:])

        nc.sync.dma_start(offsets[:], offs)
        s_rows = tab_scales.rearrange("a q c -> (a q) c").bitcast(I32)
        nc.scalar.dma_start(tab_s[88:128, :].bitcast(I32), s_rows[12:16, :].unsqueeze(0).to_broadcast([10, 4, T // 4]))
        for first, rows, source in ((0, 32, 0), (56, 32, 0), (32, 16, 4), (48, 8, 20)):
            nc.sync.dma_start(tab_s[first : first + rows, :].bitcast(I32), s_rows[source : source + rows, :])
        nc.sync.dma_start(wgo_c, wgo[0].rearrange("(p i) -> p i", p=P))
        nc.sync.dma_start(tab_w[:], tab_words[0].rearrange("p c b -> p (c b)").bitcast(I32))
        nc.sync.dma_start(wu_w[:], wu_words.rearrange("a p r b -> p a (r b)").bitcast(I32))
        load_wu_scales(nc.sync, (1, 2, 3))

        g_src = gT.rearrange("(p t) c -> t p c", t=PACK)

        def load_gates(t, rows):
            nc.sync.dma_start(rows[:], g_src[t])
            return rows

        wgo_t = fresh("wgo_t", [P, J], F32)
        for b in range(2):
            spread = bank("spread%d" % b, [P, PACK, P])
            for i in range(PACK):
                column = wgo_c[:, PACK * b + i : PACK * b + i + 1]
                nc.tensor.transpose(spread[:, i, :], column.to_broadcast([P, P]), ident[:])
            nc.scalar.copy(
                wgo_t[:].rearrange("c (p b i) -> c b p i", b=2, i=PACK)[:, b], spread[:].rearrange("c i p -> c p i")
            )

        def pick_scales(start, count):
            picked = fresh("picked_s%d" % start, [P, count], U8)
            nc.vector.tensor_copy(picked[:], tab_s.indirect(entries(start, count)))
            return [picked[:]]

        def move_scales(planes, moved):
            for first, source in ((0, 16), (64, 52)):
                nc.sync.dma_start(
                    moved[first : first + 64, :].bitcast(I32), planes[0][source : source + 64, :].bitcast(I32)
                )
            planes.append(moved[:])

        pick_s = [pick_scales(0, PIECE)]
        move_scales(pick_s[0], fresh("moved0", [P, PIECE], U8))
        g_rows = [load_gates(0, placed("g_rows0", [P, T], F32, AT_G0))]
        sm_t = placed("sm_t", [P, PACK], F32, AT_MOVED + 0.75)
        nc.sync.dma_start(sm_t[:], sm.rearrange("(p t) -> p t", t=PACK))
        pick_s.append(pick_scales(PIECE, J - PIECE))
        move_scales(pick_s[1], placed("moved1", [P, J - PIECE], U8, AT_MOVED))

        def pick_words(start, both):
            nc.vector.tensor_copy(both.bitcast(U32), tab_w[:].bitcast(U32).indirect(entries(start, both.shape[1])))
            return both

        def part_words(start, both):
            parted = fresh("parted%d" % start, [P, 2, 2 * both.shape[1]], U8)
            nc.vector.tensor_copy(parted[:].bitcast(U16), both.bitcast(U16).rearrange("p (j d) -> p d j", d=2))
            return parted

        both = [
            pick_words(0, placed("both0", [P, J], I32, AT_BOTH)[:, 0:P]),
            pick_words(P, fresh("both1", [P, P], I32)[:]),
        ]
        parted = [part_words(P * i, both[i]) for i in range(2)]
        both = [
            pick_words(PIECE, placed("both2", [P, PIECE], I32, AT_BOTH + 1)[:]),
            pick_words(HALF, placed("both3", [P, HALF], I32, AT_BOTH + 2)[:]),
        ]
        parted.extend(part_words(PIECE * (i + 1), both[i]) for i in range(2))
        g_rows.append(load_gates(1, placed("g_rows1", [P, T], F32, AT_G1)))
        g_rows.append(load_gates(2, placed("g_rows2", [P, T], F32, AT_G2)))
        wd_s = placed("wd_s", [P, N], U8, AT_WD_S)
        for q in range(QUADS):
            rows = wd_scales[0, 4 * q : 4 * q + 4, :].bitcast(I32)
            nc.sync.dma_start(wd_s[32 * q : 32 * (q + 1), :].bitcast(I32), rows.unsqueeze(0).to_broadcast([8, 4, N // 4]))
        g_rows.append(load_gates(3, placed("g_rows3", [P, T], F32, AT_G3)))
        wd_w = placed("wd_w", [P, (AT_G3 - AT_WD) * KIB // 4], I32, AT_WD)[:, 0:N]
        nc.sync.dma_start(wd_w, wd_words[0].rearrange("p n b -> p (n b)").bitcast(I32))

        def gates(t, gate):
            nc.vector.tensor_tensor(gate[:], g_rows[t][:].indirect(offsets[:]), wgo_t[:], MULT)
            return gate

        def cleared(page):
            nc.gpsimd.memset(page[:].bitcast(I32), 0)
            return page

        def gate_tile(t):
            return fresh("gate%d" % t, [P, J], F32)

        gate = [gates(0, gate_tile(0))]
        page = [cleared(placed("page0", [P, T], F32, AT_G0))]
        gate.append(gates(1, gate_tile(1)))
        page.append(cleared(placed("page1", [P, T], F32, AT_G1)))
        gate.append(gates(2, gate_tile(2)))
        wds_p = fresh("wds_p", [P, PACK, P], U8)
        nc.vector.tensor_copy(wds_p[:], wd_s[:].rearrange("p (m t) -> p t m", t=PACK))

        def rectify(k, b, pos):
            part, lo = (b, 0) if k == 0 else (min(k, 2) + 1, PIECE * max(k - 2, 0) + P * b)
            at = PIECE * max(k - 1, 0) + P * b
            sums = bank("%s%d" % ("up" if k < 2 else "even", b), [P, R])
            for a in range(2):
                nc.tensor.matmul_mx(
                    out=sums[:],
                    lhsT=parted[part][:, a, 2 * lo : 2 * (lo + P)].bitcast(FP4X4),
                    lhsT_scale=pick_s[min(k, 1)][a][:, at : at + P],
                    rhs=wu_w[:, a, :].bitcast(FP8X4),
                    rhs_scale=wu_s[:, a, :],
                    start=(a == 0),
                    stop=(a == 1),
                )
            nc.scalar.activation(pos[:], sums[:].rearrange("p (m t) -> p t m", t=PACK), ACT.Relu)
            return pos

        def block(name, tag):
            return fresh(name, [P, PACK, P], F32, tag)

        def turn_banks(kind):
            return [bank("%s%d" % (kind, b), [P, 2, PIECE]) for b in range(2)]

        def turn(b, pos, turned, sq):
            nc.scalar.activation(sq[:], pos[:], ACT.Square)
            for t in range(PACK):
                nc.tensor.transpose(turned[t // 2][:, t % 2, P * b : P * (b + 1)], sq[:, t, :], ident[:])

        def smooth(turned, rows):
            for t in range(PACK):
                nc.scalar.activation(rows[:, t, :], turned[t // 2][:, t % 2, :], ACT.Copy, scale=sm_t[:, t : t + 1])
            return rows

        def quantise(k, rows, woven, codes):
            nc.scalar.copy(
                woven.rearrange("p (c i) t -> p c t i", i=4), rows.rearrange("p t (c i) -> p c t i", i=4)
            )
            scales = fresh("h_scales%d" % k, [P, PIECE], U8)
            nc.vector.quantize_mx(out=codes.bitcast(FP8X4), scales=scales[:], in_=woven.rearrange("p c t -> p (c t)"))
            return codes, scales

        def down(h, low, high):
            banks = [bank(tag, [P, 2, PIECE]) for tag in (low, high)]
            for t in range(PACK):
                nc.tensor.matmul_mx(
                    out=banks[t // 2][:, t % 2, :],
                    lhsT=wd_p[:, t, :].bitcast(FP8X4),
                    lhsT_scale=wds_p[:, t, :],
                    rhs=h[0].bitcast(FP8X4),
                    rhs_scale=h[1][:],
                    start=True,
                    stop=True,
                )
            return banks

        def drained(held, acc):
            nc.scalar.copy(held, acc)
            return held

        def put(t, start, count, y):
            nc.vector.tensor_tensor(
                page[t][:].indirect(entries(start, count)), y, gate[t][:, start : start + count], MULT
            )

        def rows_tile(k):
            return fresh("rows%d" % k, [P, PACK, PIECE], BF16)[:]

        def woven_tile(k, tag):
            return fresh("woven%d" % k, [P, PIECE, PACK], BF16, tag)[:]

        def codes_tile(k):
            return fresh("h_codes%d" % k, [P, PIECE], I32)[:]

        def y_plane(name, tag=None):
            return fresh(name, [P, PIECE], F32, tag)[:]

        turned = [turn_banks("even"), turn_banks("odd")]
        for b in range(2):
            turn(b, rectify(0, b, block("pos0_%d" % b, "pos%d" % b)), turned[0], block("sq0_%d" % b, "sq%d" % b))
        pos = rectify(1, 0, block("pos1_0", "pos2"))
        rows = smooth(turned[0], rows_tile(0))
        turn(0, pos, turned[1], block("sq1_0", "sq0"))
        woven = placed("woven0", [P, T, PACK], BF16, AT_PAGES)[:, 0:PIECE, :]
        h = quantise(0, rows, woven, placed("h_codes0", [P, PIECE], I32, AT_G2)[:])
        gate.append(gates(3, gate_tile(3)))
        page.extend(cleared(placed("page%d" % t, [P, T], F32, AT_PAGES + 8 * (t - 2))) for t in (2, 3))
        turn(1, rectify(1, 1, block("pos1_1", "pos3")), turned[1], block("sq1_1", "sq1"))
        pos = [rectify(2, 0, block("pos2_0", "pos0"))]
        wd_p = fresh("wd_p", [P, PACK, P], I32)
        nc.scalar.copy(
            wd_p[:].bitcast(U32).rearrange("p t (c i) -> p c t i", i=4),
            wd_w.bitcast(U32).rearrange("p (c i t) -> p c t i", i=4, t=PACK),
        )
        banks = down(h, "up0", "up1")
        for t in range(2):
            put(t, 0, PIECE, drained(y_plane("y0_%d" % t), banks[0][:, t, :]))
        rows = smooth(turned[1], placed("rows1", [P, 4 * PACK, PIECE], BF16, AT_ROWS1)[:, 0:PACK, :])
        pos.append(rectify(2, 1, placed("pos2_1", [P, PACK, P], F32, AT_WD + 2)))
        h = quantise(1, rows, woven_tile(1, "woven1"), codes_tile(1))
        y_two = placed("y_two", [P, J], F32, AT_ROWS1)
        put(2, 0, PIECE, drained(y_two[:, 0:PIECE], banks[1][:, 0, :]))
        high = [banks[1]]

        turned.append(turn_banks("spread"))
        turn(0, pos[0], turned[2], placed("sq2_0", [P, PACK, P], F32, AT_ROWS1 + 4))
        turn(1, pos[1], turned[2], block("sq2_1", "sq1"))
        banks = down(h, "odd0", "odd1")
        for t in range(2):
            put(t, PIECE, PIECE, drained(y_plane("y1_%d" % t), banks[0][:, t, :]))
        put(2, PIECE, PIECE, drained(y_two[:, PIECE:HALF], banks[1][:, 0, :]))
        high.append(banks[1])
        rows = smooth(turned[2], placed("rows2", [P, 2 * PACK, PIECE], BF16, AT_ROWS2)[:, 0:PACK, :])
        h = quantise(2, rows, woven_tile(2, "woven2"), codes_tile(2))
        y_three = placed("y_three", [P, J], F32, AT_ROWS2)
        for k in range(2):
            drained(y_three[:, PIECE * k : PIECE * (k + 1)], high[k][:, 1, :])
        put(3, 0, EARLY, y_three[:, 0:EARLY])

        pos = [rectify(3, 0, block("pos3_0", "pos0")), rectify(3, 1, placed("pos3_1", [P, PACK, P], F32, AT_WD + 2))]
        turned.append(turn_banks("spread"))
        for b in range(2):
            turn(b, pos[b], turned[3], block("sq3_%d" % b, "sq%d" % b))
        rows = smooth(turned[3], rows_tile(3))
        banks = down(h, "spread0", "spread1")
        put(0, HALF, PIECE, drained(y_plane("y2_0"), banks[0][:, 0, :]))
        h = quantise(3, rows, woven_tile(3, "woven3"), codes_tile(3))
        put(1, HALF, PIECE, drained(y_plane("y2_1", "rows3"), banks[0][:, 1, :]))
        high = [banks[1]]

        banks = down(h, "even0", "even1")
        for t in range(2):
            put(t, J - PIECE, PIECE, drained(y_plane("y3_%d" % t), banks[0][:, t, :]))
        high.append(banks[1])
        for plane, held in enumerate((y_two, y_three)):
            for k in range(2):
                drained(held[:, HALF + PIECE * k : HALF + PIECE * (k + 1)], high[k][:, plane, :])
        put(2, HALF, HALF, y_two[:, HALF:J])
        put(3, EARLY, J - EARLY, y_three[:, EARLY:J])

        out_rows = out_0.rearrange("(p t) c -> t p c", t=PACK)
        for t in range(PACK):
            nc.sync.dma_start(out_rows[t], page[t][:])

        o_scales = keep.tile([P, T], U8, name="o_scales", align_bytes=64)
        o_codes = keep.tile([P, T], I32, name="o_codes", align_bytes=64)
        words_out = out_1[0].rearrange("p c b -> p (c b)").bitcast(I32)
        split = T // 2 + P
        own = HALF + PIECE
        spans = [(0, own), (own, split - own), (split, HALF - P), (T - HALF, HALF)]
        chunks = [(c, HALF) for c in range(0, T // 2, HALF)] + [(c, PIECE) for c in range(T // 2, T, PIECE)]
        woven_o = [keep.tile([P, n, 2], U32, name="woven_o%d" % c, align_bytes=64) for c, n in chunks]
        pairs = [keep.tile([P, 2, n, 2], BF16, name="pairs%d" % c, align_bytes=64) for c, n in spans]
        for t in range(3):
            for (c, n), pair in zip(spans, pairs):
                if t < 2 or c > 0:
                    nc.scalar.copy(pair[:, t // 2, :, t % 2], page[t][:, c : c + n])

        def weave_out(engine_copy, s, k):
            (first, count), (c, n) = spans[s], chunks[k]
            lo, hi = max(first, c), min(first + count, c + n)
            words = pairs[s][:].rearrange("p u c e -> p (u c e)").bitcast(U32).rearrange("p (u c) -> p c u", u=2)
            engine_copy(woven_o[k][:, lo - c : hi - c, :], words[:, lo - first : hi - first, :])

        def planes(k):
            c, n = chunks[k]
            nc.vector.quantize_mx(
                out=o_codes[:, c : c + n].bitcast(FP8X4),
                scales=o_scales[:, c : c + n],
                in_=woven_o[k][:].rearrange("p c u -> p (c u)").bitcast(BF16),
            )
            if (c + n) % HALF == 0:
                nc.sync.dma_start(words_out[:, c + n - HALF : c + n], o_codes[:, c + n - HALF : c + n])

        nc.scalar.copy(pairs[1][:, 1, :, 1], page[3][:, own:split])
        for s, ks in ((2, (2, 3)), (3, (4, 5))):
            c, n = spans[s]
            nc.scalar.copy(pairs[s][:, 1, :, 1], page[3][:, c : c + n])
            for k in ks:
                weave_out(nc.scalar.copy, s, k)
        for t in (2, 3):
            for first, last in ((0, HALF), (HALF, own)):
                nc.vector.tensor_copy(pairs[0][:, 1, first:last, t % 2], page[t][:, first:last])
        weave_out(nc.vector.tensor_copy, 0, 0)
        weave_out(nc.vector.tensor_copy, 0, 1)
        weave_out(nc.vector.tensor_copy, 1, 1)
        planes(0)
        weave_out(nc.vector.tensor_copy, 1, 2)
        for k in range(1, len(chunks)):
            planes(k)
        for q in range(QUADS):
            (nc.scalar if q % 2 else nc.sync).dma_start(
                out_2[0, 4 * q : 4 * q + 4, :].bitcast(I32), o_scales[32 * q : 32 * q + 4, :].bitcast(I32)
            )
